import numpy as np
import ml_dtypes


def mxq(x, axis, fmt="e4m3"):
    dtype, down = {"e4m3": (ml_dtypes.float8_e4m3fn, 7), "e5m2": (ml_dtypes.float8_e5m2, 14)}[fmt]
    v = np.moveaxis(np.asarray(x, np.float32).astype(ml_dtypes.bfloat16).astype(np.float64), axis, -1)
    blocks = v.reshape(v.shape[:-1] + (-1, 32))
    amax = np.abs(blocks).max(-1, keepdims=True)
    byte = np.maximum(np.where(amax > 0, np.frexp(amax)[1] - 1 + 127, 0) - down, 1)
    scale = np.exp2(byte - 127.0)
    codes = (blocks / scale).astype(np.float32).astype(dtype).astype(np.float64)
    return np.moveaxis((codes * scale).reshape(v.shape), -1, axis)


WIDE = False


def mx_kscale(k):
    if not WIDE:
        return np.ones(k)
    levels = np.array([10, -10, 5, -5, 0])
    if k % 512:
        return np.exp2(np.random.permutation(np.resize(levels, k // 32))).repeat(32)
    a = np.empty((k // 512, 16))
    for p in range(k // 512):
        a[p, :8] = np.random.permutation(np.resize(levels, 8))
        for g in range(8):
            far = levels[np.abs(levels - a[p, g]) >= 10]
            a[p, g + 8] = far[np.random.randint(len(far))]
    return np.exp2(a.ravel()).repeat(32)


def f64(x):
    return np.asarray(x).astype(np.float64)


def striped(idx):
    return np.tile(idx.reshape(-1, 16).T, (8, 1)).astype(np.uint16)


def unstriped(offs):
    return offs[:16].T.reshape(-1).astype(np.int64)


E2M1 = np.array([0.0, 0.5, 1.0, 1.5, 2.0, 3.0, 4.0, 6.0, -0.0, -0.5, -1.0, -1.5, -2.0, -3.0, -4.0, -6.0])


def pack_weight(w, fmt):
    k, n = w.shape
    w = f64(np.asarray(w, np.float32).astype(ml_dtypes.bfloat16)).reshape(k // 32, 32, n)
    amax = np.abs(w).max(1)
    if fmt == "e4m3":
        byte = np.frexp(amax)[1] - 1 + 127 - 7
    else:
        mant, ex = np.frexp(amax / 6.0)
        byte = np.where(mant > 0.5, ex, ex - 1) + 127
    byte = np.clip(np.where(amax > 0, byte, 1), 1, 254)
    scaled = (w * np.exp2(127.0 - byte)[:, None, :]).reshape(k, n).astype(np.float32)
    by_word = np.ascontiguousarray(scaled.reshape(k // 512, 128, 4, n).transpose(0, 1, 3, 2))
    if fmt == "e4m3":
        words = by_word.astype(ml_dtypes.float8_e4m3fn).view(np.uint8)
    else:
        c = by_word.astype(ml_dtypes.float4_e2m1fn).view(np.uint8) & 0xF
        words = (c[..., 0::2] | (c[..., 1::2] << 4)).reshape(k // 512, 128, 2 * n)
    return np.ascontiguousarray(words), np.ascontiguousarray(byte.astype(np.uint8).reshape(k // 512, 16, n))


def unpack_weight(words, scales, fmt):
    g, _, n = scales.shape
    words = np.ascontiguousarray(words).reshape(g, 128, n, -1)
    if fmt == "e4m3":
        vals = words.view(ml_dtypes.float8_e4m3fn).astype(np.float64)
    else:
        nib = np.empty((g, 128, n, 4), np.uint8)
        nib[..., 0::2] = words & 0xF
        nib[..., 1::2] = words >> 4
        vals = E2M1[nib]
    vals = vals * np.repeat(np.exp2(scales.astype(np.float64) - 127.0), 8, axis=1)[..., None]
    return vals.transpose(0, 1, 3, 2).reshape(g * 512, n)


def gelu(v):
    return 0.5 * v * (1.0 + np.tanh(np.sqrt(2.0 / np.pi) * (v + 0.044715 * v**3)))


def bf(x):
    return np.asarray(x, np.float32).astype(ml_dtypes.bfloat16)


def planes(Y):
    n, m = Y.shape
    b = f64(bf(Y)).reshape(n // 32, 32, m)
    amax = np.abs(b).max(1)
    byte = np.clip(np.where(amax > 0, np.frexp(amax)[1] - 1 + 127 - 7, 1), 1, 254)
    codes = (b * np.exp2(127.0 - byte)[:, None, :]).reshape(n, m).astype(np.float32).astype(ml_dtypes.float8_e4m3fn).view(np.uint8)
    words = codes.reshape(n // 512, 128, 4, m).transpose(0, 1, 3, 2)
    return np.ascontiguousarray(words), np.ascontiguousarray(byte.astype(np.uint8).reshape(n // 512, 16, m))


K, H, F, N, T, S, T2, P = 1024, 512, 1024, 512, 2048, 1024, 2048, 1024

def setup_inputs():
    n = np.random.standard_normal
    s = mx_kscale(K)[:, None]
    u = mx_kscale(F)[:, None]
    size = np.exp(0.8 * n((1, N)))
    tab_words, tab_scales = pack_weight(n((K, T)) * s, "e4m3")
    w1_words, w1_scales = pack_weight(0.33 * n((K, H)) / np.sqrt(K) / s, "e2m1")
    wb_words, wb_scales = pack_weight(2.5 * n((H, N)) / np.sqrt(H) / u[H:], "e4m3")
    return {
        "tab_words": tab_words, "tab_scales": tab_scales,
        "offs": striped(np.random.permutation(T)[:S]),
        "offs2": striped(np.random.permutation(T2)[:S]),
        "offs3": striped(np.random.permutation(T2)[:P]),
        "w1_words": w1_words, "w1_scales": w1_scales,
        "wgs": np.exp(0.3 * np.clip(n((128, S)), -2.0, 2.0)).astype(np.float32),
        "page0": (0.5 * n((H, T2))).astype(np.float32),
        "gain": (np.exp(0.2 * n(F)) * u[:, 0]).astype(np.float32),
        "wa": (2.0 * n((H, N)) / np.sqrt(H) / u[:H] * size).astype(np.float32),
        "wb_words": wb_words, "wb_scales": wb_scales,
        "wd": (1.5 * n((F, N)) / np.sqrt(F) / u * size).astype(np.float32),
        "bias": (0.4 * n(N) * size[0]).astype(np.float32),
    }

def reference(tab_words, tab_scales, offs, offs2, offs3, w1_words, w1_scales, wgs, page0, gain, wa, wb_words, wb_scales, wd, bias):
    v = unpack_weight(tab_words, tab_scales, "e4m3")[:, unstriped(offs)]
    h = unpack_weight(w1_words, w1_scales, "e2m1").T @ v
    page = f64(page0).copy()
    page[:, unstriped(offs2)] = np.tile(f64(wgs), (H // 128, 1)) * h
    x = page[:, unstriped(offs3)]
    z = np.concatenate((np.sin(x), np.square(x)), axis=0) * f64(gain)[:, None]
    zq = mxq(z, 0, "e4m3")
    a = mxq(f64(wa), 0, "e4m3").T @ zq[:H]
    b = unpack_weight(wb_words, wb_scales, "e4m3").T @ zq[H:]
    d = mxq(f64(wd), 0, "e4m3").T @ zq
    y = a * b + d + f64(bias)[:, None]
    words, scales = planes(y)
    return y, words, scales

@@ -1,0 +1,267 @@
+from contextlib import ExitStack
+
+import concourse.mybir as mybir
+
+K, H, F, N, T, S, T2, M = 1024, 512, 1024, 512, 2048, 1024, 2048, 1024
+FLOPS = 2 * (K * H * S + H * N * M + H * N * M + F * N * M)
+
+F32 = mybir.dt.float32
+BF16 = mybir.dt.bfloat16
+I32 = mybir.dt.int32
+U32 = mybir.dt.uint32
+U16 = mybir.dt.uint16
+U8 = mybir.dt.uint8
+FP8X4 = mybir.dt.float8_e4m3fn_x4
+FP4X4 = mybir.dt.float4_e2m1fn_x4
+ALU = mybir.AluOpType
+ACT = mybir.ActivationFunctionType
+
+P = 128
+PACK = 4
+QUAD = 32
+HALF = 512
+CHUNKS = ((0, 256), (256, 512), (768, 256))
+
+
+def tile_list_electrode_refit_kernel(
+    tc, tab_words, tab_scales, offs, offs2, offs3, w1_words, w1_scales, wgs, page0, gain, wa, wb_words, wb_scales, wd, bias,
+    out_0, out_1, out_2,
+):
+    nc = tc.nc
+    with ExitStack() as ctx:
+        lists = ctx.enter_context(tc.tile_pool(name="lists", bufs=1))
+        keep = ctx.enter_context(tc.tile_pool(name="keep", bufs=1))
+        ring = ctx.enter_context(tc.tile_pool(name="ring", bufs=2))
+        deep = ctx.enter_context(tc.tile_pool(name="deep", bufs=4))
+        psum = ctx.enter_context(tc.psum_pool(name="psum", bufs=8))
+
+        def held(name, shape, dtype):
+            return keep.tile(shape, dtype, name=name, align_bytes=64)
+
+        idx = lists.tile([P, S // 16], U16, name="idx")
+        idx2 = lists.tile([P, S // 16], U16, name="idx2")
+        idx3 = lists.tile([P, M // 16], U16, name="idx3")
+
+        def shared(tag, name, shape, dtype):
+            return keep.tile(shape, dtype, name=name, tag=tag, align_bytes=64)
+
+        tab_s = shared("tab_s", "tab_s", [P, T], U8)
+        w1_s_raw = shared("w1_s_raw", "w1_s_raw", [P, 2, H], U8)
+        wb_s_raw = held("wb_s_raw", [P, N], U8)
+        v_s = shared("v_s", "v_s", [P, 2, S], U8)
+        nc.vector.memset(tab_s[0:96, :].bitcast(I32), 0)
+        nc.gpsimd.memset(w1_s_raw[:].rearrange("p a c -> p (a c)").bitcast(I32), 0)
+        for q in range(4):
+            eng = nc.gpsimd if q % 2 == 0 else nc.scalar
+            eng.dma_start(
+                w1_s_raw[QUAD * q : QUAD * q + 4, :, :].bitcast(I32),
+                w1_scales[:, 4 * q : 4 * q + 4, :].rearrange("a r c -> r a c").bitcast(I32),
+            )
+        nc.vector.memset(v_s[:].rearrange("p a c -> p (a c)").bitcast(I32), 0)
+        nc.gpsimd.memset(wb_s_raw[:].bitcast(I32), 0)
+        warm = shared("warm", "warm", [P, 1], F32)
+        warm_out = held("warm_out", [P, 1], F32)
+        nc.vector.memset(warm[:], 0.0)
+        nc.scalar.activation(warm_out[:], warm[:], ACT.Sin)
+
+        nc.sync.dma_start(idx[:], offs)
+        nc.sync.dma_start(tab_s[96:128, :].bitcast(I32), tab_scales.rearrange("a q n -> q a n").bitcast(I32))
+        nc.sync.dma_start(idx2[:], offs2)
+        nc.sync.dma_start(idx3[:], offs3)
+        tab_w = [shared("tab%d" % a, "tab_w%d" % a, [P, T], I32) for a in range(2)]
+        w1_w_raw = shared("w1", "w1_w_raw", [P, 2, 2 * H], U8)
+        nc.sync.dma_start(tab_w[0][:], tab_words[0].rearrange("p t i -> p (t i)").bitcast(I32))
+        nc.sync.dma_start(w1_w_raw[:].bitcast(I32), w1_words.rearrange("a p c -> p a c").bitcast(I32))
+        nc.sync.dma_start(tab_w[1][:], tab_words[1].rearrange("p t i -> p (t i)").bitcast(I32))
+
+        page_rows = page0.rearrange("(p t) n -> t p n", t=PACK)
+        wgs_rows = wgs.rearrange("(i t) j -> t i j", t=PACK)
+        page, wg, w_raw = {}, {}, {}
+
+        def load_page(t, tag):
+            page[t] = shared(tag, "page%d" % t, [P, T2], F32)
+            nc.sync.dma_start(page[t][:], page_rows[t])
+
+        def load_wg(t, tag):
+            wg[t] = shared(tag, "wg%d" % t, [P, S], F32)
+            for q in (0, 2, 1, 3):
+                nc.sync.dma_start(wg[t][QUAD * q : QUAD * (q + 1), :], wgs_rows[t])
+
+        w_src = (wa, wd[0:H, :], wd[H:F, :])
+
+        def load_weight(i, tag):
+            w_raw[i] = shared(tag, "w_raw%d" % i, [P, PACK, N], F32)
+            nc.sync.dma_start(w_raw[i][:], w_src[i].rearrange("(p j) n -> p j n", j=PACK))
+
+        picked_s = shared("picked", "picked_s", [P, S], U8)
+        nc.vector.tensor_copy(picked_s[:], tab_s[:].indirect(idx[:]))
+        for q in range(4):
+            nc.sync.dma_start(v_s[QUAD * q : QUAD * q + 4, :, :].bitcast(I32), picked_s[96 + 8 * q : 104 + 8 * q, :].bitcast(I32))
+        load_page(0, "tab_s")
+
+        for q in range(4):
+            nc.gpsimd.dma_start(wb_s_raw[QUAD * q : QUAD * q + 4, :].bitcast(I32), wb_scales[0, 4 * q : 4 * q + 4, :].bitcast(I32))
+
+        w1_w = shared("w1_w", "w1_w", [P, 2, PACK, 2 * P], U8)
+        w1_s = shared("w1_s", "w1_s", [P, 2, PACK, P], U8)
+        for a in range(2):
+            nc.vector.tensor_copy(
+                w1_w[:, a, :, :].bitcast(U16).rearrange("p t m -> p m t"),
+                w1_w_raw[:, a, :].bitcast(U16).rearrange("p (m t) -> p m t", t=PACK),
+            )
+        load_wg(0, "w1")
+
+        v_w = [[shared("v%d%d" % (a, u), "v_w%d_%d" % (a, u), [P, HALF], U32) for u in range(2)] for a in range(2)]
+        for a in range(2):
+            for u in range(2):
+                nc.vector.tensor_copy(v_w[a][u][:], tab_w[a][:].bitcast(U32).indirect(idx[:, 32 * u : 32 * (u + 1)]))
+            if a == 0:
+                nc.vector.tensor_copy(w1_s[:].rearrange("p a t m -> p a m t"), w1_s_raw[:].rearrange("p a (m t) -> p a m t", t=PACK))
+        gain_sb = shared("w1_s_raw", "gain_sb", [P, 2, PACK], F32)
+        bias_sb = shared("warm", "bias_sb", [P, PACK], F32)
+        nc.gpsimd.dma_start(gain_sb[:], gain.rearrange("(f p t) -> p f t", f=2, t=PACK))
+        nc.gpsimd.dma_start(bias_sb[:], bias.rearrange("(p t) -> p t", t=PACK))
+
+
+        h_sb = [[shared("h%d%d" % (t, u), "h_sb%d_%d" % (t, u), [P, HALF], F32) for u in range(2)] if t == 0 else held("h_sb%d" % t, [P, S], F32) for t in range(PACK)]
+        for t in range(PACK):
+            for u in range(2):
+                cols = slice(HALF * u, HALF * (u + 1))
+                acc = psum.tile([P, HALF], F32, name="acc", tag="bank")
+                for a in range(2):
+                    nc.tensor.matmul_mx(
+                        acc[:], lhsT=w1_w[:, a, t, :].bitcast(FP4X4), lhsT_scale=w1_s[:, a, t, :],
+                        rhs=v_w[a][u][:].bitcast(FP8X4), rhs_scale=v_s[:, a, cols], start=(a == 0), stop=(a == 1),
+                    )
+                nc.scalar.copy(h_sb[t][u][:] if t == 0 else h_sb[t][:, cols], acc[:])
+
+        load_weight(0, "tab0")
+        load_weight(1, "picked")
+        load_weight(2, "tab1")
+        load_page(1, "v00")
+        load_wg(1, "v10")
+        load_page(2, "v01")
+        load_wg(2, "v11")
+        wb_w_raw = shared("w1_s", "wb_w_raw", [P, N], I32)
+        nc.sync.dma_start(wb_w_raw[:], wb_words[0].rearrange("p c i -> p (c i)").bitcast(I32))
+        load_page(3, "w1_w")
+        load_wg(3, "v_s")
+
+        w_w = [held("w_w%d" % i, [P, N], U32) for i in range(3)]
+        w_s = [held("w_s%d" % i, [P, N], U8) for i in range(3)]
+
+        def round_weight(i):
+            grouped = shared(("h00", "tab0", "picked")[i], "grouped%d" % i, [P, N * PACK], BF16)
+            nc.scalar.copy(
+                grouped[:].rearrange("p (t m j) -> p m j t", t=PACK, j=PACK),
+                w_raw[i][:].rearrange("p j (m t) -> p m j t", t=PACK),
+            )
+            return grouped
+
+        def quantise_weight(i, grouped):
+            nc.vector.quantize_mx(w_w[i][:].bitcast(FP8X4), w_s[i][:], grouped[:])
+
+        z_bf = [held("z_bf%d" % f, [P, M * PACK], BF16) for f in range(2)]
+
+        def scatter(t, parts):
+            width = S // parts
+            for u in range(parts):
+                cols = slice(width * u, width * (u + 1))
+                where = idx2[:, width // 16 * u : width // 16 * (u + 1)]
+                nc.vector.tensor_tensor(page[t][:].indirect(where), h_sb[t][u][:] if t == 0 else h_sb[t][:], wg[t][:, cols], ALU.mult)
+
+        def features(t, x, c0, width, sine_on_vector):
+            if t == 0:
+                both = shared("tab1", "feat_first", [P, 2 * width], F32)
+            else:
+                both = ring.tile([P, 2 * width], F32, name="feat", tag="feat")
+            for f, func in enumerate((ACT.Sin, ACT.Square)):
+                feat = both[:, f * width : (f + 1) * width]
+                nc.scalar.activation(feat, x, func)
+                dst = z_bf[f][:, PACK * c0 + t : PACK * (c0 + width) : PACK]
+                if f == 0 and sine_on_vector:
+                    nc.vector.tensor_scalar(dst, feat, gain_sb[:, f, t : t + 1], None, ALU.mult)
+                else:
+                    nc.scalar.activation(dst, feat, ACT.Copy, scale=gain_sb[:, f, t : t + 1])
+
+        def whole_slot(t):
+            x = ring.tile([P, M], F32, name="x", tag="x")
+            nc.vector.tensor_copy(x[:], page[t][:].indirect(idx3[:]))
+            features(t, x[:], 0, M, False)
+
+        scatter(0, 2)
+        grouped = [round_weight(i) for i in range(3)]
+        whole_slot(0)
+        quantise_weight(0, grouped[0])
+        quantise_weight(1, grouped[1])
+        scatter(1, 1)
+        whole_slot(1)
+        wb_w = held("wb_w", [P, N], I32)
+        wb_s = held("wb_s", [P, N], U8)
+        scatter(2, 1)
+        whole_slot(2)
+        quantise_weight(2, grouped[2])
+        nc.vector.tensor_copy(wb_w[:].rearrange("p (t m) -> p m t", t=PACK), wb_w_raw[:].rearrange("p (m t) -> p m t", t=PACK))
+        nc.vector.tensor_copy(wb_s[:].rearrange("p (t m) -> p m t", t=PACK), wb_s_raw[:].rearrange("p (m t) -> p m t", t=PACK))
+        scatter(3, 1)
+
+        last = PACK - 1
+        z_w = [[held("z_w%d_%d" % (f, c), [P, w], U32) for c, (c0, w) in enumerate(CHUNKS)] for f in range(2)]
+        z_s = [[held("z_s%d_%d" % (f, c), [P, w], U8) for c, (c0, w) in enumerate(CHUNKS)] for f in range(2)]
+        x_last = [held("x_last%d" % c, [P, w], F32) for c, (c0, w) in enumerate(CHUNKS)]
+        y_s = held("y_s", [P, M], U8)
+        y_rows = out_0.rearrange("(p t) m -> p t m", t=PACK)
+        code_rows = out_1[0].rearrange("p m t -> p (m t)")
+
+        def finish_z(c):
+            c0, w = CHUNKS[c]
+            nc.vector.tensor_copy(x_last[c][:], page[last][:].indirect(idx3[:, c0 // 16 : (c0 + w) // 16]))
+            features(last, x_last[c][:], c0, w, True)
+            for f in range(2):
+                nc.vector.quantize_mx(z_w[f][c][:].bitcast(FP8X4), z_s[f][c][:], z_bf[f][:, PACK * c0 : PACK * (c0 + w)])
+
+        def product(c, t, terms):
+            w = CHUNKS[c][1]
+            cols = slice(P * t, P * (t + 1))
+            acc = psum.tile([P, w], F32, name="acc", tag="bank")
+            for n, (words, scales, f) in enumerate(terms):
+                nc.tensor.matmul_mx(
+                    acc[:], lhsT=words[:, cols].bitcast(FP8X4), lhsT_scale=scales[:, cols],
+                    rhs=z_w[f][c][:].bitcast(FP8X4), rhs_scale=z_s[f][c][:], start=(n == 0), stop=(n == len(terms) - 1),
+                )
+            return acc
+
+        def finish_y(c):
+            c0, w = CHUNKS[c]
+            y = held("y%d" % c, [P, PACK, w], F32)
+            pending = None
+            for t in range(PACK + 1):
+                if t < PACK:
+                    a_ps = product(c, t, [(w_w[0], w_s[0], 0)])
+                    b_ps = product(c, t, [(wb_w, wb_s, 1)])
+                    d_ps = product(c, t, [(w_w[1], w_s[1], 0), (w_w[2], w_s[2], 1)])
+                    a_sb = deep.tile([P, w], F32, name="a_sb", tag="a_sb")
+                    nc.scalar.copy(a_sb[:], a_ps[:])
+                    ab = deep.tile([P, w], F32, name="ab", tag="ab")
+                    nc.vector.tensor_tensor(ab[:], b_ps[:], a_sb[:], ALU.mult)
+                if pending is not None:
+                    tp, d_prev, ab_prev = pending
+                    nc.vector.scalar_tensor_tensor(y[:, tp, :], d_prev[:], bias_sb[:, tp : tp + 1], ab_prev[:], ALU.add, ALU.add)
+                pending = (t, d_ps, ab) if t < PACK else None
+            nc.sync.dma_start(y_rows[:, :, c0 : c0 + w], y[:])
+            y_bf = held("y_bf%d" % c, [P, w * PACK], BF16)
+            cast = nc.vector.tensor_copy if c == len(CHUNKS) - 1 else nc.scalar.copy
+            cast(y_bf[:].rearrange("p (g i t) -> p g t i", i=4, t=PACK), y[:].rearrange("p t (g i) -> p g t i", i=4))
+            y_w = held("y_w%d" % c, [P, w], I32)
+            nc.vector.quantize_mx(y_w[:].bitcast(FP8X4), y_s[:, c0 : c0 + w], y_bf[:])
+            nc.sync.dma_start(code_rows[:, PACK * c0 : PACK * (c0 + w)].bitcast(I32), y_w[:])
+
+        finish_z(0)
+        finish_z(1)
+        finish_y(0)
+        finish_z(2)
+        finish_y(1)
+        finish_y(2)
+        for q in range(4):
+            eng = nc.sync if q % 2 == 0 else nc.scalar
+            eng.dma_start(out_2[0, 4 * q : 4 * q + 4, :].bitcast(I32), y_s[QUAD * q : QUAD * q + 4, :].bitcast(I32))

@@ -47,7 +47,6 @@ def tile_list_electrode_refit_kernel(
 
         tab_s = shared("tab_s", "tab_s", [P, T], U8)
         w1_s_raw = shared("w1_s_raw", "w1_s_raw", [P, 2, H], U8)
-        wb_s_raw = held("wb_s_raw", [P, N], U8)
         v_s = shared("v_s", "v_s", [P, 2, S], U8)
         nc.vector.memset(tab_s[0:96, :].bitcast(I32), 0)
         nc.gpsimd.memset(w1_s_raw[:].rearrange("p a c -> p (a c)").bitcast(I32), 0)
@@ -58,9 +57,8 @@ def tile_list_electrode_refit_kernel(
                 w1_scales[:, 4 * q : 4 * q + 4, :].rearrange("a r c -> r a c").bitcast(I32),
             )
         nc.vector.memset(v_s[:].rearrange("p a c -> p (a c)").bitcast(I32), 0)
-        nc.gpsimd.memset(wb_s_raw[:].bitcast(I32), 0)
         warm = shared("warm", "warm", [P, 1], F32)
-        warm_out = held("warm_out", [P, 1], F32)
+        warm_out = shared("warm_out", "warm_out", [P, 1], F32)
         nc.vector.memset(warm[:], 0.0)
         nc.scalar.activation(warm_out[:], warm[:], ACT.Sin)
 
@@ -99,11 +97,7 @@ def tile_list_electrode_refit_kernel(
             nc.sync.dma_start(v_s[QUAD * q : QUAD * q + 4, :, :].bitcast(I32), picked_s[96 + 8 * q : 104 + 8 * q, :].bitcast(I32))
         load_page(0, "tab_s")
 
-        for q in range(4):
-            nc.gpsimd.dma_start(wb_s_raw[QUAD * q : QUAD * q + 4, :].bitcast(I32), wb_scales[0, 4 * q : 4 * q + 4, :].bitcast(I32))
-
         w1_w = shared("w1_w", "w1_w", [P, 2, PACK, 2 * P], U8)
-        w1_s = shared("w1_s", "w1_s", [P, 2, PACK, P], U8)
         for a in range(2):
             nc.vector.tensor_copy(
                 w1_w[:, a, :, :].bitcast(U16).rearrange("p t m -> p m t"),
@@ -111,19 +105,22 @@ def tile_list_electrode_refit_kernel(
             )
         load_wg(0, "w1")
 
-        v_w = [[shared("v%d%d" % (a, u), "v_w%d_%d" % (a, u), [P, HALF], U32) for u in range(2)] for a in range(2)]
+        v_tags = (("v00", "v01"), ("v10", "v11"))
+        v_w = [[None, None], [None, None]]
         for a in range(2):
             for u in range(2):
+                v_w[a][u] = shared(v_tags[a][u], "v_w%d_%d" % (a, u), [P, HALF], U32)
                 nc.vector.tensor_copy(v_w[a][u][:], tab_w[a][:].bitcast(U32).indirect(idx[:, 32 * u : 32 * (u + 1)]))
             if a == 0:
+                w1_s = shared("tab0", "w1_s", [P, 2, PACK, P], U8)
                 nc.vector.tensor_copy(w1_s[:].rearrange("p a t m -> p a m t"), w1_s_raw[:].rearrange("p a (m t) -> p a m t", t=PACK))
-        gain_sb = shared("w1_s_raw", "gain_sb", [P, 2, PACK], F32)
+        gain_sb = shared("warm_out", "gain_sb", [P, 2, PACK], F32)
         bias_sb = shared("warm", "bias_sb", [P, PACK], F32)
         nc.gpsimd.dma_start(gain_sb[:], gain.rearrange("(f p t) -> p f t", f=2, t=PACK))
         nc.gpsimd.dma_start(bias_sb[:], bias.rearrange("(p t) -> p t", t=PACK))
 
 
-        h_sb = [[shared("h%d%d" % (t, u), "h_sb%d_%d" % (t, u), [P, HALF], F32) for u in range(2)] if t == 0 else held("h_sb%d" % t, [P, S], F32) for t in range(PACK)]
+        h_sb = [[shared("h%d%d" % (t, u), "h_sb%d_%d" % (t, u), [P, HALF], F32) for u in range(2)] if t == 0 else shared("h%d" % t, "h_sb%d" % t, [P, S], F32) for t in range(PACK)]
         for t in range(PACK):
             for u in range(2):
                 cols = slice(HALF * u, HALF * (u + 1))
@@ -135,31 +132,27 @@ def tile_list_electrode_refit_kernel(
                     )
                 nc.scalar.copy(h_sb[t][u][:] if t == 0 else h_sb[t][:, cols], acc[:])
 
-        load_weight(0, "tab0")
-        load_weight(1, "picked")
+        load_weight(0, "picked")
+        load_weight(1, "w1_s_raw")
         load_weight(2, "tab1")
         load_page(1, "v00")
         load_wg(1, "v10")
         load_page(2, "v01")
         load_wg(2, "v11")
-        wb_w_raw = shared("w1_s", "wb_w_raw", [P, N], I32)
+        wb_w_raw = shared("tab0", "wb_w_raw", [P, N], I32)
         nc.sync.dma_start(wb_w_raw[:], wb_words[0].rearrange("p c i -> p (c i)").bitcast(I32))
         load_page(3, "w1_w")
         load_wg(3, "v_s")
 
-        w_w = [held("w_w%d" % i, [P, N], U32) for i in range(3)]
         w_s = [held("w_s%d" % i, [P, N], U8) for i in range(3)]
 
         def round_weight(i):
-            grouped = shared(("h00", "tab0", "picked")[i], "grouped%d" % i, [P, N * PACK], BF16)
+            grouped = shared(("h00", "picked", "w1_s_raw")[i], "grouped%d" % i, [P, N * PACK], BF16)
             nc.scalar.copy(
                 grouped[:].rearrange("p (t m j) -> p m j t", t=PACK, j=PACK),
                 w_raw[i][:].rearrange("p j (m t) -> p m j t", t=PACK),
             )
             return grouped
-
-        def quantise_weight(i, grouped):
-            nc.vector.quantize_mx(w_w[i][:].bitcast(FP8X4), w_s[i][:], grouped[:])
 
         z_bf = [held("z_bf%d" % f, [P, M * PACK], BF16) for f in range(2)]
 
@@ -170,42 +163,58 @@ def tile_list_electrode_refit_kernel(
                 where = idx2[:, width // 16 * u : width // 16 * (u + 1)]
                 nc.vector.tensor_tensor(page[t][:].indirect(where), h_sb[t][u][:] if t == 0 else h_sb[t][:], wg[t][:, cols], ALU.mult)
 
-        def features(t, x, c0, width, sine_on_vector):
-            if t == 0:
-                both = shared("tab1", "feat_first", [P, 2 * width], F32)
-            else:
-                both = ring.tile([P, 2 * width], F32, name="feat", tag="feat")
+        last = PACK - 1
+        planes = [held("planes%d" % f, [P, last * M], BF16) for f in range(2)]
+
+        def features(x, both, targets, t, on_vector):
+            width = x.shape[1]
             for f, func in enumerate((ACT.Sin, ACT.Square)):
                 feat = both[:, f * width : (f + 1) * width]
                 nc.scalar.activation(feat, x, func)
-                dst = z_bf[f][:, PACK * c0 + t : PACK * (c0 + width) : PACK]
-                if f == 0 and sine_on_vector:
-                    nc.vector.tensor_scalar(dst, feat, gain_sb[:, f, t : t + 1], None, ALU.mult)
+                if f < on_vector:
+                    nc.vector.tensor_scalar(targets[f], feat, gain_sb[:, f, t : t + 1], None, ALU.mult)
                 else:
-                    nc.scalar.activation(dst, feat, ACT.Copy, scale=gain_sb[:, f, t : t + 1])
+                    nc.scalar.activation(targets[f], feat, ACT.Copy, scale=gain_sb[:, f, t : t + 1])
 
         def whole_slot(t):
             x = ring.tile([P, M], F32, name="x", tag="x")
             nc.vector.tensor_copy(x[:], page[t][:].indirect(idx3[:]))
-            features(t, x[:], 0, M, False)
+            if t == 0:
+                both = shared("tab1", "feat_first", [P, 2 * M], F32)
+            else:
+                both = ring.tile([P, 2 * M], F32, name="feat", tag="feat")
+            features(x[:], both, [planes[f][:, t * M : (t + 1) * M] for f in range(2)], t, 0)
+
+        def weave(c):
+            c0, w = CHUNKS[c]
+            for f in range(2):
+                nc.scalar.copy(
+                    z_bf[f][:, PACK * c0 : PACK * (c0 + w)].rearrange("p (g i t) -> p g t i", i=8, t=PACK)[:, :, 0:last, :],
+                    planes[f][:].rearrange("p (t m) -> p t m", t=last)[:, :, c0 : c0 + w].rearrange("p t (g i) -> p g t i", i=8),
+                )
 
         scatter(0, 2)
+        wb_s_raw = shared("h01", "wb_s_raw", [P, N], U8)
+        nc.gpsimd.memset(wb_s_raw[:].bitcast(I32), 0)
+        for q in range(4):
+            nc.gpsimd.dma_start(wb_s_raw[QUAD * q : QUAD * q + 4, :].bitcast(I32), wb_scales[0, 4 * q : 4 * q + 4, :].bitcast(I32))
         grouped = [round_weight(i) for i in range(3)]
         whole_slot(0)
-        quantise_weight(0, grouped[0])
-        quantise_weight(1, grouped[1])
         scatter(1, 1)
         whole_slot(1)
-        wb_w = held("wb_w", [P, N], I32)
-        wb_s = held("wb_s", [P, N], U8)
         scatter(2, 1)
         whole_slot(2)
-        quantise_weight(2, grouped[2])
+        weave(0)
+        weave(1)
+        w_w = [shared(tag, "w_w%d" % i, [P, N], U32) for i, tag in enumerate(("v01", "v11", "h2"))]
+        wb_w = shared("v00", "wb_w", [P, N], I32)
+        wb_s = shared("v10", "wb_s", [P, N], U8)
+        for i in range(3):
+            nc.vector.quantize_mx(w_w[i][:].bitcast(FP8X4), w_s[i][:], grouped[i][:])
         nc.vector.tensor_copy(wb_w[:].rearrange("p (t m) -> p m t", t=PACK), wb_w_raw[:].rearrange("p (m t) -> p m t", t=PACK))
         nc.vector.tensor_copy(wb_s[:].rearrange("p (t m) -> p m t", t=PACK), wb_s_raw[:].rearrange("p (m t) -> p m t", t=PACK))
         scatter(3, 1)
 
-        last = PACK - 1
         z_w = [[held("z_w%d_%d" % (f, c), [P, w], U32) for c, (c0, w) in enumerate(CHUNKS)] for f in range(2)]
         z_s = [[held("z_s%d_%d" % (f, c), [P, w], U8) for c, (c0, w) in enumerate(CHUNKS)] for f in range(2)]
         x_last = [held("x_last%d" % c, [P, w], F32) for c, (c0, w) in enumerate(CHUNKS)]
@@ -216,38 +225,44 @@ def tile_list_electrode_refit_kernel(
         def finish_z(c):
             c0, w = CHUNKS[c]
             nc.vector.tensor_copy(x_last[c][:], page[last][:].indirect(idx3[:, c0 // 16 : (c0 + w) // 16]))
-            features(last, x_last[c][:], c0, w, True)
+            both = ring.tile([P, 2 * w], F32, name="feat", tag="feat")
+            features(x_last[c][:], both, [z_bf[f][:, PACK * c0 + last : PACK * (c0 + w) : PACK] for f in range(2)], last, 2 if c == 0 else 1)
             for f in range(2):
                 nc.vector.quantize_mx(z_w[f][c][:].bitcast(FP8X4), z_s[f][c][:], z_bf[f][:, PACK * c0 : PACK * (c0 + w)])
 
-        def product(c, t, terms):
+        def product(c, slots, terms):
             w = CHUNKS[c][1]
-            cols = slice(P * t, P * (t + 1))
-            acc = psum.tile([P, w], F32, name="acc", tag="bank")
-            for n, (words, scales, f) in enumerate(terms):
-                nc.tensor.matmul_mx(
-                    acc[:], lhsT=words[:, cols].bitcast(FP8X4), lhsT_scale=scales[:, cols],
-                    rhs=z_w[f][c][:].bitcast(FP8X4), rhs_scale=z_s[f][c][:], start=(n == 0), stop=(n == len(terms) - 1),
-                )
+            acc = psum.tile([P, len(slots) * w], F32, name="acc", tag="bank")
+            for i, t in enumerate(slots):
+                cols = slice(P * t, P * (t + 1))
+                for n, (words, scales, f) in enumerate(terms):
+                    nc.tensor.matmul_mx(
+                        acc[:, i * w : (i + 1) * w], lhsT=words[:, cols].bitcast(FP8X4), lhsT_scale=scales[:, cols],
+                        rhs=z_w[f][c][:].bitcast(FP8X4), rhs_scale=z_s[f][c][:], start=(n == 0), stop=(n == len(terms) - 1),
+                    )
             return acc
 
         def finish_y(c):
             c0, w = CHUNKS[c]
             y = held("y%d" % c, [P, PACK, w], F32)
+            per_bank = HALF // w
             pending = None
-            for t in range(PACK + 1):
-                if t < PACK:
-                    a_ps = product(c, t, [(w_w[0], w_s[0], 0)])
-                    b_ps = product(c, t, [(wb_w, wb_s, 1)])
-                    d_ps = product(c, t, [(w_w[1], w_s[1], 0), (w_w[2], w_s[2], 1)])
-                    a_sb = deep.tile([P, w], F32, name="a_sb", tag="a_sb")
+            for t0 in range(0, PACK + per_bank, per_bank):
+                slots = range(t0, t0 + per_bank)
+                if t0 < PACK:
+                    a_ps = product(c, slots, [(w_w[0], w_s[0], 0)])
+                    b_ps = product(c, slots, [(wb_w, wb_s, 1)])
+                    d_ps = product(c, slots, [(w_w[1], w_s[1], 0), (w_w[2], w_s[2], 1)])
+                    a_sb = deep.tile([P, HALF], F32, name="a_sb", tag="a_sb")
                     nc.scalar.copy(a_sb[:], a_ps[:])
-                    ab = deep.tile([P, w], F32, name="ab", tag="ab")
+                    ab = deep.tile([P, HALF], F32, name="ab", tag="ab")
                     nc.vector.tensor_tensor(ab[:], b_ps[:], a_sb[:], ALU.mult)
                 if pending is not None:
-                    tp, d_prev, ab_prev = pending
-                    nc.vector.scalar_tensor_tensor(y[:, tp, :], d_prev[:], bias_sb[:, tp : tp + 1], ab_prev[:], ALU.add, ALU.add)
-                pending = (t, d_ps, ab) if t < PACK else None
+                    done, d_prev, ab_prev = pending
+                    for i, t in enumerate(done):
+                        cols = slice(i * w, (i + 1) * w)
+                        nc.vector.scalar_tensor_tensor(y[:, t, :], d_prev[:, cols], bias_sb[:, t : t + 1], ab_prev[:, cols], ALU.add, ALU.add)
+                pending = (slots, d_ps, ab)
             nc.sync.dma_start(y_rows[:, :, c0 : c0 + w], y[:])
             y_bf = held("y_bf%d" % c, [P, w * PACK], BF16)
             cast = nc.vector.tensor_copy if c == len(CHUNKS) - 1 else nc.scalar.copy
@@ -259,6 +274,7 @@ def tile_list_electrode_refit_kernel(
         finish_z(0)
         finish_z(1)
         finish_y(0)
+        weave(2)
         finish_z(2)
         finish_y(1)
         finish_y(2)

@@ -100,8 +100,8 @@ def tile_list_electrode_refit_kernel(
         w1_w = shared("w1_w", "w1_w", [P, 2, PACK, 2 * P], U8)
         for a in range(2):
             nc.vector.tensor_copy(
-                w1_w[:, a, :, :].bitcast(U16).rearrange("p t m -> p m t"),
-                w1_w_raw[:, a, :].bitcast(U16).rearrange("p (m t) -> p m t", t=PACK),
+                w1_w[:, a, :, :].bitcast(U16),
+                w1_w_raw[:, a, :].bitcast(U16).rearrange("p (m t) -> p t m", t=PACK),
             )
         load_wg(0, "w1")
 
@@ -113,7 +113,7 @@ def tile_list_electrode_refit_kernel(
                 nc.vector.tensor_copy(v_w[a][u][:], tab_w[a][:].bitcast(U32).indirect(idx[:, 32 * u : 32 * (u + 1)]))
             if a == 0:
                 w1_s = shared("tab0", "w1_s", [P, 2, PACK, P], U8)
-                nc.vector.tensor_copy(w1_s[:].rearrange("p a t m -> p a m t"), w1_s_raw[:].rearrange("p a (m t) -> p a m t", t=PACK))
+                nc.vector.tensor_copy(w1_s[:], w1_s_raw[:].rearrange("p a (m t) -> p a t m", t=PACK))
         gain_sb = shared("warm_out", "gain_sb", [P, 2, PACK], F32)
         bias_sb = shared("warm", "bias_sb", [P, PACK], F32)
         nc.gpsimd.dma_start(gain_sb[:], gain.rearrange("(f p t) -> p f t", f=2, t=PACK))
@@ -149,8 +149,8 @@ def tile_list_electrode_refit_kernel(
         def round_weight(i):
             grouped = shared(("h00", "picked", "w1_s_raw")[i], "grouped%d" % i, [P, N * PACK], BF16)
             nc.scalar.copy(
-                grouped[:].rearrange("p (t m j) -> p m j t", t=PACK, j=PACK),
-                w_raw[i][:].rearrange("p j (m t) -> p m j t", t=PACK),
+                grouped[:].rearrange("p (t m j) -> p m t j", t=PACK, j=PACK),
+                w_raw[i][:].rearrange("p j (m t) -> p m t j", t=PACK),
             )
             return grouped
 
@@ -164,34 +164,25 @@ def tile_list_electrode_refit_kernel(
                 nc.vector.tensor_tensor(page[t][:].indirect(where), h_sb[t][u][:] if t == 0 else h_sb[t][:], wg[t][:, cols], ALU.mult)
 
         last = PACK - 1
-        planes = [held("planes%d" % f, [P, last * M], BF16) for f in range(2)]
 
-        def features(x, both, targets, t, on_vector):
+        def features(t, x, c0, both, on_vector):
             width = x.shape[1]
             for f, func in enumerate((ACT.Sin, ACT.Square)):
                 feat = both[:, f * width : (f + 1) * width]
                 nc.scalar.activation(feat, x, func)
+                target = z_bf[f][:, PACK * c0 + t : PACK * (c0 + width) : PACK]
                 if f < on_vector:
-                    nc.vector.tensor_scalar(targets[f], feat, gain_sb[:, f, t : t + 1], None, ALU.mult)
+                    nc.vector.tensor_scalar(target, feat, gain_sb[:, f, t : t + 1], None, ALU.mult)
                 else:
-                    nc.scalar.activation(targets[f], feat, ACT.Copy, scale=gain_sb[:, f, t : t + 1])
+                    nc.scalar.activation(target, feat, ACT.Copy, scale=gain_sb[:, f, t : t + 1])
 
-        def whole_slot(t):
+        def read_page(t):
             x = ring.tile([P, M], F32, name="x", tag="x")
             nc.vector.tensor_copy(x[:], page[t][:].indirect(idx3[:]))
-            if t == 0:
-                both = shared("tab1", "feat_first", [P, 2 * M], F32)
-            else:
-                both = ring.tile([P, 2 * M], F32, name="feat", tag="feat")
-            features(x[:], both, [planes[f][:, t * M : (t + 1) * M] for f in range(2)], t, 0)
+            return x
 
-        def weave(c):
-            c0, w = CHUNKS[c]
-            for f in range(2):
-                nc.scalar.copy(
-                    z_bf[f][:, PACK * c0 : PACK * (c0 + w)].rearrange("p (g i t) -> p g t i", i=8, t=PACK)[:, :, 0:last, :],
-                    planes[f][:].rearrange("p (t m) -> p t m", t=last)[:, :, c0 : c0 + w].rearrange("p t (g i) -> p g t i", i=8),
-                )
+        def feature_tile(width):
+            return ring.tile([P, 2 * width], F32, name="feat", tag="feat")
 
         scatter(0, 2)
         wb_s_raw = shared("h01", "wb_s_raw", [P, N], U8)
@@ -199,20 +190,20 @@ def tile_list_electrode_refit_kernel(
         for q in range(4):
             nc.gpsimd.dma_start(wb_s_raw[QUAD * q : QUAD * q + 4, :].bitcast(I32), wb_scales[0, 4 * q : 4 * q + 4, :].bitcast(I32))
         grouped = [round_weight(i) for i in range(3)]
-        whole_slot(0)
+        features(0, read_page(0)[:], 0, shared("tab1", "feat_first", [P, 2 * M], F32), 0)
         scatter(1, 1)
-        whole_slot(1)
+        features(1, read_page(1)[:], 0, feature_tile(M), 0)
         scatter(2, 1)
-        whole_slot(2)
-        weave(0)
-        weave(1)
+        x2 = read_page(2)
+        early = CHUNKS[-1][0]
+        features(2, x2[:, 0:early], 0, feature_tile(early), 0)
         w_w = [shared(tag, "w_w%d" % i, [P, N], U32) for i, tag in enumerate(("v01", "v11", "h2"))]
         wb_w = shared("v00", "wb_w", [P, N], I32)
         wb_s = shared("v10", "wb_s", [P, N], U8)
         for i in range(3):
             nc.vector.quantize_mx(w_w[i][:].bitcast(FP8X4), w_s[i][:], grouped[i][:])
-        nc.vector.tensor_copy(wb_w[:].rearrange("p (t m) -> p m t", t=PACK), wb_w_raw[:].rearrange("p (m t) -> p m t", t=PACK))
-        nc.vector.tensor_copy(wb_s[:].rearrange("p (t m) -> p m t", t=PACK), wb_s_raw[:].rearrange("p (m t) -> p m t", t=PACK))
+        nc.vector.tensor_copy(wb_w[:].rearrange("p (t m) -> p t m", t=PACK), wb_w_raw[:].rearrange("p (m t) -> p t m", t=PACK))
+        nc.vector.tensor_copy(wb_s[:].rearrange("p (t m) -> p t m", t=PACK), wb_s_raw[:].rearrange("p (m t) -> p t m", t=PACK))
         scatter(3, 1)
 
         z_w = [[held("z_w%d_%d" % (f, c), [P, w], U32) for c, (c0, w) in enumerate(CHUNKS)] for f in range(2)]
@@ -225,8 +216,7 @@ def tile_list_electrode_refit_kernel(
         def finish_z(c):
             c0, w = CHUNKS[c]
             nc.vector.tensor_copy(x_last[c][:], page[last][:].indirect(idx3[:, c0 // 16 : (c0 + w) // 16]))
-            both = ring.tile([P, 2 * w], F32, name="feat", tag="feat")
-            features(x_last[c][:], both, [z_bf[f][:, PACK * c0 + last : PACK * (c0 + w) : PACK] for f in range(2)], last, 2 if c == 0 else 1)
+            features(last, x_last[c][:], c0, feature_tile(w), 2 if c == 0 else 1)
             for f in range(2):
                 nc.vector.quantize_mx(z_w[f][c][:].bitcast(FP8X4), z_s[f][c][:], z_bf[f][:, PACK * c0 : PACK * (c0 + w)])
 
@@ -266,7 +256,7 @@ def tile_list_electrode_refit_kernel(
             nc.sync.dma_start(y_rows[:, :, c0 : c0 + w], y[:])
             y_bf = held("y_bf%d" % c, [P, w * PACK], BF16)
             cast = nc.vector.tensor_copy if c == len(CHUNKS) - 1 else nc.scalar.copy
-            cast(y_bf[:].rearrange("p (g i t) -> p g t i", i=4, t=PACK), y[:].rearrange("p t (g i) -> p g t i", i=4))
+            cast(y_bf[:].rearrange("p (m t) -> p m t", t=PACK), y[:].rearrange("p t m -> p m t"))
             y_w = held("y_w%d" % c, [P, w], I32)
             nc.vector.quantize_mx(y_w[:].bitcast(FP8X4), y_s[:, c0 : c0 + w], y_bf[:])
             nc.sync.dma_start(code_rows[:, PACK * c0 : PACK * (c0 + w)].bitcast(I32), y_w[:])
@@ -274,7 +264,7 @@ def tile_list_electrode_refit_kernel(
         finish_z(0)
         finish_z(1)
         finish_y(0)
-        weave(2)
+        features(2, x2[:, early:M], early, feature_tile(M - early), 0)
         finish_z(2)
         finish_y(1)
         finish_y(2)

@@ -57,10 +57,14 @@ def tile_list_electrode_refit_kernel(
                 w1_scales[:, 4 * q : 4 * q + 4, :].rearrange("a r c -> r a c").bitcast(I32),
             )
         nc.vector.memset(v_s[:].rearrange("p a c -> p (a c)").bitcast(I32), 0)
-        warm = shared("warm", "warm", [P, 1], F32)
-        warm_out = shared("warm_out", "warm_out", [P, 1], F32)
-        nc.vector.memset(warm[:], 0.0)
+        warm = held("warm", [P, 1], F32)
+        warm_out = held("warm_out", [P, 1], F32)
+        nc.gpsimd.memset(warm[:], 0.0)
         nc.scalar.activation(warm_out[:], warm[:], ACT.Sin)
+        gain_sb = held("gain_sb", [P, 2, PACK], F32)
+        bias_sb = held("bias_sb", [P, PACK], F32)
+        nc.scalar.dma_start(gain_sb[:], gain.rearrange("(f p t) -> p f t", f=2, t=PACK))
+        nc.scalar.dma_start(bias_sb[:], bias.rearrange("(p t) -> p t", t=PACK))
 
         nc.sync.dma_start(idx[:], offs)
         nc.sync.dma_start(tab_s[96:128, :].bitcast(I32), tab_scales.rearrange("a q n -> q a n").bitcast(I32))
@@ -80,10 +84,13 @@ def tile_list_electrode_refit_kernel(
             page[t] = shared(tag, "page%d" % t, [P, T2], F32)
             nc.sync.dma_start(page[t][:], page_rows[t])
 
-        def load_wg(t, tag):
+        def load_wg(t, tag, parts):
             wg[t] = shared(tag, "wg%d" % t, [P, S], F32)
-            for q in (0, 2, 1, 3):
-                nc.sync.dma_start(wg[t][QUAD * q : QUAD * (q + 1), :], wgs_rows[t])
+            width = S // parts
+            for u in range(parts):
+                cols = slice(width * u, width * (u + 1))
+                for q in (0, 2, 1, 3):
+                    nc.sync.dma_start(wg[t][QUAD * q : QUAD * (q + 1), cols], wgs_rows[t][:, cols])
 
         w_src = (wa, wd[0:H, :], wd[H:F, :])
 
@@ -97,13 +104,13 @@ def tile_list_electrode_refit_kernel(
             nc.sync.dma_start(v_s[QUAD * q : QUAD * q + 4, :, :].bitcast(I32), picked_s[96 + 8 * q : 104 + 8 * q, :].bitcast(I32))
         load_page(0, "tab_s")
 
-        w1_w = shared("w1_w", "w1_w", [P, 2, PACK, 2 * P], U8)
+        w1_w = [shared("w1_w%d" % a, "w1_w%d" % a, [P, PACK, 2 * P], U8) for a in range(2)]
         for a in range(2):
             nc.vector.tensor_copy(
-                w1_w[:, a, :, :].bitcast(U16),
+                w1_w[a][:].bitcast(U16),
                 w1_w_raw[:, a, :].bitcast(U16).rearrange("p (m t) -> p t m", t=PACK),
             )
-        load_wg(0, "w1")
+        load_wg(0, "w1", 2)
 
         v_tags = (("v00", "v01"), ("v10", "v11"))
         v_w = [[None, None], [None, None]]
@@ -114,11 +121,6 @@ def tile_list_electrode_refit_kernel(
             if a == 0:
                 w1_s = shared("tab0", "w1_s", [P, 2, PACK, P], U8)
                 nc.vector.tensor_copy(w1_s[:], w1_s_raw[:].rearrange("p a (m t) -> p a t m", t=PACK))
-        gain_sb = shared("warm_out", "gain_sb", [P, 2, PACK], F32)
-        bias_sb = shared("warm", "bias_sb", [P, PACK], F32)
-        nc.gpsimd.dma_start(gain_sb[:], gain.rearrange("(f p t) -> p f t", f=2, t=PACK))
-        nc.gpsimd.dma_start(bias_sb[:], bias.rearrange("(p t) -> p t", t=PACK))
-
 
         h_sb = [[shared("h%d%d" % (t, u), "h_sb%d_%d" % (t, u), [P, HALF], F32) for u in range(2)] if t == 0 else shared("h%d" % t, "h_sb%d" % t, [P, S], F32) for t in range(PACK)]
         for t in range(PACK):
@@ -127,22 +129,26 @@ def tile_list_electrode_refit_kernel(
                 acc = psum.tile([P, HALF], F32, name="acc", tag="bank")
                 for a in range(2):
                     nc.tensor.matmul_mx(
-                        acc[:], lhsT=w1_w[:, a, t, :].bitcast(FP4X4), lhsT_scale=w1_s[:, a, t, :],
+                        acc[:], lhsT=w1_w[a][:, t, :].bitcast(FP4X4), lhsT_scale=w1_s[:, a, t, :],
                         rhs=v_w[a][u][:].bitcast(FP8X4), rhs_scale=v_s[:, a, cols], start=(a == 0), stop=(a == 1),
                     )
                 nc.scalar.copy(h_sb[t][u][:] if t == 0 else h_sb[t][:, cols], acc[:])
 
         load_weight(0, "picked")
         load_weight(1, "w1_s_raw")
-        load_weight(2, "tab1")
-        load_page(1, "v00")
-        load_wg(1, "v10")
+        load_page(1, "tab1")
+        load_wg(1, "v00", 2)
+        load_weight(2, "v10")
         load_page(2, "v01")
-        load_wg(2, "v11")
+        load_wg(2, "v11", 1)
         wb_w_raw = shared("tab0", "wb_w_raw", [P, N], I32)
         nc.sync.dma_start(wb_w_raw[:], wb_words[0].rearrange("p c i -> p (c i)").bitcast(I32))
-        load_page(3, "w1_w")
-        load_wg(3, "v_s")
+        wb_s_raw = shared("w1_w0", "wb_s_raw", [P, N], U8)
+        nc.gpsimd.memset(wb_s_raw[:].bitcast(I32), 0)
+        for q in range(4):
+            nc.sync.dma_start(wb_s_raw[QUAD * q : QUAD * q + 4, :].bitcast(I32), wb_scales[0, 4 * q : 4 * q + 4, :].bitcast(I32))
+        load_page(3, "w1_w1")
+        load_wg(3, "v_s", 1)
 
         w_s = [held("w_s%d" % i, [P, N], U8) for i in range(3)]
 
@@ -161,7 +167,7 @@ def tile_list_electrode_refit_kernel(
             for u in range(parts):
                 cols = slice(width * u, width * (u + 1))
                 where = idx2[:, width // 16 * u : width // 16 * (u + 1)]
-                nc.vector.tensor_tensor(page[t][:].indirect(where), h_sb[t][u][:] if t == 0 else h_sb[t][:], wg[t][:, cols], ALU.mult)
+                nc.vector.tensor_tensor(page[t][:].indirect(where), h_sb[t][u][:] if t == 0 else h_sb[t][:, cols], wg[t][:, cols], ALU.mult)
 
         last = PACK - 1
 
@@ -185,22 +191,21 @@ def tile_list_electrode_refit_kernel(
             return ring.tile([P, 2 * width], F32, name="feat", tag="feat")
 
         scatter(0, 2)
-        wb_s_raw = shared("h01", "wb_s_raw", [P, N], U8)
-        nc.gpsimd.memset(wb_s_raw[:].bitcast(I32), 0)
-        for q in range(4):
-            nc.gpsimd.dma_start(wb_s_raw[QUAD * q : QUAD * q + 4, :].bitcast(I32), wb_scales[0, 4 * q : 4 * q + 4, :].bitcast(I32))
-        grouped = [round_weight(i) for i in range(3)]
-        features(0, read_page(0)[:], 0, shared("tab1", "feat_first", [P, 2 * M], F32), 0)
-        scatter(1, 1)
-        features(1, read_page(1)[:], 0, feature_tile(M), 0)
+        grouped = [round_weight(0), round_weight(1)]
+        features(0, read_page(0)[:], 0, shared("w1_s_raw", "feat_slot0", [P, 2 * M], F32), 0)
+        grouped.append(round_weight(2))
+        w_w = [held("w_w0", [P, N], U32)]
+        nc.vector.quantize_mx(w_w[0][:].bitcast(FP8X4), w_s[0][:], grouped[0][:])
+        scatter(1, 2)
+        features(1, read_page(1)[:], 0, shared("v10", "feat_slot1", [P, 2 * M], F32), 0)
         scatter(2, 1)
         x2 = read_page(2)
         early = CHUNKS[-1][0]
         features(2, x2[:, 0:early], 0, feature_tile(early), 0)
-        w_w = [shared(tag, "w_w%d" % i, [P, N], U32) for i, tag in enumerate(("v01", "v11", "h2"))]
-        wb_w = shared("v00", "wb_w", [P, N], I32)
-        wb_s = shared("v10", "wb_s", [P, N], U8)
-        for i in range(3):
+        w_w.extend([shared("v01", "w_w1", [P, N], U32), shared("v11", "w_w2", [P, N], U32)])
+        wb_w = shared("h2", "wb_w", [P, N], I32)
+        wb_s = shared("v00", "wb_s", [P, N], U8)
+        for i in (1, 2):
             nc.vector.quantize_mx(w_w[i][:].bitcast(FP8X4), w_s[i][:], grouped[i][:])
         nc.vector.tensor_copy(wb_w[:].rearrange("p (t m) -> p t m", t=PACK), wb_w_raw[:].rearrange("p (m t) -> p t m", t=PACK))
         nc.vector.tensor_copy(wb_s[:].rearrange("p (t m) -> p t m", t=PACK), wb_s_raw[:].rearrange("p (m t) -> p t m", t=PACK))

@@ -20,7 +20,9 @@ P = 128
 PACK = 4
 QUAD = 32
 HALF = 512
-CHUNKS = ((0, 256), (256, 512), (768, 256))
+W = 256
+NCH = M // W
+KB = 1024
 
 
 def tile_list_electrode_refit_kernel(
@@ -30,220 +32,220 @@ def tile_list_electrode_refit_kernel(
     nc = tc.nc
     with ExitStack() as ctx:
         lists = ctx.enter_context(tc.tile_pool(name="lists", bufs=1))
+        arena = ctx.enter_context(tc.tile_pool(name="arena", bufs=1))
         keep = ctx.enter_context(tc.tile_pool(name="keep", bufs=1))
-        ring = ctx.enter_context(tc.tile_pool(name="ring", bufs=2))
         deep = ctx.enter_context(tc.tile_pool(name="deep", bufs=4))
         psum = ctx.enter_context(tc.psum_pool(name="psum", bufs=8))
 
         def held(name, shape, dtype):
             return keep.tile(shape, dtype, name=name, align_bytes=64)
 
+        def placed(name, shape, dtype, kb):
+            return arena.tile(shape, dtype, name=name, align_bytes=64, offset=int(kb * KB))
+
         idx = lists.tile([P, S // 16], U16, name="idx")
         idx2 = lists.tile([P, S // 16], U16, name="idx2")
         idx3 = lists.tile([P, M // 16], U16, name="idx3")
 
-        def shared(tag, name, shape, dtype):
-            return keep.tile(shape, dtype, name=name, tag=tag, align_bytes=64)
-
-        tab_s = shared("tab_s", "tab_s", [P, T], U8)
-        w1_s_raw = shared("w1_s_raw", "w1_s_raw", [P, 2, H], U8)
-        v_s = shared("v_s", "v_s", [P, 2, S], U8)
-        nc.vector.memset(tab_s[0:96, :].bitcast(I32), 0)
+        tab_s = placed("tab_s", [P, T], U8, 16)
+        w1_s_raw = placed("w1_s_raw", [P, 2, H], U8, 50)
+        v_s = placed("v_s", [P, 2, S], U8, 56)
         nc.gpsimd.memset(w1_s_raw[:].rearrange("p a c -> p (a c)").bitcast(I32), 0)
+        nc.vector.memset(tab_s[0:96, :].bitcast(I32), 0)
+        nc.vector.memset(v_s[:].rearrange("p a c -> p (a c)").bitcast(I32), 0)
         for q in range(4):
             eng = nc.gpsimd if q % 2 == 0 else nc.scalar
             eng.dma_start(
                 w1_s_raw[QUAD * q : QUAD * q + 4, :, :].bitcast(I32),
                 w1_scales[:, 4 * q : 4 * q + 4, :].rearrange("a r c -> r a c").bitcast(I32),
             )
-        nc.vector.memset(v_s[:].rearrange("p a c -> p (a c)").bitcast(I32), 0)
         warm = held("warm", [P, 1], F32)
         warm_out = held("warm_out", [P, 1], F32)
         nc.gpsimd.memset(warm[:], 0.0)
         nc.scalar.activation(warm_out[:], warm[:], ACT.Sin)
-        gain_sb = held("gain_sb", [P, 2, PACK], F32)
-        bias_sb = held("bias_sb", [P, PACK], F32)
-        nc.scalar.dma_start(gain_sb[:], gain.rearrange("(f p t) -> p f t", f=2, t=PACK))
-        nc.scalar.dma_start(bias_sb[:], bias.rearrange("(p t) -> p t", t=PACK))
 
         nc.sync.dma_start(idx[:], offs)
         nc.sync.dma_start(tab_s[96:128, :].bitcast(I32), tab_scales.rearrange("a q n -> q a n").bitcast(I32))
         nc.sync.dma_start(idx2[:], offs2)
         nc.sync.dma_start(idx3[:], offs3)
-        tab_w = [shared("tab%d" % a, "tab_w%d" % a, [P, T], I32) for a in range(2)]
-        w1_w_raw = shared("w1", "w1_w_raw", [P, 2, 2 * H], U8)
-        nc.sync.dma_start(tab_w[0][:], tab_words[0].rearrange("p t i -> p (t i)").bitcast(I32))
+        w1_w_raw = placed("w1_w_raw", [P, 2, 2 * H], U8, 24)
         nc.sync.dma_start(w1_w_raw[:].bitcast(I32), w1_words.rearrange("a p c -> p a c").bitcast(I32))
-        nc.sync.dma_start(tab_w[1][:], tab_words[1].rearrange("p t i -> p (t i)").bitcast(I32))
+        tab_w = [placed("tab_w%d" % a, [P, T], I32, 97 * a) for a in range(2)]
+        for a in range(2):
+            nc.sync.dma_start(tab_w[a][:], tab_words[a].rearrange("p t i -> p (t i)").bitcast(I32))
 
         page_rows = page0.rearrange("(p t) n -> t p n", t=PACK)
         wgs_rows = wgs.rearrange("(i t) j -> t i j", t=PACK)
         page, wg, w_raw = {}, {}, {}
 
-        def load_page(t, tag):
-            page[t] = shared(tag, "page%d" % t, [P, T2], F32)
+        def load_page(t, kb):
+            page[t] = placed("page%d" % t, [P, T2], F32, kb)
             nc.sync.dma_start(page[t][:], page_rows[t])
 
-        def load_wg(t, tag, parts):
-            wg[t] = shared(tag, "wg%d" % t, [P, S], F32)
-            width = S // parts
-            for u in range(parts):
-                cols = slice(width * u, width * (u + 1))
-                for q in (0, 2, 1, 3):
-                    nc.sync.dma_start(wg[t][QUAD * q : QUAD * (q + 1), cols], wgs_rows[t][:, cols])
+        def load_wg(t, kb):
+            wg[t] = placed("wg%d" % t, [P, S], F32, kb)
+            for q in (0, 2, 1, 3):
+                nc.sync.dma_start(wg[t][QUAD * q : QUAD * (q + 1), :], wgs_rows[t])
 
         w_src = (wa, wd[0:H, :], wd[H:F, :])
 
-        def load_weight(i, tag):
-            w_raw[i] = shared(tag, "w_raw%d" % i, [P, PACK, N], F32)
+        def load_weight(i, kb):
+            w_raw[i] = placed("w_raw%d" % i, [P, PACK, N], F32, kb)
             nc.sync.dma_start(w_raw[i][:], w_src[i].rearrange("(p j) n -> p j n", j=PACK))
 
-        picked_s = shared("picked", "picked_s", [P, S], U8)
+        picked_s = placed("picked_s", [P, S], U8, 35)
         nc.vector.tensor_copy(picked_s[:], tab_s[:].indirect(idx[:]))
         for q in range(4):
             nc.sync.dma_start(v_s[QUAD * q : QUAD * q + 4, :, :].bitcast(I32), picked_s[96 + 8 * q : 104 + 8 * q, :].bitcast(I32))
-        load_page(0, "tab_s")
+        load_page(0, 16)
 
-        w1_w = [shared("w1_w%d" % a, "w1_w%d" % a, [P, PACK, 2 * P], U8) for a in range(2)]
-        for a in range(2):
-            nc.vector.tensor_copy(
-                w1_w[a][:].bitcast(U16),
-                w1_w_raw[:, a, :].bitcast(U16).rearrange("p (m t) -> p t m", t=PACK),
-            )
-        load_wg(0, "w1", 2)
+        w1_w = placed("w1_w", [P, 2, PACK, 2 * P], U8, 71)
+        nc.vector.tensor_copy(w1_w[:].bitcast(U16), w1_w_raw[:].bitcast(U16).rearrange("p a (m t) -> p a t m", t=PACK))
+        load_wg(0, 24)
+        w1_s = placed("w1_s", [P, 2, PACK, P], U8, 0)
+        nc.vector.tensor_copy(w1_s[:], w1_s_raw[:].rearrange("p a (m t) -> p a t m", t=PACK))
 
-        v_tags = (("v00", "v01"), ("v10", "v11"))
-        v_w = [[None, None], [None, None]]
-        for a in range(2):
-            for u in range(2):
-                v_w[a][u] = shared(v_tags[a][u], "v_w%d_%d" % (a, u), [P, HALF], U32)
-                nc.vector.tensor_copy(v_w[a][u][:], tab_w[a][:].bitcast(U32).indirect(idx[:, 32 * u : 32 * (u + 1)]))
-            if a == 0:
-                w1_s = shared("tab0", "w1_s", [P, 2, PACK, P], U8)
-                nc.vector.tensor_copy(w1_s[:], w1_s_raw[:].rearrange("p a (m t) -> p a t m", t=PACK))
+        first = ((0, 256), (256, 512), (768, 256))
+        v_w = [placed("v_w0", [P, S], U32, 36), placed("v_w1", [P, S], U32, 50)]
+        nc.vector.tensor_copy(v_w[0][:], tab_w[0][:].bitcast(U32).indirect(idx[:]))
+        for c0, w in first:
+            nc.vector.tensor_copy(v_w[1][:, c0 : c0 + w], tab_w[1][:].bitcast(U32).indirect(idx[:, c0 // 16 : (c0 + w) // 16]))
 
-        h_sb = [[shared("h%d%d" % (t, u), "h_sb%d_%d" % (t, u), [P, HALF], F32) for u in range(2)] if t == 0 else shared("h%d" % t, "h_sb%d" % t, [P, S], F32) for t in range(PACK)]
-        for t in range(PACK):
-            for u in range(2):
-                cols = slice(HALF * u, HALF * (u + 1))
-                acc = psum.tile([P, HALF], F32, name="acc", tag="bank")
+        h_first = [placed("h0_%d" % u, [P, w], F32, (93, 78, 80)[u]) for u, (c0, w) in enumerate(first)]
+        h_sb = {t: placed("h%d" % t, [P, S], F32, 77 + 4 * t) for t in range(1, PACK)}
+
+        def make_h(t, c0, w, target):
+            acc = psum.tile([P, w], F32, name="acc", tag="bank")
+            n = HALF if w == HALF else P
+            for b in range(0, w, n):
+                cols = slice(c0 + b, c0 + b + n)
                 for a in range(2):
                     nc.tensor.matmul_mx(
-                        acc[:], lhsT=w1_w[a][:, t, :].bitcast(FP4X4), lhsT_scale=w1_s[:, a, t, :],
-                        rhs=v_w[a][u][:].bitcast(FP8X4), rhs_scale=v_s[:, a, cols], start=(a == 0), stop=(a == 1),
+                        acc[:, b : b + n], lhsT=w1_w[:, a, t, :].bitcast(FP4X4), lhsT_scale=w1_s[:, a, t, :],
+                        rhs=v_w[a][:, cols].bitcast(FP8X4), rhs_scale=v_s[:, a, cols], start=(a == 0), stop=(a == 1),
                     )
-                nc.scalar.copy(h_sb[t][u][:] if t == 0 else h_sb[t][:, cols], acc[:])
+            nc.scalar.copy(target, acc[:])
 
-        load_weight(0, "picked")
-        load_weight(1, "w1_s_raw")
-        load_page(1, "tab1")
-        load_wg(1, "v00", 2)
-        load_weight(2, "v10")
-        load_page(2, "v01")
-        load_wg(2, "v11", 1)
-        wb_w_raw = shared("tab0", "wb_w_raw", [P, N], I32)
+        for u, (c0, w) in enumerate(first):
+            make_h(0, c0, w, h_first[u][:])
+        for t in range(1, PACK):
+            for c0 in (0, HALF):
+                make_h(t, c0, HALF, h_sb[t][:, c0 : c0 + HALF])
+
+        load_weight(0, 28)
+        load_weight(1, 1)
+        load_page(1, 97)
+        load_wg(1, 93)
+        gain_sb = placed("gain_sb", [P, 2, PACK], F32, 56)
+        bias_sb = placed("bias_sb", [P, PACK], F32, 56.0625)
+        nc.sync.dma_start(gain_sb[:], gain.rearrange("(f p t) -> p f t", f=2, t=PACK))
+        load_weight(2, 36)
+        load_page(2, 44)
+        load_wg(2, 57)
+        nc.sync.dma_start(bias_sb[:], bias.rearrange("(p t) -> p t", t=PACK))
+        wb_w_raw = placed("wb_w_raw", [P, N], I32, 52)
         nc.sync.dma_start(wb_w_raw[:], wb_words[0].rearrange("p c i -> p (c i)").bitcast(I32))
-        wb_s_raw = shared("w1_w0", "wb_s_raw", [P, N], U8)
+        wb_s_raw = placed("wb_s_raw", [P, N], U8, 56.25)
         nc.gpsimd.memset(wb_s_raw[:].bitcast(I32), 0)
         for q in range(4):
             nc.sync.dma_start(wb_s_raw[QUAD * q : QUAD * q + 4, :].bitcast(I32), wb_scales[0, 4 * q : 4 * q + 4, :].bitcast(I32))
-        load_page(3, "w1_w1")
-        load_wg(3, "v_s", 1)
+        load_page(3, 64)
+        load_wg(3, 72)
 
         w_s = [held("w_s%d" % i, [P, N], U8) for i in range(3)]
+        w_w = {}
 
         def round_weight(i):
-            grouped = shared(("h00", "picked", "w1_s_raw")[i], "grouped%d" % i, [P, N * PACK], BF16)
+            grouped = held("grouped%d" % i, [P, N * PACK], BF16)
             nc.scalar.copy(
-                grouped[:].rearrange("p (t m j) -> p m t j", t=PACK, j=PACK),
-                w_raw[i][:].rearrange("p j (m t) -> p m t j", t=PACK),
+                grouped[:].rearrange("p (t m j) -> p m j t", t=PACK, j=PACK),
+                w_raw[i][:].rearrange("p j (m t) -> p m j t", t=PACK),
             )
             return grouped
 
-        z_bf = [held("z_bf%d" % f, [P, M * PACK], BF16) for f in range(2)]
+        def quantise_weight(i, words, grouped):
+            w_w[i] = words
+            nc.vector.quantize_mx(words[:].bitcast(FP8X4), w_s[i][:], grouped[:])
 
-        def scatter(t, parts):
-            width = S // parts
-            for u in range(parts):
-                cols = slice(width * u, width * (u + 1))
-                where = idx2[:, width // 16 * u : width // 16 * (u + 1)]
-                nc.vector.tensor_tensor(page[t][:].indirect(where), h_sb[t][u][:] if t == 0 else h_sb[t][:, cols], wg[t][:, cols], ALU.mult)
+        pairs = [held("pairs%d" % c, [P, 2, 2, 2 * W], BF16) for c in range(NCH)]
+        z_bf = [held("z_bf%d" % c, [P, 2 * W * PACK], BF16) for c in range(NCH)]
 
-        last = PACK - 1
+        def scatter(t):
+            if t == 0:
+                for u, (c0, w) in enumerate(first):
+                    where = idx2[:, c0 // 16 : (c0 + w) // 16]
+                    nc.vector.tensor_tensor(page[t][:].indirect(where), h_first[u][:], wg[t][:, c0 : c0 + w], ALU.mult)
+            else:
+                nc.vector.tensor_tensor(page[t][:].indirect(idx2[:]), h_sb[t][:], wg[t][:], ALU.mult)
 
-        def features(t, x, c0, both, on_vector):
-            width = x.shape[1]
+        def features(t, x, c0, n, kb, on_vector):
+            both = placed("feat%d_%d" % (t, c0), [P, 2, n * W], F32, kb)
             for f, func in enumerate((ACT.Sin, ACT.Square)):
-                feat = both[:, f * width : (f + 1) * width]
-                nc.scalar.activation(feat, x, func)
-                target = z_bf[f][:, PACK * c0 + t : PACK * (c0 + width) : PACK]
-                if f < on_vector:
-                    nc.vector.tensor_scalar(target, feat, gain_sb[:, f, t : t + 1], None, ALU.mult)
-                else:
-                    nc.scalar.activation(target, feat, ACT.Copy, scale=gain_sb[:, f, t : t + 1])
+                nc.scalar.activation(both[:, f, :], x, func)
+                for c in range(n):
+                    feat = both[:, f, W * c : W * (c + 1)]
+                    target = pairs[c0 + c][:, t // 2, f, t % 2 : 2 * W : 2]
+                    if f < on_vector:
+                        nc.vector.tensor_scalar(target, feat, gain_sb[:, f, t : t + 1], None, ALU.mult)
+                    else:
+                        nc.scalar.activation(target, feat, ACT.Copy, scale=gain_sb[:, f, t : t + 1])
+
+        def weave(c, copy, dtype):
+            copy(
+                z_bf[c][:].bitcast(dtype).rearrange("p (m u) -> p m u", u=2),
+                pairs[c][:].rearrange("p u f m -> p u (f m)").bitcast(dtype).rearrange("p u m -> p m u"),
+            )
 
         def read_page(t):
-            x = ring.tile([P, M], F32, name="x", tag="x")
+            x = held("x%d" % t, [P, M], F32)
             nc.vector.tensor_copy(x[:], page[t][:].indirect(idx3[:]))
             return x
 
-        def feature_tile(width):
-            return ring.tile([P, 2 * width], F32, name="feat", tag="feat")
-
-        scatter(0, 2)
+        scatter(0)
         grouped = [round_weight(0), round_weight(1)]
-        features(0, read_page(0)[:], 0, shared("w1_s_raw", "feat_slot0", [P, 2 * M], F32), 0)
+        features(0, read_page(0)[:], 0, NCH, 1, 0)
         grouped.append(round_weight(2))
-        w_w = [held("w_w0", [P, N], U32)]
-        nc.vector.quantize_mx(w_w[0][:].bitcast(FP8X4), w_s[0][:], grouped[0][:])
-        scatter(1, 2)
-        features(1, read_page(1)[:], 0, shared("v10", "feat_slot1", [P, 2 * M], F32), 0)
-        scatter(2, 1)
-        x2 = read_page(2)
-        early = CHUNKS[-1][0]
-        features(2, x2[:, 0:early], 0, feature_tile(early), 0)
-        w_w.extend([shared("v01", "w_w1", [P, N], U32), shared("v11", "w_w2", [P, N], U32)])
-        wb_w = shared("h2", "wb_w", [P, N], I32)
-        wb_s = shared("v00", "wb_s", [P, N], U8)
-        for i in (1, 2):
-            nc.vector.quantize_mx(w_w[i][:].bitcast(FP8X4), w_s[i][:], grouped[i][:])
-        nc.vector.tensor_copy(wb_w[:].rearrange("p (t m) -> p t m", t=PACK), wb_w_raw[:].rearrange("p (m t) -> p t m", t=PACK))
-        nc.vector.tensor_copy(wb_s[:].rearrange("p (t m) -> p t m", t=PACK), wb_s_raw[:].rearrange("p (m t) -> p t m", t=PACK))
-        scatter(3, 1)
+        scatter(1)
+        quantise_weight(0, placed("w_w0", [P, N], U32, 93), grouped[0])
+        features(1, read_page(1)[:], 0, NCH, 28, 0)
+        scatter(2)
+        quantise_weight(1, placed("w_w1", [P, N], U32, 57), grouped[1])
+        features(2, read_page(2)[:], 0, NCH, 1, 0)
+        scatter(3)
 
-        z_w = [[held("z_w%d_%d" % (f, c), [P, w], U32) for c, (c0, w) in enumerate(CHUNKS)] for f in range(2)]
-        z_s = [[held("z_s%d_%d" % (f, c), [P, w], U8) for c, (c0, w) in enumerate(CHUNKS)] for f in range(2)]
-        x_last = [held("x_last%d" % c, [P, w], F32) for c, (c0, w) in enumerate(CHUNKS)]
+        last = PACK - 1
+        z_w = [held("z_w%d" % c, [P, 2, W], U32) for c in range(NCH)]
+        z_s = [held("z_s%d" % c, [P, 2, W], U8) for c in range(NCH)]
+        x_last = [held("x_last%d" % c, [P, W], F32) for c in range(NCH)]
         y_s = held("y_s", [P, M], U8)
         y_rows = out_0.rearrange("(p t) m -> p t m", t=PACK)
         code_rows = out_1[0].rearrange("p m t -> p (m t)")
 
-        def finish_z(c):
-            c0, w = CHUNKS[c]
-            nc.vector.tensor_copy(x_last[c][:], page[last][:].indirect(idx3[:, c0 // 16 : (c0 + w) // 16]))
-            features(last, x_last[c][:], c0, feature_tile(w), 2 if c == 0 else 1)
-            for f in range(2):
-                nc.vector.quantize_mx(z_w[f][c][:].bitcast(FP8X4), z_s[f][c][:], z_bf[f][:, PACK * c0 : PACK * (c0 + w)])
+        def read_last(c):
+            nc.vector.tensor_copy(x_last[c][:], page[last][:].indirect(idx3[:, W * c // 16 : W * (c + 1) // 16]))
+
+        def quantise_z(c):
+            nc.vector.quantize_mx(
+                z_w[c][:].rearrange("p f m -> p (f m)").bitcast(FP8X4), z_s[c][:].rearrange("p f m -> p (f m)"),
+                z_bf[c][:],
+            )
 
         def product(c, slots, terms):
-            w = CHUNKS[c][1]
-            acc = psum.tile([P, len(slots) * w], F32, name="acc", tag="bank")
+            acc = psum.tile([P, len(slots) * W], F32, name="acc", tag="bank")
             for i, t in enumerate(slots):
                 cols = slice(P * t, P * (t + 1))
                 for n, (words, scales, f) in enumerate(terms):
                     nc.tensor.matmul_mx(
-                        acc[:, i * w : (i + 1) * w], lhsT=words[:, cols].bitcast(FP8X4), lhsT_scale=scales[:, cols],
-                        rhs=z_w[f][c][:].bitcast(FP8X4), rhs_scale=z_s[f][c][:], start=(n == 0), stop=(n == len(terms) - 1),
+                        acc[:, i * W : (i + 1) * W], lhsT=words[:, cols].bitcast(FP8X4), lhsT_scale=scales[:, cols],
+                        rhs=z_w[c][:, f, :].bitcast(FP8X4), rhs_scale=z_s[c][:, f, :], start=(n == 0), stop=(n == len(terms) - 1),
                     )
             return acc
 
-        def finish_y(c):
-            c0, w = CHUNKS[c]
-            y = held("y%d" % c, [P, PACK, w], F32)
-            per_bank = HALF // w
+        def finish_y(c, cast):
+            y = held("y%d" % c, [P, PACK, W], F32)
             pending = None
-            for t0 in range(0, PACK + per_bank, per_bank):
-                slots = range(t0, t0 + per_bank)
+            for t0 in range(0, PACK + 2, 2):
+                slots = range(t0, t0 + 2)
                 if t0 < PACK:
                     a_ps = product(c, slots, [(w_w[0], w_s[0], 0)])
                     b_ps = product(c, slots, [(wb_w, wb_s, 1)])
@@ -255,24 +257,41 @@ def tile_list_electrode_refit_kernel(
                 if pending is not None:
                     done, d_prev, ab_prev = pending
                     for i, t in enumerate(done):
-                        cols = slice(i * w, (i + 1) * w)
+                        cols = slice(i * W, (i + 1) * W)
                         nc.vector.scalar_tensor_tensor(y[:, t, :], d_prev[:, cols], bias_sb[:, t : t + 1], ab_prev[:, cols], ALU.add, ALU.add)
                 pending = (slots, d_ps, ab)
-            nc.sync.dma_start(y_rows[:, :, c0 : c0 + w], y[:])
-            y_bf = held("y_bf%d" % c, [P, w * PACK], BF16)
-            cast = nc.vector.tensor_copy if c == len(CHUNKS) - 1 else nc.scalar.copy
-            cast(y_bf[:].rearrange("p (m t) -> p m t", t=PACK), y[:].rearrange("p t m -> p m t"))
-            y_w = held("y_w%d" % c, [P, w], I32)
-            nc.vector.quantize_mx(y_w[:].bitcast(FP8X4), y_s[:, c0 : c0 + w], y_bf[:])
-            nc.sync.dma_start(code_rows[:, PACK * c0 : PACK * (c0 + w)].bitcast(I32), y_w[:])
+            nc.sync.dma_start(y_rows[:, :, W * c : W * (c + 1)], y[:])
+            y_bf = held("y_bf%d" % c, [P, W * PACK], BF16)
+            cast(y_bf[:].rearrange("p (g i t) -> p g t i", i=4, t=PACK), y[:].rearrange("p t (g i) -> p g t i", i=4))
+            y_w = held("y_w%d" % c, [P, W], I32)
+            nc.vector.quantize_mx(y_w[:].bitcast(FP8X4), y_s[:, W * c : W * (c + 1)], y_bf[:])
+            nc.sync.dma_start(code_rows[:, PACK * W * c : PACK * W * (c + 1)].bitcast(I32), y_w[:])
 
-        finish_z(0)
-        finish_z(1)
-        finish_y(0)
-        features(2, x2[:, early:M], early, feature_tile(M - early), 0)
-        finish_z(2)
-        finish_y(1)
-        finish_y(2)
+        quantise_weight(2, placed("w_w2", [P, N], U32, 89), grouped[2])
+        read_last(0)
+        features(last, x_last[0][:], 0, 1, 28, 0)
+        read_last(1)
+        weave(0, nc.vector.tensor_copy, I32)
+        wb_w = placed("wb_w", [P, N], I32, 91)
+        wb_s = placed("wb_s", [P, N], U8, 72)
+        nc.vector.tensor_copy(wb_w[:].rearrange("p (t m) -> p t m", t=PACK), wb_w_raw[:].rearrange("p (m t) -> p t m", t=PACK))
+        nc.vector.tensor_copy(wb_s[:].rearrange("p (t m) -> p t m", t=PACK), wb_s_raw[:].rearrange("p (m t) -> p t m", t=PACK))
+        quantise_z(0)
+        features(last, x_last[1][:], 1, 1, 30, 0)
+        weave(1, nc.scalar.copy, U32)
+        read_last(2)
+        read_last(3)
+        quantise_z(1)
+        features(last, x_last[2][:], 2, 1, 32, 0)
+        finish_y(0, nc.scalar.copy)
+        weave(2, nc.scalar.copy, U32)
+        quantise_z(2)
+        features(last, x_last[3][:], 3, 1, 34, 0)
+        finish_y(1, nc.scalar.copy)
+        weave(3, nc.scalar.copy, U32)
+        quantise_z(3)
+        finish_y(2, nc.scalar.copy)
+        finish_y(3, nc.vector.tensor_copy)
         for q in range(4):
             eng = nc.sync if q % 2 == 0 else nc.scalar
             eng.dma_start(out_2[0, 4 * q : 4 * q + 4, :].bitcast(I32), y_s[QUAD * q : QUAD * q + 4, :].bitcast(I32))

@@ -70,7 +70,7 @@ def tile_list_electrode_refit_kernel(
         nc.sync.dma_start(idx3[:], offs3)
         w1_w_raw = placed("w1_w_raw", [P, 2, 2 * H], U8, 24)
         nc.sync.dma_start(w1_w_raw[:].bitcast(I32), w1_words.rearrange("a p c -> p a c").bitcast(I32))
-        tab_w = [placed("tab_w%d" % a, [P, T], I32, 97 * a) for a in range(2)]
+        tab_w = [placed("tab_w%d" % a, [P, T], I32, 8 * a) for a in range(2)]
         for a in range(2):
             nc.sync.dma_start(tab_w[a][:], tab_words[a].rearrange("p t i -> p (t i)").bitcast(I32))
 
@@ -93,7 +93,7 @@ def tile_list_electrode_refit_kernel(
             w_raw[i] = placed("w_raw%d" % i, [P, PACK, N], F32, kb)
             nc.sync.dma_start(w_raw[i][:], w_src[i].rearrange("(p j) n -> p j n", j=PACK))
 
-        picked_s = placed("picked_s", [P, S], U8, 35)
+        picked_s = placed("picked_s", [P, S], U8, 28)
         nc.vector.tensor_copy(picked_s[:], tab_s[:].indirect(idx[:]))
         for q in range(4):
             nc.sync.dma_start(v_s[QUAD * q : QUAD * q + 4, :, :].bitcast(I32), picked_s[96 + 8 * q : 104 + 8 * q, :].bitcast(I32))
@@ -132,16 +132,16 @@ def tile_list_electrode_refit_kernel(
             for c0 in (0, HALF):
                 make_h(t, c0, HALF, h_sb[t][:, c0 : c0 + HALF])
 
-        load_weight(0, 28)
-        load_weight(1, 1)
-        load_page(1, 97)
-        load_wg(1, 93)
-        gain_sb = placed("gain_sb", [P, 2, PACK], F32, 56)
-        bias_sb = placed("bias_sb", [P, PACK], F32, 56.0625)
+        load_page(1, 28)
+        load_wg(1, 1)
+        gain_sb = placed("gain_sb", [P, 2, PACK], F32, 5)
+        bias_sb = placed("bias_sb", [P, PACK], F32, 56)
         nc.sync.dma_start(gain_sb[:], gain.rearrange("(f p t) -> p f t", f=2, t=PACK))
-        load_weight(2, 36)
-        load_page(2, 44)
+        load_weight(0, 8)
+        load_weight(2, 93)
+        load_page(2, 36)
         load_wg(2, 57)
+        load_weight(1, 44)
         nc.sync.dma_start(bias_sb[:], bias.rearrange("(p t) -> p t", t=PACK))
         wb_w_raw = placed("wb_w_raw", [P, N], I32, 52)
         nc.sync.dma_start(wb_w_raw[:], wb_words[0].rearrange("p c i -> p (c i)").bitcast(I32))
@@ -202,15 +202,20 @@ def tile_list_electrode_refit_kernel(
             return x
 
         scatter(0)
-        grouped = [round_weight(0), round_weight(1)]
-        features(0, read_page(0)[:], 0, NCH, 1, 0)
-        grouped.append(round_weight(2))
+        grouped = {0: round_weight(0)}
+        features(0, read_page(0)[:], 0, NCH, 8, 0)
+        grouped[2] = round_weight(2)
         scatter(1)
-        quantise_weight(0, placed("w_w0", [P, N], U32, 93), grouped[0])
-        features(1, read_page(1)[:], 0, NCH, 28, 0)
+        quantise_weight(0, placed("w_w0", [P, N], U32, 1), grouped[0])
+        features(1, read_page(1)[:], 0, NCH, 93, 0)
+        grouped[1] = round_weight(1)
         scatter(2)
-        quantise_weight(1, placed("w_w1", [P, N], U32, 57), grouped[1])
-        features(2, read_page(2)[:], 0, NCH, 1, 0)
+        quantise_weight(2, placed("w_w2", [P, N], U32, 57), grouped[2])
+        wb_w = placed("wb_w", [P, N], I32, 85)
+        wb_s = placed("wb_s", [P, N], U8, 87)
+        nc.vector.tensor_copy(wb_w[:].rearrange("p (t m) -> p t m", t=PACK), wb_w_raw[:].rearrange("p (m t) -> p t m", t=PACK))
+        nc.vector.tensor_copy(wb_s[:].rearrange("p (t m) -> p t m", t=PACK), wb_s_raw[:].rearrange("p (m t) -> p t m", t=PACK))
+        features(2, read_page(2)[:], 0, NCH, 44, 0)
         scatter(3)
 
         last = PACK - 1
@@ -267,26 +272,18 @@ def tile_list_electrode_refit_kernel(
             nc.vector.quantize_mx(y_w[:].bitcast(FP8X4), y_s[:, W * c : W * (c + 1)], y_bf[:])
             nc.sync.dma_start(code_rows[:, PACK * W * c : PACK * W * (c + 1)].bitcast(I32), y_w[:])
 
-        quantise_weight(2, placed("w_w2", [P, N], U32, 89), grouped[2])
-        read_last(0)
-        features(last, x_last[0][:], 0, 1, 28, 0)
-        read_last(1)
-        weave(0, nc.vector.tensor_copy, I32)
-        wb_w = placed("wb_w", [P, N], I32, 91)
-        wb_s = placed("wb_s", [P, N], U8, 72)
-        nc.vector.tensor_copy(wb_w[:].rearrange("p (t m) -> p t m", t=PACK), wb_w_raw[:].rearrange("p (m t) -> p t m", t=PACK))
-        nc.vector.tensor_copy(wb_s[:].rearrange("p (t m) -> p t m", t=PACK), wb_s_raw[:].rearrange("p (m t) -> p t m", t=PACK))
-        quantise_z(0)
-        features(last, x_last[1][:], 1, 1, 30, 0)
-        weave(1, nc.scalar.copy, U32)
-        read_last(2)
-        read_last(3)
-        quantise_z(1)
-        features(last, x_last[2][:], 2, 1, 32, 0)
+        quantise_weight(1, placed("w_w1", [P, N], U32, 89), grouped[1])
+        for c in range(NCH):
+            read_last(c)
+        for c in range(2):
+            features(last, x_last[c][:], c, 1, 8 + 2 * c, 0)
+            weave(c, nc.vector.tensor_copy, I32)
+            quantise_z(c)
+        features(last, x_last[2][:], 2, 1, 12, 0)
         finish_y(0, nc.scalar.copy)
         weave(2, nc.scalar.copy, U32)
         quantise_z(2)
-        features(last, x_last[3][:], 3, 1, 34, 0)
+        features(last, x_last[3][:], 3, 1, 14, 0)
         finish_y(1, nc.scalar.copy)
         weave(3, nc.scalar.copy, U32)
         quantise_z(3)

@@ -59,10 +59,6 @@ def tile_list_electrode_refit_kernel(
                 w1_s_raw[QUAD * q : QUAD * q + 4, :, :].bitcast(I32),
                 w1_scales[:, 4 * q : 4 * q + 4, :].rearrange("a r c -> r a c").bitcast(I32),
             )
-        warm = held("warm", [P, 1], F32)
-        warm_out = held("warm_out", [P, 1], F32)
-        nc.gpsimd.memset(warm[:], 0.0)
-        nc.scalar.activation(warm_out[:], warm[:], ACT.Sin)
 
         nc.sync.dma_start(idx[:], offs)
         nc.sync.dma_start(tab_s[96:128, :].bitcast(I32), tab_scales.rearrange("a q n -> q a n").bitcast(I32))
@@ -82,10 +78,11 @@ def tile_list_electrode_refit_kernel(
             page[t] = placed("page%d" % t, [P, T2], F32, kb)
             nc.sync.dma_start(page[t][:], page_rows[t])
 
-        def load_wg(t, kb):
+        def load_wg(t, kb, cuts=(0, S)):
             wg[t] = placed("wg%d" % t, [P, S], F32, kb)
-            for q in (0, 2, 1, 3):
-                nc.sync.dma_start(wg[t][QUAD * q : QUAD * (q + 1), :], wgs_rows[t])
+            for c0, c1 in zip(cuts, cuts[1:]):
+                for q in (0, 2, 1, 3):
+                    nc.sync.dma_start(wg[t][QUAD * q : QUAD * (q + 1), c0:c1], wgs_rows[t][:, c0:c1])
 
         w_src = (wa, wd[0:H, :], wd[H:F, :])
 
@@ -93,7 +90,7 @@ def tile_list_electrode_refit_kernel(
             w_raw[i] = placed("w_raw%d" % i, [P, PACK, N], F32, kb)
             nc.sync.dma_start(w_raw[i][:], w_src[i].rearrange("(p j) n -> p j n", j=PACK))
 
-        picked_s = placed("picked_s", [P, S], U8, 28)
+        picked_s = placed("picked_s", [P, S], U8, 108.5)
         nc.vector.tensor_copy(picked_s[:], tab_s[:].indirect(idx[:]))
         for q in range(4):
             nc.sync.dma_start(v_s[QUAD * q : QUAD * q + 4, :, :].bitcast(I32), picked_s[96 + 8 * q : 104 + 8 * q, :].bitcast(I32))
@@ -101,7 +98,7 @@ def tile_list_electrode_refit_kernel(
 
         w1_w = placed("w1_w", [P, 2, PACK, 2 * P], U8, 71)
         nc.vector.tensor_copy(w1_w[:].bitcast(U16), w1_w_raw[:].bitcast(U16).rearrange("p a (m t) -> p a t m", t=PACK))
-        load_wg(0, 24)
+        load_wg(0, 24, (0, 256, S))
         w1_s = placed("w1_s", [P, 2, PACK, P], U8, 0)
         nc.vector.tensor_copy(w1_s[:], w1_s_raw[:].rearrange("p a (m t) -> p a t m", t=PACK))
 
@@ -111,29 +108,33 @@ def tile_list_electrode_refit_kernel(
         for c0, w in first:
             nc.vector.tensor_copy(v_w[1][:, c0 : c0 + w], tab_w[1][:].bitcast(U32).indirect(idx[:, c0 // 16 : (c0 + w) // 16]))
 
-        h_first = [placed("h0_%d" % u, [P, w], F32, (93, 78, 80)[u]) for u, (c0, w) in enumerate(first)]
+        h_head = placed("h_head", [P, 256], F32, 93)
+        h_rest = placed("h_rest", [P, S - 256], F32, 78)
         h_sb = {t: placed("h%d" % t, [P, S], F32, 77 + 4 * t) for t in range(1, PACK)}
 
         def make_h(t, c0, w, target):
             acc = psum.tile([P, w], F32, name="acc", tag="bank")
             n = HALF if w == HALF else P
-            for b in range(0, w, n):
-                cols = slice(c0 + b, c0 + b + n)
-                for a in range(2):
+            for a in range(2):
+                for b in range(0, w, n):
+                    cols = slice(c0 + b, c0 + b + n)
                     nc.tensor.matmul_mx(
                         acc[:, b : b + n], lhsT=w1_w[:, a, t, :].bitcast(FP4X4), lhsT_scale=w1_s[:, a, t, :],
-                        rhs=v_w[a][:, cols].bitcast(FP8X4), rhs_scale=v_s[:, a, cols], start=(a == 0), stop=(a == 1),
+                        rhs=v_w[a][:, cols].bitcast(FP8X4), rhs_scale=v_s[:, a, cols],
+                        start=(a == 0 and b == 0), stop=(a == 1 and b == w - n),
                     )
             nc.scalar.copy(target, acc[:])
 
         for u, (c0, w) in enumerate(first):
-            make_h(0, c0, w, h_first[u][:])
+            make_h(0, c0, w, h_head[:] if u == 0 else h_rest[:, c0 - 256 : c0 - 256 + w])
         for t in range(1, PACK):
             for c0 in (0, HALF):
                 make_h(t, c0, HALF, h_sb[t][:, c0 : c0 + HALF])
 
-        load_page(1, 28)
         load_wg(1, 1)
+        load_page(1, 101)
+        wb_w_raw = placed("wb_w_raw", [P, N], I32, 109)
+        nc.sync.dma_start(wb_w_raw[:], wb_words[0].rearrange("p c i -> p (c i)").bitcast(I32))
         gain_sb = placed("gain_sb", [P, 2, PACK], F32, 5)
         bias_sb = placed("bias_sb", [P, PACK], F32, 56)
         nc.sync.dma_start(gain_sb[:], gain.rearrange("(f p t) -> p f t", f=2, t=PACK))
@@ -141,14 +142,12 @@ def tile_list_electrode_refit_kernel(
         load_weight(2, 93)
         load_page(2, 36)
         load_wg(2, 57)
-        load_weight(1, 44)
-        nc.sync.dma_start(bias_sb[:], bias.rearrange("(p t) -> p t", t=PACK))
-        wb_w_raw = placed("wb_w_raw", [P, N], I32, 52)
-        nc.sync.dma_start(wb_w_raw[:], wb_words[0].rearrange("p c i -> p (c i)").bitcast(I32))
         wb_s_raw = placed("wb_s_raw", [P, N], U8, 56.25)
         nc.gpsimd.memset(wb_s_raw[:].bitcast(I32), 0)
         for q in range(4):
             nc.sync.dma_start(wb_s_raw[QUAD * q : QUAD * q + 4, :].bitcast(I32), wb_scales[0, 4 * q : 4 * q + 4, :].bitcast(I32))
+        load_weight(1, 44)
+        nc.sync.dma_start(bias_sb[:], bias.rearrange("(p t) -> p t", t=PACK))
         load_page(3, 64)
         load_wg(3, 72)
 
@@ -172,9 +171,8 @@ def tile_list_electrode_refit_kernel(
 
         def scatter(t):
             if t == 0:
-                for u, (c0, w) in enumerate(first):
-                    where = idx2[:, c0 // 16 : (c0 + w) // 16]
-                    nc.vector.tensor_tensor(page[t][:].indirect(where), h_first[u][:], wg[t][:, c0 : c0 + w], ALU.mult)
+                nc.vector.tensor_tensor(page[t][:].indirect(idx2[:, 0:16]), h_head[:], wg[t][:, 0:256], ALU.mult)
+                nc.vector.tensor_tensor(page[t][:].indirect(idx2[:, 16:64]), h_rest[:], wg[t][:, 256:S], ALU.mult)
             else:
                 nc.vector.tensor_tensor(page[t][:].indirect(idx2[:]), h_sb[t][:], wg[t][:], ALU.mult)
 
@@ -205,15 +203,15 @@ def tile_list_electrode_refit_kernel(
         grouped = {0: round_weight(0)}
         features(0, read_page(0)[:], 0, NCH, 8, 0)
         grouped[2] = round_weight(2)
+        quantise_weight(0, held("w_w0", [P, N], U32), grouped[0])
         scatter(1)
-        quantise_weight(0, placed("w_w0", [P, N], U32, 1), grouped[0])
+        wb_w = held("wb_w", [P, N], I32)
+        nc.vector.tensor_copy(wb_w[:].rearrange("p (t m) -> p t m", t=PACK), wb_w_raw[:].rearrange("p (m t) -> p t m", t=PACK))
         features(1, read_page(1)[:], 0, NCH, 93, 0)
         grouped[1] = round_weight(1)
+        quantise_weight(2, held("w_w2", [P, N], U32), grouped[2])
         scatter(2)
-        quantise_weight(2, placed("w_w2", [P, N], U32, 57), grouped[2])
-        wb_w = placed("wb_w", [P, N], I32, 85)
-        wb_s = placed("wb_s", [P, N], U8, 87)
-        nc.vector.tensor_copy(wb_w[:].rearrange("p (t m) -> p t m", t=PACK), wb_w_raw[:].rearrange("p (m t) -> p t m", t=PACK))
+        wb_s = held("wb_s", [P, N], U8)
         nc.vector.tensor_copy(wb_s[:].rearrange("p (t m) -> p t m", t=PACK), wb_s_raw[:].rearrange("p (m t) -> p t m", t=PACK))
         features(2, read_page(2)[:], 0, NCH, 44, 0)
         scatter(3)

@@ -48,7 +48,7 @@ def tile_list_electrode_refit_kernel(
         idx3 = lists.tile([P, M // 16], U16, name="idx3")
 
         tab_s = placed("tab_s", [P, T], U8, 16)
-        w1_s_raw = placed("w1_s_raw", [P, 2, H], U8, 50)
+        w1_s_raw = placed("w1_s_raw", [P, 2, H], U8, 76)
         v_s = placed("v_s", [P, 2, S], U8, 56)
         nc.gpsimd.memset(w1_s_raw[:].rearrange("p a c -> p (a c)").bitcast(I32), 0)
         nc.vector.memset(tab_s[0:96, :].bitcast(I32), 0)
@@ -99,8 +99,8 @@ def tile_list_electrode_refit_kernel(
         w1_w = placed("w1_w", [P, 2, PACK, 2 * P], U8, 71)
         nc.vector.tensor_copy(w1_w[:].bitcast(U16), w1_w_raw[:].bitcast(U16).rearrange("p a (m t) -> p a t m", t=PACK))
         load_wg(0, 24, (0, 256, S))
-        w1_s = placed("w1_s", [P, 2, PACK, P], U8, 0)
-        nc.vector.tensor_copy(w1_s[:], w1_s_raw[:].rearrange("p a (m t) -> p a t m", t=PACK))
+        w1_s = held("w1_s", [P, 2, PACK, P], U8)
+        nc.gpsimd.tensor_copy(w1_s[:], w1_s_raw[:].rearrange("p a (m t) -> p a t m", t=PACK))
 
         first = ((0, 256), (256, 512), (768, 256))
         v_w = [placed("v_w0", [P, S], U32, 36), placed("v_w1", [P, S], U32, 50)]

@@ -23,6 +23,7 @@ HALF = 512
 W = 256
 NCH = M // W
 KB = 1024
+DIRECT = (0,)
 
 
 def tile_list_electrode_refit_kernel(
@@ -131,14 +132,14 @@ def tile_list_electrode_refit_kernel(
             for c0 in (0, HALF):
                 make_h(t, c0, HALF, h_sb[t][:, c0 : c0 + HALF])
 
-        load_wg(1, 1)
+        load_weight(0, 0)
         load_page(1, 101)
-        wb_w_raw = placed("wb_w_raw", [P, N], I32, 109)
+        load_wg(1, 8)
+        wb_w_raw = placed("wb_w_raw", [P, N], I32, 12)
         nc.sync.dma_start(wb_w_raw[:], wb_words[0].rearrange("p c i -> p (c i)").bitcast(I32))
-        gain_sb = placed("gain_sb", [P, 2, PACK], F32, 5)
+        gain_sb = placed("gain_sb", [P, 2, PACK], F32, 14)
         bias_sb = placed("bias_sb", [P, PACK], F32, 56)
         nc.sync.dma_start(gain_sb[:], gain.rearrange("(f p t) -> p f t", f=2, t=PACK))
-        load_weight(0, 8)
         load_weight(2, 93)
         load_page(2, 36)
         load_wg(2, 57)
@@ -182,7 +183,10 @@ def tile_list_electrode_refit_kernel(
                 nc.scalar.activation(both[:, f, :], x, func)
                 for c in range(n):
                     feat = both[:, f, W * c : W * (c + 1)]
-                    target = pairs[c0 + c][:, t // 2, f, t % 2 : 2 * W : 2]
+                    if t >= 2 and c0 + c in DIRECT:
+                        target = z_bf[c0 + c][:, PACK * W * f + t : PACK * W * (f + 1) : PACK]
+                    else:
+                        target = pairs[c0 + c][:, t // 2, f, t % 2 : 2 * W : 2]
                     if f < on_vector:
                         nc.vector.tensor_scalar(target, feat, gain_sb[:, f, t : t + 1], None, ALU.mult)
                     else:
@@ -200,16 +204,16 @@ def tile_list_electrode_refit_kernel(
             return x
 
         scatter(0)
-        grouped = {0: round_weight(0)}
-        features(0, read_page(0)[:], 0, NCH, 8, 0)
-        grouped[2] = round_weight(2)
+        grouped = {0: round_weight(0), 2: round_weight(2)}
+        features(0, read_page(0)[:], 0, NCH, 93, 0)
+        grouped[1] = round_weight(1)
         quantise_weight(0, held("w_w0", [P, N], U32), grouped[0])
         scatter(1)
         wb_w = held("wb_w", [P, N], I32)
         nc.vector.tensor_copy(wb_w[:].rearrange("p (t m) -> p t m", t=PACK), wb_w_raw[:].rearrange("p (m t) -> p t m", t=PACK))
-        features(1, read_page(1)[:], 0, NCH, 93, 0)
-        grouped[1] = round_weight(1)
-        quantise_weight(2, held("w_w2", [P, N], U32), grouped[2])
+        features(1, read_page(1)[:], 0, NCH, 44, 0)
+        for c in DIRECT:
+            nc.scalar.copy(z_bf[c][:].bitcast(U32)[:, 0 : 4 * W : 2], pairs[c][:, 0, :, :].rearrange("p f m -> p (f m)").bitcast(U32))
         scatter(2)
         wb_s = held("wb_s", [P, N], U8)
         nc.vector.tensor_copy(wb_s[:].rearrange("p (t m) -> p t m", t=PACK), wb_s_raw[:].rearrange("p (m t) -> p t m", t=PACK))
@@ -244,8 +248,11 @@ def tile_list_electrode_refit_kernel(
                     )
             return acc
 
-        def finish_y(c, cast):
+        ys = {}
+
+        def make_y(c):
             y = held("y%d" % c, [P, PACK, W], F32)
+            ys[c] = y
             pending = None
             for t0 in range(0, PACK + 2, 2):
                 slots = range(t0, t0 + 2)
@@ -263,30 +270,47 @@ def tile_list_electrode_refit_kernel(
                         cols = slice(i * W, (i + 1) * W)
                         nc.vector.scalar_tensor_tensor(y[:, t, :], d_prev[:, cols], bias_sb[:, t : t + 1], ab_prev[:, cols], ALU.add, ALU.add)
                 pending = (slots, d_ps, ab)
-            nc.sync.dma_start(y_rows[:, :, W * c : W * (c + 1)], y[:])
+            step = PACK if c < NCH - 1 else 2
+            for t0 in range(0, PACK, step):
+                nc.sync.dma_start(y_rows[:, t0 : t0 + step, W * c : W * (c + 1)], y[:, t0 : t0 + step, :])
+
+        def make_planes(c, cast):
+            y = ys[c]
             y_bf = held("y_bf%d" % c, [P, W * PACK], BF16)
-            cast(y_bf[:].rearrange("p (g i t) -> p g t i", i=4, t=PACK), y[:].rearrange("p t (g i) -> p g t i", i=4))
+            target = y_bf[:].rearrange("p (g i t) -> p g t i", i=4, t=PACK)
+            source = y[:].rearrange("p t (g i) -> p g t i", i=4)
+            if c < NCH - 1:
+                cast(target, source)
+            else:
+                nc.scalar.copy(target[:, :, 0:2, :], source[:, :, 0:2, :])
+                nc.vector.tensor_copy(target[:, :, 2:4, :], source[:, :, 2:4, :])
             y_w = held("y_w%d" % c, [P, W], I32)
             nc.vector.quantize_mx(y_w[:].bitcast(FP8X4), y_s[:, W * c : W * (c + 1)], y_bf[:])
             nc.sync.dma_start(code_rows[:, PACK * W * c : PACK * W * (c + 1)].bitcast(I32), y_w[:])
 
-        quantise_weight(1, placed("w_w1", [P, N], U32, 89), grouped[1])
         for c in range(NCH):
             read_last(c)
-        for c in range(2):
-            features(last, x_last[c][:], c, 1, 8 + 2 * c, 0)
-            weave(c, nc.vector.tensor_copy, I32)
-            quantise_z(c)
-        features(last, x_last[2][:], 2, 1, 12, 0)
-        finish_y(0, nc.scalar.copy)
+        quantise_weight(1, placed("w_w1", [P, N], U32, 89), grouped[1])
+        features(last, x_last[0][:], 0, 1, 0, 0)
+        quantise_z(0)
+        features(last, x_last[1][:], 1, 1, 2, 0)
+        weave(1, nc.vector.tensor_copy, I32)
+        quantise_z(1)
+        quantise_weight(2, placed("w_w2", [P, N], U32, 0), grouped[2])
+        features(last, x_last[2][:], 2, 1, 4, 0)
+        make_y(0)
         weave(2, nc.scalar.copy, U32)
         quantise_z(2)
-        features(last, x_last[3][:], 3, 1, 14, 0)
-        finish_y(1, nc.scalar.copy)
+        features(last, x_last[3][:], 3, 1, 6, 0)
+        make_y(1)
         weave(3, nc.scalar.copy, U32)
         quantise_z(3)
-        finish_y(2, nc.scalar.copy)
-        finish_y(3, nc.vector.tensor_copy)
+        make_planes(0, nc.scalar.copy)
+        make_y(2)
+        make_planes(1, nc.scalar.copy)
+        make_y(3)
+        make_planes(2, nc.scalar.copy)
+        make_planes(3, nc.vector.tensor_copy)
         for q in range(4):
             eng = nc.sync if q % 2 == 0 else nc.scalar
             eng.dma_start(out_2[0, 4 * q : 4 * q + 4, :].bitcast(I32), y_s[QUAD * q : QUAD * q + 4, :].bitcast(I32))

@@ -101,7 +101,9 @@ def tile_list_electrode_refit_kernel(
         nc.vector.tensor_copy(w1_w[:].bitcast(U16), w1_w_raw[:].bitcast(U16).rearrange("p a (m t) -> p a t m", t=PACK))
         load_wg(0, 24, (0, 256, S))
         w1_s = held("w1_s", [P, 2, PACK, P], U8)
-        nc.gpsimd.tensor_copy(w1_s[:], w1_s_raw[:].rearrange("p a (m t) -> p a t m", t=PACK))
+        w1_s_dealt = w1_s_raw[:].rearrange("p a (m t) -> p a t m", t=PACK)
+        nc.gpsimd.tensor_copy(w1_s[:, :, 0, :], w1_s_dealt[:, :, 0, :])
+        nc.gpsimd.tensor_copy(w1_s[:, :, 1:PACK, :], w1_s_dealt[:, :, 1:PACK, :])
 
         first = ((0, 256), (256, 512), (768, 256))
         v_w = [placed("v_w0", [P, S], U32, 36), placed("v_w1", [P, S], U32, 50)]

@@ -225,13 +225,12 @@ def tile_list_electrode_refit_kernel(
         last = PACK - 1
         z_w = [held("z_w%d" % c, [P, 2, W], U32) for c in range(NCH)]
         z_s = [held("z_s%d" % c, [P, 2, W], U8) for c in range(NCH)]
-        x_last = [held("x_last%d" % c, [P, W], F32) for c in range(NCH)]
+        x_head = held("x_head", [P, W], F32)
+        x_rest = held("x_rest", [P, M - W], F32)
+        x_last = [x_head[:]] + [x_rest[:, W * c : W * (c + 1)] for c in range(NCH - 1)]
         y_s = held("y_s", [P, M], U8)
         y_rows = out_0.rearrange("(p t) m -> p t m", t=PACK)
         code_rows = out_1[0].rearrange("p m t -> p (m t)")
-
-        def read_last(c):
-            nc.vector.tensor_copy(x_last[c][:], page[last][:].indirect(idx3[:, W * c // 16 : W * (c + 1) // 16]))
 
         def quantise_z(c):
             nc.vector.quantize_mx(
@@ -255,23 +254,20 @@ def tile_list_electrode_refit_kernel(
         def make_y(c):
             y = held("y%d" % c, [P, PACK, W], F32)
             ys[c] = y
-            pending = None
-            for t0 in range(0, PACK + 2, 2):
-                slots = range(t0, t0 + 2)
-                if t0 < PACK:
-                    a_ps = product(c, slots, [(w_w[0], w_s[0], 0)])
-                    b_ps = product(c, slots, [(wb_w, wb_s, 1)])
-                    d_ps = product(c, slots, [(w_w[1], w_s[1], 0), (w_w[2], w_s[2], 1)])
-                    a_sb = deep.tile([P, HALF], F32, name="a_sb", tag="a_sb")
-                    nc.scalar.copy(a_sb[:], a_ps[:])
-                    ab = deep.tile([P, HALF], F32, name="ab", tag="ab")
-                    nc.vector.tensor_tensor(ab[:], b_ps[:], a_sb[:], ALU.mult)
-                if pending is not None:
-                    done, d_prev, ab_prev = pending
-                    for i, t in enumerate(done):
-                        cols = slice(i * W, (i + 1) * W)
-                        nc.vector.scalar_tensor_tensor(y[:, t, :], d_prev[:, cols], bias_sb[:, t : t + 1], ab_prev[:, cols], ALU.add, ALU.add)
-                pending = (slots, d_ps, ab)
+            pairs_of_slots = (range(0, 2), range(2, 4))
+            ab = []
+            for slots in pairs_of_slots:
+                a_ps = product(c, slots, [(w_w[0], w_s[0], 0)])
+                b_ps = product(c, slots, [(wb_w, wb_s, 1)])
+                a_sb = deep.tile([P, HALF], F32, name="a_sb", tag="a_sb")
+                nc.scalar.copy(a_sb[:], a_ps[:])
+                ab.append(deep.tile([P, HALF], F32, name="ab", tag="ab"))
+                nc.vector.tensor_tensor(ab[-1][:], b_ps[:], a_sb[:], ALU.mult)
+            for slots, prod in zip(pairs_of_slots, ab):
+                d_ps = product(c, slots, [(w_w[1], w_s[1], 0), (w_w[2], w_s[2], 1)])
+                for i, t in enumerate(slots):
+                    cols = slice(i * W, (i + 1) * W)
+                    nc.vector.scalar_tensor_tensor(y[:, t, :], d_ps[:, cols], bias_sb[:, t : t + 1], prod[:, cols], ALU.add, ALU.add)
             step = PACK if c < NCH - 1 else 2
             for t0 in range(0, PACK, step):
                 nc.sync.dma_start(y_rows[:, t0 : t0 + step, W * c : W * (c + 1)], y[:, t0 : t0 + step, :])
@@ -290,20 +286,20 @@ def tile_list_electrode_refit_kernel(
             nc.vector.quantize_mx(y_w[:].bitcast(FP8X4), y_s[:, W * c : W * (c + 1)], y_bf[:])
             nc.sync.dma_start(code_rows[:, PACK * W * c : PACK * W * (c + 1)].bitcast(I32), y_w[:])
 
-        for c in range(NCH):
-            read_last(c)
+        nc.vector.tensor_copy(x_head[:], page[last][:].indirect(idx3[:, 0 : W // 16]))
+        nc.vector.tensor_copy(x_rest[:], page[last][:].indirect(idx3[:, W // 16 : M // 16]))
         quantise_weight(1, placed("w_w1", [P, N], U32, 89), grouped[1])
-        features(last, x_last[0][:], 0, 1, 0, 0)
+        features(last, x_last[0], 0, 1, 0, 0)
         quantise_z(0)
-        features(last, x_last[1][:], 1, 1, 2, 0)
+        features(last, x_last[1], 1, 1, 2, 0)
         weave(1, nc.vector.tensor_copy, I32)
         quantise_z(1)
         quantise_weight(2, placed("w_w2", [P, N], U32, 0), grouped[2])
-        features(last, x_last[2][:], 2, 1, 4, 0)
+        features(last, x_last[2], 2, 1, 4, 0)
         make_y(0)
         weave(2, nc.scalar.copy, U32)
         quantise_z(2)
-        features(last, x_last[3][:], 3, 1, 6, 0)
+        features(last, x_last[3], 3, 1, 6, 0)
         make_y(1)
         weave(3, nc.scalar.copy, U32)
         quantise_z(3)

@@ -297,7 +297,7 @@ def tile_list_electrode_refit_kernel(
         quantise_weight(2, placed("w_w2", [P, N], U32, 0), grouped[2])
         features(last, x_last[2], 2, 1, 4, 0)
         make_y(0)
-        weave(2, nc.scalar.copy, U32)
+        weave(2, nc.vector.tensor_copy, I32)
         quantise_z(2)
         features(last, x_last[3], 3, 1, 6, 0)
         make_y(1)

@@ -19,11 +19,14 @@ ACT = mybir.ActivationFunctionType
 P = 128
 PACK = 4
 QUAD = 32
-HALF = 512
-W = 256
-NCH = M // W
+BANK = 512
+PER_COL = 16
 KB = 1024
-DIRECT = (0,)
+HEAD = 256
+PIECES = ((0, HEAD), (HEAD, BANK), (HEAD + BANK, S - HEAD - BANK))
+W = BANK // 2
+NCH = M // W
+LAST = PACK - 1
 
 
 def tile_list_electrode_refit_kernel(
@@ -44,15 +47,15 @@ def tile_list_electrode_refit_kernel(
         def placed(name, shape, dtype, kb):
             return arena.tile(shape, dtype, name=name, align_bytes=64, offset=int(kb * KB))
 
-        idx = lists.tile([P, S // 16], U16, name="idx")
-        idx2 = lists.tile([P, S // 16], U16, name="idx2")
-        idx3 = lists.tile([P, M // 16], U16, name="idx3")
+        idx = lists.tile([P, S // PER_COL], U16, name="idx")
+        idx2 = lists.tile([P, S // PER_COL], U16, name="idx2")
+        idx3 = lists.tile([P, M // PER_COL], U16, name="idx3")
 
         tab_s = placed("tab_s", [P, T], U8, 16)
         w1_s_raw = placed("w1_s_raw", [P, 2, H], U8, 76)
         v_s = placed("v_s", [P, 2, S], U8, 56)
         nc.gpsimd.memset(w1_s_raw[:].rearrange("p a c -> p (a c)").bitcast(I32), 0)
-        nc.vector.memset(tab_s[0:96, :].bitcast(I32), 0)
+        nc.vector.memset(tab_s[0 : P - QUAD, :].bitcast(I32), 0)
         nc.vector.memset(v_s[:].rearrange("p a c -> p (a c)").bitcast(I32), 0)
         for q in range(4):
             eng = nc.gpsimd if q % 2 == 0 else nc.scalar
@@ -62,7 +65,7 @@ def tile_list_electrode_refit_kernel(
             )
 
         nc.sync.dma_start(idx[:], offs)
-        nc.sync.dma_start(tab_s[96:128, :].bitcast(I32), tab_scales.rearrange("a q n -> q a n").bitcast(I32))
+        nc.sync.dma_start(tab_s[P - QUAD : P, :].bitcast(I32), tab_scales.rearrange("a q n -> q a n").bitcast(I32))
         nc.sync.dma_start(idx2[:], offs2)
         nc.sync.dma_start(idx3[:], offs3)
         w1_w_raw = placed("w1_w_raw", [P, 2, 2 * H], U8, 24)
@@ -73,6 +76,7 @@ def tile_list_electrode_refit_kernel(
 
         page_rows = page0.rearrange("(p t) n -> t p n", t=PACK)
         wgs_rows = wgs.rearrange("(i t) j -> t i j", t=PACK)
+        w_src = (wa, wd[0:H, :], wd[H:F, :])
         page, wg, w_raw = {}, {}, {}
 
         def load_page(t, kb):
@@ -85,8 +89,6 @@ def tile_list_electrode_refit_kernel(
                 for q in (0, 2, 1, 3):
                     nc.sync.dma_start(wg[t][QUAD * q : QUAD * (q + 1), c0:c1], wgs_rows[t][:, c0:c1])
 
-        w_src = (wa, wd[0:H, :], wd[H:F, :])
-
         def load_weight(i, kb):
             w_raw[i] = placed("w_raw%d" % i, [P, PACK, N], F32, kb)
             nc.sync.dma_start(w_raw[i][:], w_src[i].rearrange("(p j) n -> p j n", j=PACK))
@@ -94,30 +96,31 @@ def tile_list_electrode_refit_kernel(
         picked_s = placed("picked_s", [P, S], U8, 108.5)
         nc.vector.tensor_copy(picked_s[:], tab_s[:].indirect(idx[:]))
         for q in range(4):
-            nc.sync.dma_start(v_s[QUAD * q : QUAD * q + 4, :, :].bitcast(I32), picked_s[96 + 8 * q : 104 + 8 * q, :].bitcast(I32))
+            row = P - QUAD + 8 * q
+            nc.sync.dma_start(v_s[QUAD * q : QUAD * q + 4, :, :].bitcast(I32), picked_s[row : row + 8, :].bitcast(I32))
         load_page(0, 16)
 
         w1_w = placed("w1_w", [P, 2, PACK, 2 * P], U8, 71)
         nc.vector.tensor_copy(w1_w[:].bitcast(U16), w1_w_raw[:].bitcast(U16).rearrange("p a (m t) -> p a t m", t=PACK))
-        load_wg(0, 24, (0, 256, S))
+        load_wg(0, 24, (0, HEAD, S))
         w1_s = held("w1_s", [P, 2, PACK, P], U8)
-        w1_s_dealt = w1_s_raw[:].rearrange("p a (m t) -> p a t m", t=PACK)
-        nc.gpsimd.tensor_copy(w1_s[:, :, 0, :], w1_s_dealt[:, :, 0, :])
-        nc.gpsimd.tensor_copy(w1_s[:, :, 1:PACK, :], w1_s_dealt[:, :, 1:PACK, :])
+        w1_s_by_slot = w1_s_raw[:].rearrange("p a (m t) -> p a t m", t=PACK)
+        nc.gpsimd.tensor_copy(w1_s[:, :, 0, :], w1_s_by_slot[:, :, 0, :])
+        nc.gpsimd.tensor_copy(w1_s[:, :, 1:PACK, :], w1_s_by_slot[:, :, 1:PACK, :])
 
-        first = ((0, 256), (256, 512), (768, 256))
         v_w = [placed("v_w0", [P, S], U32, 36), placed("v_w1", [P, S], U32, 50)]
         nc.vector.tensor_copy(v_w[0][:], tab_w[0][:].bitcast(U32).indirect(idx[:]))
-        for c0, w in first:
-            nc.vector.tensor_copy(v_w[1][:, c0 : c0 + w], tab_w[1][:].bitcast(U32).indirect(idx[:, c0 // 16 : (c0 + w) // 16]))
+        for c0, w in PIECES:
+            where = idx[:, c0 // PER_COL : (c0 + w) // PER_COL]
+            nc.vector.tensor_copy(v_w[1][:, c0 : c0 + w], tab_w[1][:].bitcast(U32).indirect(where))
 
-        h_head = placed("h_head", [P, 256], F32, 93)
-        h_rest = placed("h_rest", [P, S - 256], F32, 78)
+        h_head = placed("h_head", [P, HEAD], F32, 93)
+        h_rest = placed("h_rest", [P, S - HEAD], F32, 78)
         h_sb = {t: placed("h%d" % t, [P, S], F32, 77 + 4 * t) for t in range(1, PACK)}
 
         def make_h(t, c0, w, target):
             acc = psum.tile([P, w], F32, name="acc", tag="bank")
-            n = HALF if w == HALF else P
+            n = BANK if w == BANK else P
             for a in range(2):
                 for b in range(0, w, n):
                     cols = slice(c0 + b, c0 + b + n)
@@ -128,11 +131,11 @@ def tile_list_electrode_refit_kernel(
                     )
             nc.scalar.copy(target, acc[:])
 
-        for u, (c0, w) in enumerate(first):
-            make_h(0, c0, w, h_head[:] if u == 0 else h_rest[:, c0 - 256 : c0 - 256 + w])
+        for c0, w in PIECES:
+            make_h(0, c0, w, h_head[:] if c0 == 0 else h_rest[:, c0 - HEAD : c0 - HEAD + w])
         for t in range(1, PACK):
-            for c0 in (0, HALF):
-                make_h(t, c0, HALF, h_sb[t][:, c0 : c0 + HALF])
+            for c0 in (0, BANK):
+                make_h(t, c0, BANK, h_sb[t][:, c0 : c0 + BANK])
 
         load_weight(0, 0)
         load_page(1, 101)
@@ -174,55 +177,57 @@ def tile_list_electrode_refit_kernel(
 
         def scatter(t):
             if t == 0:
-                nc.vector.tensor_tensor(page[t][:].indirect(idx2[:, 0:16]), h_head[:], wg[t][:, 0:256], ALU.mult)
-                nc.vector.tensor_tensor(page[t][:].indirect(idx2[:, 16:64]), h_rest[:], wg[t][:, 256:S], ALU.mult)
+                cut = HEAD // PER_COL
+                nc.vector.tensor_tensor(page[t][:].indirect(idx2[:, 0:cut]), h_head[:], wg[t][:, 0:HEAD], ALU.mult)
+                nc.vector.tensor_tensor(page[t][:].indirect(idx2[:, cut : S // PER_COL]), h_rest[:], wg[t][:, HEAD:S], ALU.mult)
             else:
                 nc.vector.tensor_tensor(page[t][:].indirect(idx2[:]), h_sb[t][:], wg[t][:], ALU.mult)
-
-        def features(t, x, c0, n, kb, on_vector):
-            both = placed("feat%d_%d" % (t, c0), [P, 2, n * W], F32, kb)
-            for f, func in enumerate((ACT.Sin, ACT.Square)):
-                nc.scalar.activation(both[:, f, :], x, func)
-                for c in range(n):
-                    feat = both[:, f, W * c : W * (c + 1)]
-                    if t >= 2 and c0 + c in DIRECT:
-                        target = z_bf[c0 + c][:, PACK * W * f + t : PACK * W * (f + 1) : PACK]
-                    else:
-                        target = pairs[c0 + c][:, t // 2, f, t % 2 : 2 * W : 2]
-                    if f < on_vector:
-                        nc.vector.tensor_scalar(target, feat, gain_sb[:, f, t : t + 1], None, ALU.mult)
-                    else:
-                        nc.scalar.activation(target, feat, ACT.Copy, scale=gain_sb[:, f, t : t + 1])
-
-        def weave(c, copy, dtype):
-            copy(
-                z_bf[c][:].bitcast(dtype).rearrange("p (m u) -> p m u", u=2),
-                pairs[c][:].rearrange("p u f m -> p u (f m)").bitcast(dtype).rearrange("p u m -> p m u"),
-            )
 
         def read_page(t):
             x = held("x%d" % t, [P, M], F32)
             nc.vector.tensor_copy(x[:], page[t][:].indirect(idx3[:]))
             return x
 
+        def features(t, x, chunks, kb, sine_gain_on_vector=False):
+            both = placed("feat%d_%d" % (t, chunks[0]), [P, 2, len(chunks) * W], F32, kb)
+            for f, func in enumerate((ACT.Sin, ACT.Square)):
+                nc.scalar.activation(both[:, f, :], x, func)
+                for i, c in enumerate(chunks):
+                    feat = both[:, f, W * i : W * (i + 1)]
+                    if c == 0 and t >= 2:
+                        target = z_bf[c][:, PACK * W * f + t : PACK * W * (f + 1) : PACK]
+                    else:
+                        target = pairs[c][:, t // 2, f, t % 2 : 2 * W : 2]
+                    if f == 0 and sine_gain_on_vector:
+                        nc.vector.tensor_scalar(target, feat, gain_sb[:, f, t : t + 1], None, ALU.mult)
+                    else:
+                        nc.scalar.activation(target, feat, ACT.Copy, scale=gain_sb[:, f, t : t + 1])
+
+        on_vector = (nc.vector.tensor_copy, I32)
+        on_scalar = (nc.scalar.copy, U32)
+
+        def weave(c, f0, f1, mover):
+            copy, dtype = mover
+            copy(
+                z_bf[c][:, PACK * W * f0 : PACK * W * f1].bitcast(dtype).rearrange("p (m u) -> p m u", u=2),
+                pairs[c][:, :, f0:f1, :].rearrange("p u f m -> p u (f m)").bitcast(dtype).rearrange("p u m -> p m u"),
+            )
+
         scatter(0)
         grouped = {0: round_weight(0), 2: round_weight(2)}
-        features(0, read_page(0)[:], 0, NCH, 93, 0)
+        features(0, read_page(0)[:], range(NCH), 93)
         grouped[1] = round_weight(1)
-        quantise_weight(0, held("w_w0", [P, N], U32), grouped[0])
         scatter(1)
         wb_w = held("wb_w", [P, N], I32)
         nc.vector.tensor_copy(wb_w[:].rearrange("p (t m) -> p t m", t=PACK), wb_w_raw[:].rearrange("p (m t) -> p t m", t=PACK))
-        features(1, read_page(1)[:], 0, NCH, 44, 0)
-        for c in DIRECT:
-            nc.scalar.copy(z_bf[c][:].bitcast(U32)[:, 0 : 4 * W : 2], pairs[c][:, 0, :, :].rearrange("p f m -> p (f m)").bitcast(U32))
+        features(1, read_page(1)[:], range(NCH), 44)
+        nc.scalar.copy(z_bf[0][:].bitcast(U32)[:, 0 : 4 * W : 2], pairs[0][:, 0, :, :].rearrange("p f m -> p (f m)").bitcast(U32))
         scatter(2)
         wb_s = held("wb_s", [P, N], U8)
         nc.vector.tensor_copy(wb_s[:].rearrange("p (t m) -> p t m", t=PACK), wb_s_raw[:].rearrange("p (m t) -> p t m", t=PACK))
-        features(2, read_page(2)[:], 0, NCH, 44, 0)
-        scatter(3)
+        features(2, read_page(2)[:], range(NCH), 44)
+        scatter(LAST)
 
-        last = PACK - 1
         z_w = [held("z_w%d" % c, [P, 2, W], U32) for c in range(NCH)]
         z_s = [held("z_s%d" % c, [P, 2, W], U8) for c in range(NCH)]
         x_head = held("x_head", [P, W], F32)
@@ -231,11 +236,14 @@ def tile_list_electrode_refit_kernel(
         y_s = held("y_s", [P, M], U8)
         y_rows = out_0.rearrange("(p t) m -> p t m", t=PACK)
         code_rows = out_1[0].rearrange("p m t -> p (m t)")
+        y = {}
+
+        def last_features(c, sine_gain_on_vector=False):
+            features(LAST, x_last[c], [c], 2 * c, sine_gain_on_vector)
 
         def quantise_z(c):
             nc.vector.quantize_mx(
-                z_w[c][:].rearrange("p f m -> p (f m)").bitcast(FP8X4), z_s[c][:].rearrange("p f m -> p (f m)"),
-                z_bf[c][:],
+                z_w[c][:].rearrange("p f m -> p (f m)").bitcast(FP8X4), z_s[c][:].rearrange("p f m -> p (f m)"), z_bf[c][:]
             )
 
         def product(c, slots, terms):
@@ -249,36 +257,32 @@ def tile_list_electrode_refit_kernel(
                     )
             return acc
 
-        ys = {}
-
         def make_y(c):
-            y = held("y%d" % c, [P, PACK, W], F32)
-            ys[c] = y
-            pairs_of_slots = (range(0, 2), range(2, 4))
+            y[c] = held("y%d" % c, [P, PACK, W], F32)
+            slot_pairs = (range(0, 2), range(2, 4))
             ab = []
-            for slots in pairs_of_slots:
+            for slots in slot_pairs:
                 a_ps = product(c, slots, [(w_w[0], w_s[0], 0)])
                 b_ps = product(c, slots, [(wb_w, wb_s, 1)])
-                a_sb = deep.tile([P, HALF], F32, name="a_sb", tag="a_sb")
+                a_sb = deep.tile([P, BANK], F32, name="a_sb", tag="a_sb")
                 nc.scalar.copy(a_sb[:], a_ps[:])
-                ab.append(deep.tile([P, HALF], F32, name="ab", tag="ab"))
+                ab.append(deep.tile([P, BANK], F32, name="ab", tag="ab"))
                 nc.vector.tensor_tensor(ab[-1][:], b_ps[:], a_sb[:], ALU.mult)
-            for slots, prod in zip(pairs_of_slots, ab):
+            for slots, prod in zip(slot_pairs, ab):
                 d_ps = product(c, slots, [(w_w[1], w_s[1], 0), (w_w[2], w_s[2], 1)])
                 for i, t in enumerate(slots):
                     cols = slice(i * W, (i + 1) * W)
-                    nc.vector.scalar_tensor_tensor(y[:, t, :], d_ps[:, cols], bias_sb[:, t : t + 1], prod[:, cols], ALU.add, ALU.add)
+                    nc.vector.scalar_tensor_tensor(y[c][:, t, :], d_ps[:, cols], bias_sb[:, t : t + 1], prod[:, cols], ALU.add, ALU.add)
             step = PACK if c < NCH - 1 else 2
             for t0 in range(0, PACK, step):
-                nc.sync.dma_start(y_rows[:, t0 : t0 + step, W * c : W * (c + 1)], y[:, t0 : t0 + step, :])
+                nc.sync.dma_start(y_rows[:, t0 : t0 + step, W * c : W * (c + 1)], y[c][:, t0 : t0 + step, :])
 
-        def make_planes(c, cast):
-            y = ys[c]
+        def make_planes(c):
             y_bf = held("y_bf%d" % c, [P, W * PACK], BF16)
             target = y_bf[:].rearrange("p (g i t) -> p g t i", i=4, t=PACK)
-            source = y[:].rearrange("p t (g i) -> p g t i", i=4)
+            source = y[c][:].rearrange("p t (g i) -> p g t i", i=4)
             if c < NCH - 1:
-                cast(target, source)
+                nc.scalar.copy(target, source)
             else:
                 nc.scalar.copy(target[:, :, 0:2, :], source[:, :, 0:2, :])
                 nc.vector.tensor_copy(target[:, :, 2:4, :], source[:, :, 2:4, :])
@@ -286,29 +290,29 @@ def tile_list_electrode_refit_kernel(
             nc.vector.quantize_mx(y_w[:].bitcast(FP8X4), y_s[:, W * c : W * (c + 1)], y_bf[:])
             nc.sync.dma_start(code_rows[:, PACK * W * c : PACK * W * (c + 1)].bitcast(I32), y_w[:])
 
-        nc.vector.tensor_copy(x_head[:], page[last][:].indirect(idx3[:, 0 : W // 16]))
-        nc.vector.tensor_copy(x_rest[:], page[last][:].indirect(idx3[:, W // 16 : M // 16]))
+        nc.vector.tensor_copy(x_head[:], page[LAST][:].indirect(idx3[:, 0 : W // PER_COL]))
+        nc.vector.tensor_copy(x_rest[:], page[LAST][:].indirect(idx3[:, W // PER_COL : M // PER_COL]))
+        quantise_weight(0, placed("w_w0", [P, N], U32, 91), grouped[0])
         quantise_weight(1, placed("w_w1", [P, N], U32, 89), grouped[1])
-        features(last, x_last[0], 0, 1, 0, 0)
+        last_features(0)
         quantise_z(0)
-        features(last, x_last[1], 1, 1, 2, 0)
-        weave(1, nc.vector.tensor_copy, I32)
+        last_features(1, sine_gain_on_vector=True)
+        weave(1, 0, 2, on_vector)
         quantise_z(1)
         quantise_weight(2, placed("w_w2", [P, N], U32, 0), grouped[2])
-        features(last, x_last[2], 2, 1, 4, 0)
+        last_features(2)
         make_y(0)
-        weave(2, nc.vector.tensor_copy, I32)
+        weave(2, 0, 1, on_vector)
+        weave(2, 1, 2, on_scalar)
         quantise_z(2)
-        features(last, x_last[3], 3, 1, 6, 0)
+        last_features(3)
         make_y(1)
-        weave(3, nc.scalar.copy, U32)
+        weave(3, 0, 2, on_scalar)
         quantise_z(3)
-        make_planes(0, nc.scalar.copy)
-        make_y(2)
-        make_planes(1, nc.scalar.copy)
-        make_y(3)
-        make_planes(2, nc.scalar.copy)
-        make_planes(3, nc.vector.tensor_copy)
+        for c in range(NCH):
+            make_planes(c)
+            if c + 2 < NCH:
+                make_y(c + 2)
         for q in range(4):
             eng = nc.sync if q % 2 == 0 else nc.scalar
             eng.dma_start(out_2[0, 4 * q : 4 * q + 4, :].bitcast(I32), y_s[QUAD * q : QUAD * q + 4, :].bitcast(I32))

@@ -24,9 +24,11 @@ PER_COL = 16
 KB = 1024
 HEAD = 256
 PIECES = ((0, HEAD), (HEAD, BANK), (HEAD + BANK, S - HEAD - BANK))
-W = BANK // 2
-NCH = M // W
+WIDTHS = (128, 256, 256, 256, 128)
+STARTS = tuple(sum(WIDTHS[:c]) for c in range(len(WIDTHS)))
+NCH = len(WIDTHS)
 LAST = PACK - 1
+SIN, SQUARE = 0, 1
 
 
 def tile_list_electrode_refit_kernel(
@@ -51,9 +53,9 @@ def tile_list_electrode_refit_kernel(
         idx2 = lists.tile([P, S // PER_COL], U16, name="idx2")
         idx3 = lists.tile([P, M // PER_COL], U16, name="idx3")
 
-        tab_s = placed("tab_s", [P, T], U8, 16)
-        w1_s_raw = placed("w1_s_raw", [P, 2, H], U8, 76)
-        v_s = placed("v_s", [P, 2, S], U8, 56)
+        tab_s = placed("tab_s", [P, T], U8, 83)
+        w1_s_raw = placed("w1_s_raw", [P, 2, H], U8, 95)
+        v_s = placed("v_s", [P, 2, S], U8, 36)
         nc.gpsimd.memset(w1_s_raw[:].rearrange("p a c -> p (a c)").bitcast(I32), 0)
         nc.vector.memset(tab_s[0 : P - QUAD, :].bitcast(I32), 0)
         nc.vector.memset(v_s[:].rearrange("p a c -> p (a c)").bitcast(I32), 0)
@@ -68,9 +70,9 @@ def tile_list_electrode_refit_kernel(
         nc.sync.dma_start(tab_s[P - QUAD : P, :].bitcast(I32), tab_scales.rearrange("a q n -> q a n").bitcast(I32))
         nc.sync.dma_start(idx2[:], offs2)
         nc.sync.dma_start(idx3[:], offs3)
-        w1_w_raw = placed("w1_w_raw", [P, 2, 2 * H], U8, 24)
+        w1_w_raw = placed("w1_w_raw", [P, 2, 2 * H], U8, 91)
         nc.sync.dma_start(w1_w_raw[:].bitcast(I32), w1_words.rearrange("a p c -> p a c").bitcast(I32))
-        tab_w = [placed("tab_w%d" % a, [P, T], I32, 8 * a) for a in range(2)]
+        tab_w = [placed("tab_w%d" % a, [P, T], I32, 12 + 104 * a) for a in range(2)]
         for a in range(2):
             nc.sync.dma_start(tab_w[a][:], tab_words[a].rearrange("p t i -> p (t i)").bitcast(I32))
 
@@ -93,30 +95,30 @@ def tile_list_electrode_refit_kernel(
             w_raw[i] = placed("w_raw%d" % i, [P, PACK, N], F32, kb)
             nc.sync.dma_start(w_raw[i][:], w_src[i].rearrange("(p j) n -> p j n", j=PACK))
 
-        picked_s = placed("picked_s", [P, S], U8, 108.5)
+        picked_s = placed("picked_s", [P, S], U8, 96)
         nc.vector.tensor_copy(picked_s[:], tab_s[:].indirect(idx[:]))
         for q in range(4):
             row = P - QUAD + 8 * q
             nc.sync.dma_start(v_s[QUAD * q : QUAD * q + 4, :, :].bitcast(I32), picked_s[row : row + 8, :].bitcast(I32))
-        load_page(0, 16)
+        load_page(0, 83)
 
-        w1_w = placed("w1_w", [P, 2, PACK, 2 * P], U8, 71)
+        w1_w = placed("w1_w", [P, 2, PACK, 2 * P], U8, 45)
         nc.vector.tensor_copy(w1_w[:].bitcast(U16), w1_w_raw[:].bitcast(U16).rearrange("p a (m t) -> p a t m", t=PACK))
-        load_wg(0, 24, (0, HEAD, S))
-        w1_s = held("w1_s", [P, 2, PACK, P], U8)
+        load_wg(0, 91, (0, HEAD, S))
+        w1_s = placed("w1_s", [P, 2, PACK, P], U8, 53)
         w1_s_by_slot = w1_s_raw[:].rearrange("p a (m t) -> p a t m", t=PACK)
         nc.gpsimd.tensor_copy(w1_s[:, :, 0, :], w1_s_by_slot[:, :, 0, :])
         nc.gpsimd.tensor_copy(w1_s[:, :, 1:PACK, :], w1_s_by_slot[:, :, 1:PACK, :])
 
-        v_w = [placed("v_w0", [P, S], U32, 36), placed("v_w1", [P, S], U32, 50)]
+        v_w = [placed("v_w0", [P, S], U32, 24), placed("v_w1", [P, S], U32, 32)]
         nc.vector.tensor_copy(v_w[0][:], tab_w[0][:].bitcast(U32).indirect(idx[:]))
         for c0, w in PIECES:
             where = idx[:, c0 // PER_COL : (c0 + w) // PER_COL]
             nc.vector.tensor_copy(v_w[1][:, c0 : c0 + w], tab_w[1][:].bitcast(U32).indirect(where))
 
-        h_head = placed("h_head", [P, HEAD], F32, 93)
-        h_rest = placed("h_rest", [P, S - HEAD], F32, 78)
-        h_sb = {t: placed("h%d" % t, [P, S], F32, 77 + 4 * t) for t in range(1, PACK)}
+        h_head = placed("h_head", [P, HEAD], F32, 79)
+        h_rest = placed("h_rest", [P, S - HEAD], F32, 80)
+        h_sb = {t: placed("h%d" % t, [P, S], F32, kb) for t, kb in ((1, 4), (2, 71), (3, 0))}
 
         def make_h(t, c0, w, target):
             acc = psum.tile([P, w], F32, name="acc", tag="bank")
@@ -137,182 +139,162 @@ def tile_list_electrode_refit_kernel(
             for c0 in (0, BANK):
                 make_h(t, c0, BANK, h_sb[t][:, c0 : c0 + BANK])
 
-        load_weight(0, 0)
-        load_page(1, 101)
-        load_wg(1, 8)
-        wb_w_raw = placed("wb_w_raw", [P, N], I32, 12)
-        nc.sync.dma_start(wb_w_raw[:], wb_words[0].rearrange("p c i -> p (c i)").bitcast(I32))
-        gain_sb = placed("gain_sb", [P, 2, PACK], F32, 14)
-        bias_sb = placed("bias_sb", [P, PACK], F32, 56)
+        load_wg(1, 16)
+        load_weight(0, 8)
+        load_page(1, 112)
+        gain_sb = placed("gain_sb", [P, 2, PACK], F32, 36.5)
+        bias_sb = placed("bias_sb", [P, PACK], F32, 36.75)
         nc.sync.dma_start(gain_sb[:], gain.rearrange("(f p t) -> p f t", f=2, t=PACK))
-        load_weight(2, 93)
-        load_page(2, 36)
-        load_wg(2, 57)
-        wb_s_raw = placed("wb_s_raw", [P, N], U8, 56.25)
+        load_weight(1, 24)
+        load_wg(2, 120)
+        load_wg(3, 32)
+        load_page(2, 37)
+        load_weight(2, 45)
+        wb_w_raw = placed("wb_w_raw", [P, N], I32, 53)
+        nc.sync.dma_start(wb_w_raw[:], wb_words[0].rearrange("p c i -> p (c i)").bitcast(I32))
+        wb_s_raw = placed("wb_s_raw", [P, N], U8, 36)
         nc.gpsimd.memset(wb_s_raw[:].bitcast(I32), 0)
         for q in range(4):
             nc.sync.dma_start(wb_s_raw[QUAD * q : QUAD * q + 4, :].bitcast(I32), wb_scales[0, 4 * q : 4 * q + 4, :].bitcast(I32))
-        load_weight(1, 44)
         nc.sync.dma_start(bias_sb[:], bias.rearrange("(p t) -> p t", t=PACK))
-        load_page(3, 64)
-        load_wg(3, 72)
 
-        w_s = [held("w_s%d" % i, [P, N], U8) for i in range(3)]
-        w_w = {}
+        w_s = [held("w_s0", [P, N], U8), held("w_s1", [P, N], U8), placed("w_s2", [P, N], U8, 52.5)]
+        w_w, grouped = {}, {}
 
-        def round_weight(i):
-            grouped = held("grouped%d" % i, [P, N * PACK], BF16)
+        def round_weight(i, tile):
+            grouped[i] = tile
             nc.scalar.copy(
-                grouped[:].rearrange("p (t m j) -> p m j t", t=PACK, j=PACK),
+                tile[:].rearrange("p (t m j) -> p m j t", t=PACK, j=PACK),
                 w_raw[i][:].rearrange("p j (m t) -> p m j t", t=PACK),
             )
-            return grouped
 
-        def quantise_weight(i, words, grouped):
-            w_w[i] = words
-            nc.vector.quantize_mx(words[:].bitcast(FP8X4), w_s[i][:], grouped[:])
+        def quantise_weight(i, kb):
+            w_w[i] = placed("w_w%d" % i, [P, N], U32, kb)
+            nc.vector.quantize_mx(w_w[i][:].bitcast(FP8X4), w_s[i][:], grouped[i][:])
 
-        pairs = [held("pairs%d" % c, [P, 2, 2, 2 * W], BF16) for c in range(NCH)]
-        z_bf = [held("z_bf%d" % c, [P, 2 * W * PACK], BF16) for c in range(NCH)]
+        z_bf = [held("z_bf%d" % c, [P, 2, WIDTHS[c] * PACK], BF16) for c in range(NCH)]
+        weighted = {}
+
+        def weigh(t, kb):
+            weighted[t] = placed("weighted%d" % t, [P, S], F32, kb)
+            nc.gpsimd.tensor_tensor(weighted[t][:], h_sb[t][:], wg[t][:], ALU.mult)
 
         def scatter(t):
-            if t == 0:
-                cut = HEAD // PER_COL
-                nc.vector.tensor_tensor(page[t][:].indirect(idx2[:, 0:cut]), h_head[:], wg[t][:, 0:HEAD], ALU.mult)
-                nc.vector.tensor_tensor(page[t][:].indirect(idx2[:, cut : S // PER_COL]), h_rest[:], wg[t][:, HEAD:S], ALU.mult)
-            else:
-                nc.vector.tensor_tensor(page[t][:].indirect(idx2[:]), h_sb[t][:], wg[t][:], ALU.mult)
+            nc.vector.tensor_copy(page[t][:].indirect(idx2[:]), weighted[t][:])
 
-        def read_page(t):
-            x = held("x%d" % t, [P, M], F32)
-            nc.vector.tensor_copy(x[:], page[t][:].indirect(idx3[:]))
-            return x
+        def read_page(t, kb, c0=0, w=M):
+            x = placed("x%d_%d" % (t, c0), [P, w], F32, kb)
+            nc.vector.tensor_copy(x[:], page[t][:].indirect(idx3[:, c0 // PER_COL : (c0 + w) // PER_COL]))
+            return x[:]
 
-        def features(t, x, chunks, kb, sine_gain_on_vector=False):
-            both = placed("feat%d_%d" % (t, chunks[0]), [P, 2, len(chunks) * W], F32, kb)
-            for f, func in enumerate((ACT.Sin, ACT.Square)):
-                nc.scalar.activation(both[:, f, :], x, func)
-                for i, c in enumerate(chunks):
-                    feat = both[:, f, W * i : W * (i + 1)]
-                    if c == 0 and t >= 2:
-                        target = z_bf[c][:, PACK * W * f + t : PACK * W * (f + 1) : PACK]
-                    else:
-                        target = pairs[c][:, t // 2, f, t % 2 : 2 * W : 2]
-                    if f == 0 and sine_gain_on_vector:
-                        nc.vector.tensor_scalar(target, feat, gain_sb[:, f, t : t + 1], None, ALU.mult)
-                    else:
-                        nc.scalar.activation(target, feat, ACT.Copy, scale=gain_sb[:, f, t : t + 1])
+        def features(t, x, kb_square, kb_sin, chunks=range(NCH), between=None):
+            c0 = STARTS[chunks[0]]
+            w = sum(WIDTHS[c] for c in chunks)
+            parts = [(z_bf[c], slice(t, PACK * WIDTHS[c], PACK), slice(STARTS[c] - c0, STARTS[c] - c0 + WIDTHS[c])) for c in chunks]
+            square = placed("square%d_%d" % (t, c0), [P, w], F32, kb_square)
+            nc.scalar.activation(square[:], x, ACT.Square)
+            for z, where, cols in parts:
+                nc.gpsimd.tensor_scalar(z[:, SQUARE, where], square[:, cols], gain_sb[:, SQUARE, t : t + 1], 0.0, ALU.mult, ALU.add)
+            sine = placed("sine%d_%d" % (t, c0), [P, w], F32, kb_sin)
+            nc.scalar.activation(sine[:], x, ACT.Sin)
+            if between is not None:
+                round_weight(*between)
+            for z, where, cols in parts:
+                nc.scalar.activation(z[:, SIN, where], sine[:, cols], ACT.Copy, scale=gain_sb[:, SIN, t : t + 1])
 
-        on_vector = (nc.vector.tensor_copy, I32)
-        on_scalar = (nc.scalar.copy, U32)
-
-        def weave(c, f0, f1, mover):
-            copy, dtype = mover
-            copy(
-                z_bf[c][:, PACK * W * f0 : PACK * W * f1].bitcast(dtype).rearrange("p (m u) -> p m u", u=2),
-                pairs[c][:, :, f0:f1, :].rearrange("p u f m -> p u (f m)").bitcast(dtype).rearrange("p u m -> p m u"),
-            )
-
-        scatter(0)
-        grouped = {0: round_weight(0), 2: round_weight(2)}
-        features(0, read_page(0)[:], range(NCH), 93)
-        grouped[1] = round_weight(1)
+        cut = HEAD // PER_COL
+        nc.vector.tensor_tensor(page[0][:].indirect(idx2[:, 0:cut]), h_head[:], wg[0][:, 0:HEAD], ALU.mult)
+        nc.vector.tensor_tensor(page[0][:].indirect(idx2[:, cut : S // PER_COL]), h_rest[:], wg[0][:, HEAD:S], ALU.mult)
+        weigh(1, 63)
+        round_weight(0, held("grouped0", [P, N * PACK], BF16))
+        features(0, read_page(0, 97), 14, 6, between=(1, placed("grouped1", [P, N * PACK], BF16, 97)))
+        weigh(2, 14)
+        load_page(3, 71)
+        weigh(3, 120)
         scatter(1)
-        wb_w = held("wb_w", [P, N], I32)
-        nc.vector.tensor_copy(wb_w[:].rearrange("p (t m) -> p t m", t=PACK), wb_w_raw[:].rearrange("p (m t) -> p t m", t=PACK))
-        features(1, read_page(1)[:], range(NCH), 44)
-        nc.scalar.copy(z_bf[0][:].bitcast(U32)[:, 0 : 4 * W : 2], pairs[0][:, 0, :, :].rearrange("p f m -> p (f m)").bitcast(U32))
+        features(1, read_page(1, 59), 3, 7)
+        wb_w = placed("wb_w", [P, N], I32, 3)
+        nc.gpsimd.tensor_copy(wb_w[:].rearrange("p (t m) -> p t m", t=PACK), wb_w_raw[:].rearrange("p (m t) -> p t m", t=PACK))
+        round_weight(2, placed("grouped2", [P, N * PACK], BF16, 7))
         scatter(2)
-        wb_s = held("wb_s", [P, N], U8)
-        nc.vector.tensor_copy(wb_s[:].rearrange("p (t m) -> p t m", t=PACK), wb_s_raw[:].rearrange("p (m t) -> p t m", t=PACK))
-        features(2, read_page(2)[:], range(NCH), 44)
+        quantise_weight(0, 14)
+        quantise_weight(1, 16)
+        features(2, read_page(2, 107), 45, 49)
+        wb_s = placed("wb_s", [P, N], U8, 45)
+        nc.gpsimd.tensor_copy(wb_s[:].rearrange("p (t m) -> p t m", t=PACK), wb_s_raw[:].rearrange("p (m t) -> p t m", t=PACK))
         scatter(LAST)
 
-        z_w = [held("z_w%d" % c, [P, 2, W], U32) for c in range(NCH)]
-        z_s = [held("z_s%d" % c, [P, 2, W], U8) for c in range(NCH)]
-        x_head = held("x_head", [P, W], F32)
-        x_rest = held("x_rest", [P, M - W], F32)
-        x_last = [x_head[:]] + [x_rest[:, W * c : W * (c + 1)] for c in range(NCH - 1)]
+        z_w = [held("z_w%d" % c, [P, 2, WIDTHS[c]], U32) for c in range(NCH)]
+        z_s = [held("z_s%d" % c, [P, 2, WIDTHS[c]], U8) for c in range(NCH)]
+        x_last = placed("x_last", [P, M], F32, 101)
+        for c0, c1 in ((0, STARTS[2]), (STARTS[2], M)):
+            nc.vector.tensor_copy(x_last[:, c0:c1], page[LAST][:].indirect(idx3[:, c0 // PER_COL : c1 // PER_COL]))
         y_s = held("y_s", [P, M], U8)
         y_rows = out_0.rearrange("(p t) m -> p t m", t=PACK)
         code_rows = out_1[0].rearrange("p m t -> p (m t)")
         y = {}
+        places = ((49, 52.75), (49.5, 50.5), (51.5, 50.5), (49.5, 50.5), (49, 51.5))
 
-        def last_features(c, sine_gain_on_vector=False):
-            features(LAST, x_last[c], [c], 2 * c, sine_gain_on_vector)
-
-        def quantise_z(c):
+        def make_z(c):
+            c0, w = STARTS[c], WIDTHS[c]
+            features(LAST, x_last[:, c0 : c0 + w], places[c][0], places[c][1], [c])
             nc.vector.quantize_mx(
-                z_w[c][:].rearrange("p f m -> p (f m)").bitcast(FP8X4), z_s[c][:].rearrange("p f m -> p (f m)"), z_bf[c][:]
+                z_w[c][:].rearrange("p f m -> p (f m)").bitcast(FP8X4), z_s[c][:].rearrange("p f m -> p (f m)"),
+                z_bf[c][:].rearrange("p f m -> p (f m)"),
             )
 
         def product(c, slots, terms):
-            acc = psum.tile([P, len(slots) * W], F32, name="acc", tag="bank")
+            w = WIDTHS[c]
+            acc = psum.tile([P, BANK], F32, name="acc", tag="bank")
             for i, t in enumerate(slots):
                 cols = slice(P * t, P * (t + 1))
                 for n, (words, scales, f) in enumerate(terms):
                     nc.tensor.matmul_mx(
-                        acc[:, i * W : (i + 1) * W], lhsT=words[:, cols].bitcast(FP8X4), lhsT_scale=scales[:, cols],
-                        rhs=z_w[c][:, f, :].bitcast(FP8X4), rhs_scale=z_s[c][:, f, :], start=(n == 0), stop=(n == len(terms) - 1),
+                        acc[:, i * w : (i + 1) * w], lhsT=words[:, cols].bitcast(FP8X4), lhsT_scale=scales[:, cols],
+                        rhs=z_w[c][:, f, :].bitcast(FP8X4), rhs_scale=z_s[c][:, f, :],
+                        start=(n == 0), stop=(n == len(terms) - 1),
                     )
             return acc
 
         def make_y(c):
-            y[c] = held("y%d" % c, [P, PACK, W], F32)
-            slot_pairs = (range(0, 2), range(2, 4))
+            c0, w = STARTS[c], WIDTHS[c]
+            y[c] = held("y%d" % c, [P, PACK, w], F32)
+            groups = [range(t0, t0 + BANK // w) for t0 in range(0, PACK, BANK // w)]
             ab = []
-            for slots in slot_pairs:
-                a_ps = product(c, slots, [(w_w[0], w_s[0], 0)])
-                b_ps = product(c, slots, [(wb_w, wb_s, 1)])
+            for slots in groups:
+                a_ps = product(c, slots, [(w_w[0], w_s[0], SIN)])
+                b_ps = product(c, slots, [(wb_w, wb_s, SQUARE)])
                 a_sb = deep.tile([P, BANK], F32, name="a_sb", tag="a_sb")
                 nc.scalar.copy(a_sb[:], a_ps[:])
                 ab.append(deep.tile([P, BANK], F32, name="ab", tag="ab"))
                 nc.vector.tensor_tensor(ab[-1][:], b_ps[:], a_sb[:], ALU.mult)
-            for slots, prod in zip(slot_pairs, ab):
-                d_ps = product(c, slots, [(w_w[1], w_s[1], 0), (w_w[2], w_s[2], 1)])
+            for slots, prod in zip(groups, ab):
+                d_ps = product(c, slots, [(w_w[1], w_s[1], SIN), (w_w[2], w_s[2], SQUARE)])
                 for i, t in enumerate(slots):
-                    cols = slice(i * W, (i + 1) * W)
+                    cols = slice(i * w, (i + 1) * w)
                     nc.vector.scalar_tensor_tensor(y[c][:, t, :], d_ps[:, cols], bias_sb[:, t : t + 1], prod[:, cols], ALU.add, ALU.add)
-            step = PACK if c < NCH - 1 else 2
-            for t0 in range(0, PACK, step):
-                nc.sync.dma_start(y_rows[:, t0 : t0 + step, W * c : W * (c + 1)], y[c][:, t0 : t0 + step, :])
+            nc.sync.dma_start(y_rows[:, :, c0 : c0 + w], y[c][:])
 
         def make_planes(c):
-            y_bf = held("y_bf%d" % c, [P, W * PACK], BF16)
+            c0, w = STARTS[c], WIDTHS[c]
+            y_bf = held("y_bf%d" % c, [P, w * PACK], BF16)
             target = y_bf[:].rearrange("p (g i t) -> p g t i", i=4, t=PACK)
             source = y[c][:].rearrange("p t (g i) -> p g t i", i=4)
-            if c < NCH - 1:
-                nc.scalar.copy(target, source)
-            else:
-                nc.scalar.copy(target[:, :, 0:2, :], source[:, :, 0:2, :])
-                nc.vector.tensor_copy(target[:, :, 2:4, :], source[:, :, 2:4, :])
-            y_w = held("y_w%d" % c, [P, W], I32)
-            nc.vector.quantize_mx(y_w[:].bitcast(FP8X4), y_s[:, W * c : W * (c + 1)], y_bf[:])
-            nc.sync.dma_start(code_rows[:, PACK * W * c : PACK * W * (c + 1)].bitcast(I32), y_w[:])
+            (nc.scalar.copy if c < NCH - 1 else nc.vector.tensor_copy)(target, source)
+            y_w = held("y_w%d" % c, [P, w], I32)
+            nc.vector.quantize_mx(y_w[:].bitcast(FP8X4), y_s[:, c0 : c0 + w], y_bf[:])
+            nc.sync.dma_start(code_rows[:, PACK * c0 : PACK * (c0 + w)].bitcast(I32), y_w[:])
 
-        nc.vector.tensor_copy(x_head[:], page[LAST][:].indirect(idx3[:, 0 : W // PER_COL]))
-        nc.vector.tensor_copy(x_rest[:], page[LAST][:].indirect(idx3[:, W // PER_COL : M // PER_COL]))
-        quantise_weight(0, placed("w_w0", [P, N], U32, 91), grouped[0])
-        quantise_weight(1, placed("w_w1", [P, N], U32, 89), grouped[1])
-        last_features(0)
-        quantise_z(0)
-        last_features(1, sine_gain_on_vector=True)
-        weave(1, 0, 2, on_vector)
-        quantise_z(1)
-        quantise_weight(2, placed("w_w2", [P, N], U32, 0), grouped[2])
-        last_features(2)
-        make_y(0)
-        weave(2, 0, 1, on_vector)
-        weave(2, 1, 2, on_scalar)
-        quantise_z(2)
-        last_features(3)
-        make_y(1)
-        weave(3, 0, 2, on_scalar)
-        quantise_z(3)
+        make_z(0)
+        quantise_weight(2, 105)
+        make_z(1)
         for c in range(NCH):
-            make_planes(c)
+            make_y(c)
             if c + 2 < NCH:
-                make_y(c + 2)
+                make_z(c + 2)
+            if c >= 1:
+                make_planes(c - 1)
+        make_planes(NCH - 1)
         for q in range(4):
             eng = nc.sync if q % 2 == 0 else nc.scalar
             eng.dma_start(out_2[0, 4 * q : 4 * q + 4, :].bitcast(I32), y_s[QUAD * q : QUAD * q + 4, :].bitcast(I32))

@@ -150,7 +150,7 @@ def tile_list_electrode_refit_kernel(
         load_wg(3, 32)
         load_page(2, 37)
         load_weight(2, 45)
-        wb_w_raw = placed("wb_w_raw", [P, N], I32, 53)
+        wb_w_raw = placed("wb_w_raw", [P, N], I32, 53.5)
         nc.sync.dma_start(wb_w_raw[:], wb_words[0].rearrange("p c i -> p (c i)").bitcast(I32))
         wb_s_raw = placed("wb_s_raw", [P, N], U8, 36)
         nc.gpsimd.memset(wb_s_raw[:].bitcast(I32), 0)
@@ -172,7 +172,23 @@ def tile_list_electrode_refit_kernel(
             w_w[i] = placed("w_w%d" % i, [P, N], U32, kb)
             nc.vector.quantize_mx(w_w[i][:].bitcast(FP8X4), w_s[i][:], grouped[i][:])
 
-        z_bf = [held("z_bf%d" % c, [P, 2, WIDTHS[c] * PACK], BF16) for c in range(NCH)]
+        z_all = [held("z_bf%d" % f, [P, M * PACK], BF16) for f in range(2)]
+
+        def z_bf(f, c0, c1):
+            return z_all[f][:, PACK * c0 : PACK * c1]
+
+        def apply_gain(eng, f, t, c0, c1, values):
+            target = z_bf(f, c0, c1)[:, t : PACK * (c1 - c0) : PACK]
+            if eng is nc.scalar:
+                nc.scalar.activation(target, values, ACT.Copy, scale=gain_sb[:, f, t : t + 1])
+            else:
+                eng.tensor_scalar(target, values, gain_sb[:, f, t : t + 1], 0.0, ALU.mult, ALU.add)
+
+        def feature(f, name, x, w, kb):
+            values = placed(name, [P, w], F32, kb)
+            nc.scalar.activation(values[:], x, ACT.Sin if f == SIN else ACT.Square)
+            return values
+
         weighted = {}
 
         def weigh(t, kb):
@@ -187,20 +203,13 @@ def tile_list_electrode_refit_kernel(
             nc.vector.tensor_copy(x[:], page[t][:].indirect(idx3[:, c0 // PER_COL : (c0 + w) // PER_COL]))
             return x[:]
 
-        def features(t, x, kb_square, kb_sin, chunks=range(NCH), between=None):
-            c0 = STARTS[chunks[0]]
-            w = sum(WIDTHS[c] for c in chunks)
-            parts = [(z_bf[c], slice(t, PACK * WIDTHS[c], PACK), slice(STARTS[c] - c0, STARTS[c] - c0 + WIDTHS[c])) for c in chunks]
-            square = placed("square%d_%d" % (t, c0), [P, w], F32, kb_square)
-            nc.scalar.activation(square[:], x, ACT.Square)
-            for z, where, cols in parts:
-                nc.gpsimd.tensor_scalar(z[:, SQUARE, where], square[:, cols], gain_sb[:, SQUARE, t : t + 1], 0.0, ALU.mult, ALU.add)
-            sine = placed("sine%d_%d" % (t, c0), [P, w], F32, kb_sin)
-            nc.scalar.activation(sine[:], x, ACT.Sin)
+        def features(t, x, kb_square, kb_sin, between=None):
+            square = feature(SQUARE, "square%d" % t, x, M, kb_square)
+            apply_gain(nc.gpsimd, SQUARE, t, 0, M, square[:])
+            sine = feature(SIN, "sine%d" % t, x, M, kb_sin)
             if between is not None:
                 round_weight(*between)
-            for z, where, cols in parts:
-                nc.scalar.activation(z[:, SIN, where], sine[:, cols], ACT.Copy, scale=gain_sb[:, SIN, t : t + 1])
+            apply_gain(nc.scalar, SIN, t, 0, M, sine[:])
 
         cut = HEAD // PER_COL
         nc.vector.tensor_tensor(page[0][:].indirect(idx2[:, 0:cut]), h_head[:], wg[0][:, 0:HEAD], ALU.mult)
@@ -213,19 +222,19 @@ def tile_list_electrode_refit_kernel(
         weigh(3, 120)
         scatter(1)
         features(1, read_page(1, 59), 3, 7)
-        wb_w = placed("wb_w", [P, N], I32, 3)
-        nc.gpsimd.tensor_copy(wb_w[:].rearrange("p (t m) -> p t m", t=PACK), wb_w_raw[:].rearrange("p (m t) -> p t m", t=PACK))
         round_weight(2, placed("grouped2", [P, N * PACK], BF16, 7))
         scatter(2)
         quantise_weight(0, 14)
         quantise_weight(1, 16)
         features(2, read_page(2, 107), 45, 49)
+        wb_w = placed("wb_w", [P, N], I32, 46)
+        nc.gpsimd.tensor_copy(wb_w[:].rearrange("p (t m) -> p t m", t=PACK), wb_w_raw[:].rearrange("p (m t) -> p t m", t=PACK))
         wb_s = placed("wb_s", [P, N], U8, 45)
         nc.gpsimd.tensor_copy(wb_s[:].rearrange("p (t m) -> p t m", t=PACK), wb_s_raw[:].rearrange("p (m t) -> p t m", t=PACK))
         scatter(LAST)
 
-        z_w = [held("z_w%d" % c, [P, 2, WIDTHS[c]], U32) for c in range(NCH)]
-        z_s = [held("z_s%d" % c, [P, 2, WIDTHS[c]], U8) for c in range(NCH)]
+        z_w = [held("z_w%d" % f, [P, M], U32) for f in range(2)]
+        z_s = [held("z_s%d" % f, [P, M], U8) for f in range(2)]
         x_last = placed("x_last", [P, M], F32, 101)
         for c0, c1 in ((0, STARTS[2]), (STARTS[2], M)):
             nc.vector.tensor_copy(x_last[:, c0:c1], page[LAST][:].indirect(idx3[:, c0 // PER_COL : c1 // PER_COL]))
@@ -233,25 +242,19 @@ def tile_list_electrode_refit_kernel(
         y_rows = out_0.rearrange("(p t) m -> p t m", t=PACK)
         code_rows = out_1[0].rearrange("p m t -> p (m t)")
         y = {}
-        places = ((49, 52.75), (49.5, 50.5), (51.5, 50.5), (49.5, 50.5), (49, 51.5))
 
-        def make_z(c):
-            c0, w = STARTS[c], WIDTHS[c]
-            features(LAST, x_last[:, c0 : c0 + w], places[c][0], places[c][1], [c])
-            nc.vector.quantize_mx(
-                z_w[c][:].rearrange("p f m -> p (f m)").bitcast(FP8X4), z_s[c][:].rearrange("p f m -> p (f m)"),
-                z_bf[c][:].rearrange("p f m -> p (f m)"),
-            )
+        def quantise_z(f, c0, c1):
+            nc.vector.quantize_mx(z_w[f][:, c0:c1].bitcast(FP8X4), z_s[f][:, c0:c1], z_bf(f, c0, c1))
 
         def product(c, slots, terms):
-            w = WIDTHS[c]
+            c0, w = STARTS[c], WIDTHS[c]
             acc = psum.tile([P, BANK], F32, name="acc", tag="bank")
             for i, t in enumerate(slots):
                 cols = slice(P * t, P * (t + 1))
                 for n, (words, scales, f) in enumerate(terms):
                     nc.tensor.matmul_mx(
                         acc[:, i * w : (i + 1) * w], lhsT=words[:, cols].bitcast(FP8X4), lhsT_scale=scales[:, cols],
-                        rhs=z_w[c][:, f, :].bitcast(FP8X4), rhs_scale=z_s[c][:, f, :],
+                        rhs=z_w[f][:, c0 : c0 + w].bitcast(FP8X4), rhs_scale=z_s[f][:, c0 : c0 + w],
                         start=(n == 0), stop=(n == len(terms) - 1),
                     )
             return acc
@@ -260,30 +263,46 @@ def tile_list_electrode_refit_kernel(
             c0, w = STARTS[c], WIDTHS[c]
             y[c] = held("y%d" % c, [P, PACK, w], F32)
             groups = [range(t0, t0 + BANK // w) for t0 in range(0, PACK, BANK // w)]
-            ab = []
-            for slots in groups:
-                a_ps = product(c, slots, [(w_w[0], w_s[0], SIN)])
-                b_ps = product(c, slots, [(wb_w, wb_s, SQUARE)])
-                a_sb = deep.tile([P, BANK], F32, name="a_sb", tag="a_sb")
-                nc.scalar.copy(a_sb[:], a_ps[:])
-                ab.append(deep.tile([P, BANK], F32, name="ab", tag="ab"))
-                nc.vector.tensor_tensor(ab[-1][:], b_ps[:], a_sb[:], ALU.mult)
-            for slots, prod in zip(groups, ab):
-                d_ps = product(c, slots, [(w_w[1], w_s[1], SIN), (w_w[2], w_s[2], SQUARE)])
-                for i, t in enumerate(slots):
-                    cols = slice(i * w, (i + 1) * w)
-                    nc.vector.scalar_tensor_tensor(y[c][:, t, :], d_ps[:, cols], bias_sb[:, t : t + 1], prod[:, cols], ALU.add, ALU.add)
-            nc.sync.dma_start(y_rows[:, :, c0 : c0 + w], y[c][:])
+            for pair in (groups[i : i + 2] for i in range(0, len(groups), 2)):
+                ab = []
+                for slots in pair:
+                    a_ps = product(c, slots, [(w_w[0], w_s[0], SIN)])
+                    b_ps = product(c, slots, [(wb_w, wb_s, SQUARE)])
+                    a_sb = deep.tile([P, BANK], F32, name="a_sb", tag="a_sb")
+                    nc.scalar.copy(a_sb[:], a_ps[:])
+                    ab.append(deep.tile([P, BANK], F32, name="ab", tag="ab"))
+                    nc.vector.tensor_tensor(ab[-1][:], b_ps[:], a_sb[:], ALU.mult)
+                for slots, prod in zip(pair, ab):
+                    d_ps = product(c, slots, [(w_w[1], w_s[1], SIN), (w_w[2], w_s[2], SQUARE)])
+                    for i, t in enumerate(slots):
+                        cols = slice(i * w, (i + 1) * w)
+                        nc.vector.scalar_tensor_tensor(y[c][:, t, :], d_ps[:, cols], bias_sb[:, t : t + 1], prod[:, cols], ALU.add, ALU.add)
+            step = PACK
+            for t0 in range(0, PACK, step):
+                nc.sync.dma_start(y_rows[:, t0 : t0 + step, c0 : c0 + w], y[c][:, t0 : t0 + step, :])
 
         def make_planes(c):
             c0, w = STARTS[c], WIDTHS[c]
             y_bf = held("y_bf%d" % c, [P, w * PACK], BF16)
             target = y_bf[:].rearrange("p (g i t) -> p g t i", i=4, t=PACK)
             source = y[c][:].rearrange("p t (g i) -> p g t i", i=4)
-            (nc.scalar.copy if c < NCH - 1 else nc.vector.tensor_copy)(target, source)
+            if c < NCH - 1:
+                nc.scalar.copy(target, source)
+            else:
+                nc.vector.tensor_copy(target, source)
             y_w = held("y_w%d" % c, [P, w], I32)
             nc.vector.quantize_mx(y_w[:].bitcast(FP8X4), y_s[:, c0 : c0 + w], y_bf[:])
             nc.sync.dma_start(code_rows[:, PACK * c0 : PACK * (c0 + w)].bitcast(I32), y_w[:])
+
+        places = ((49, 52.75), (49.5, 50.5), (51.5, 50.5), (49.5, 50.5), (49, 51.5))
+
+        def make_z(c):
+            c0, w = STARTS[c], WIDTHS[c]
+            x = x_last[:, c0 : c0 + w]
+            apply_gain(nc.gpsimd, SQUARE, LAST, c0, c0 + w, feature(SQUARE, "square_last%d" % c, x, w, places[c][0])[:])
+            apply_gain(nc.scalar, SIN, LAST, c0, c0 + w, feature(SIN, "sine_last%d" % c, x, w, places[c][1])[:])
+            quantise_z(SQUARE, c0, c0 + w)
+            quantise_z(SIN, c0, c0 + w)
 
         make_z(0)
         quantise_weight(2, 105)

@@ -24,7 +24,7 @@ PER_COL = 16
 KB = 1024
 HEAD = 256
 PIECES = ((0, HEAD), (HEAD, BANK), (HEAD + BANK, S - HEAD - BANK))
-WIDTHS = (128, 256, 256, 256, 128)
+WIDTHS = (256, 256, 256, 256)
 STARTS = tuple(sum(WIDTHS[:c]) for c in range(len(WIDTHS)))
 NCH = len(WIDTHS)
 LAST = PACK - 1
@@ -158,7 +158,7 @@ def tile_list_electrode_refit_kernel(
             nc.sync.dma_start(wb_s_raw[QUAD * q : QUAD * q + 4, :].bitcast(I32), wb_scales[0, 4 * q : 4 * q + 4, :].bitcast(I32))
         nc.sync.dma_start(bias_sb[:], bias.rearrange("(p t) -> p t", t=PACK))
 
-        w_s = [held("w_s0", [P, N], U8), held("w_s1", [P, N], U8), placed("w_s2", [P, N], U8, 52.5)]
+        w_s = [held("w_s0", [P, N], U8), held("w_s1", [P, N], U8), placed("w_s2", [P, N], U8, 50.75)]
         w_w, grouped = {}, {}
 
         def round_weight(i, tile):
@@ -236,7 +236,7 @@ def tile_list_electrode_refit_kernel(
         z_w = [held("z_w%d" % f, [P, M], U32) for f in range(2)]
         z_s = [held("z_s%d" % f, [P, M], U8) for f in range(2)]
         x_last = placed("x_last", [P, M], F32, 101)
-        for c0, c1 in ((0, STARTS[2]), (STARTS[2], M)):
+        for c0, c1 in ((0, STARTS[1]), (STARTS[1], M)):
             nc.vector.tensor_copy(x_last[:, c0:c1], page[LAST][:].indirect(idx3[:, c0 // PER_COL : c1 // PER_COL]))
         y_s = held("y_s", [P, M], U8)
         y_rows = out_0.rearrange("(p t) m -> p t m", t=PACK)
@@ -277,7 +277,7 @@ def tile_list_electrode_refit_kernel(
                     for i, t in enumerate(slots):
                         cols = slice(i * w, (i + 1) * w)
                         nc.vector.scalar_tensor_tensor(y[c][:, t, :], d_ps[:, cols], bias_sb[:, t : t + 1], prod[:, cols], ALU.add, ALU.add)
-            step = PACK
+            step = PACK if c < NCH - 1 else 2
             for t0 in range(0, PACK, step):
                 nc.sync.dma_start(y_rows[:, t0 : t0 + step, c0 : c0 + w], y[c][:, t0 : t0 + step, :])
 
@@ -289,17 +289,18 @@ def tile_list_electrode_refit_kernel(
             if c < NCH - 1:
                 nc.scalar.copy(target, source)
             else:
-                nc.vector.tensor_copy(target, source)
+                nc.scalar.copy(target[:, :, 0:2, :], source[:, :, 0:2, :])
+                nc.vector.tensor_copy(target[:, :, 2:4, :], source[:, :, 2:4, :])
             y_w = held("y_w%d" % c, [P, w], I32)
             nc.vector.quantize_mx(y_w[:].bitcast(FP8X4), y_s[:, c0 : c0 + w], y_bf[:])
             nc.sync.dma_start(code_rows[:, PACK * c0 : PACK * (c0 + w)].bitcast(I32), y_w[:])
 
-        places = ((49, 52.75), (49.5, 50.5), (51.5, 50.5), (49.5, 50.5), (49, 51.5))
+        places = ((49, 50.5), (49.75, 51.25), (48.75, 52), (49.75, 52))
 
         def make_z(c):
             c0, w = STARTS[c], WIDTHS[c]
             x = x_last[:, c0 : c0 + w]
-            apply_gain(nc.gpsimd, SQUARE, LAST, c0, c0 + w, feature(SQUARE, "square_last%d" % c, x, w, places[c][0])[:])
+            apply_gain(nc.gpsimd if c == 0 else nc.vector, SQUARE, LAST, c0, c0 + w, feature(SQUARE, "square_last%d" % c, x, w, places[c][0])[:])
             apply_gain(nc.scalar, SIN, LAST, c0, c0 + w, feature(SIN, "sine_last%d" % c, x, w, places[c][1])[:])
             quantise_z(SQUARE, c0, c0 + w)
             quantise_z(SIN, c0, c0 + w)

@@ -55,7 +55,7 @@ def tile_list_electrode_refit_kernel(
 
         tab_s = placed("tab_s", [P, T], U8, 83)
         w1_s_raw = placed("w1_s_raw", [P, 2, H], U8, 95)
-        v_s = placed("v_s", [P, 2, S], U8, 36)
+        v_s = placed("v_s", [P, 2, S], U8, 38)
         nc.gpsimd.memset(w1_s_raw[:].rearrange("p a c -> p (a c)").bitcast(I32), 0)
         nc.vector.memset(tab_s[0 : P - QUAD, :].bitcast(I32), 0)
         nc.vector.memset(v_s[:].rearrange("p a c -> p (a c)").bitcast(I32), 0)
@@ -72,7 +72,7 @@ def tile_list_electrode_refit_kernel(
         nc.sync.dma_start(idx3[:], offs3)
         w1_w_raw = placed("w1_w_raw", [P, 2, 2 * H], U8, 91)
         nc.sync.dma_start(w1_w_raw[:].bitcast(I32), w1_words.rearrange("a p c -> p a c").bitcast(I32))
-        tab_w = [placed("tab_w%d" % a, [P, T], I32, 12 + 104 * a) for a in range(2)]
+        tab_w = [placed("tab_w%d" % a, [P, T], I32, (13.75, 116)[a]) for a in range(2)]
         for a in range(2):
             nc.sync.dma_start(tab_w[a][:], tab_words[a].rearrange("p t i -> p (t i)").bitcast(I32))
 
@@ -102,10 +102,10 @@ def tile_list_electrode_refit_kernel(
             nc.sync.dma_start(v_s[QUAD * q : QUAD * q + 4, :, :].bitcast(I32), picked_s[row : row + 8, :].bitcast(I32))
         load_page(0, 83)
 
-        w1_w = placed("w1_w", [P, 2, PACK, 2 * P], U8, 45)
+        w1_w = placed("w1_w", [P, 2, PACK, 2 * P], U8, 47)
         nc.vector.tensor_copy(w1_w[:].bitcast(U16), w1_w_raw[:].bitcast(U16).rearrange("p a (m t) -> p a t m", t=PACK))
         load_wg(0, 91, (0, HEAD, S))
-        w1_s = placed("w1_s", [P, 2, PACK, P], U8, 53)
+        w1_s = placed("w1_s", [P, 2, PACK, P], U8, 63)
         w1_s_by_slot = w1_s_raw[:].rearrange("p a (m t) -> p a t m", t=PACK)
         nc.gpsimd.tensor_copy(w1_s[:, :, 0, :], w1_s_by_slot[:, :, 0, :])
         nc.gpsimd.tensor_copy(w1_s[:, :, 1:PACK, :], w1_s_by_slot[:, :, 1:PACK, :])
@@ -118,7 +118,10 @@ def tile_list_electrode_refit_kernel(
 
         h_head = placed("h_head", [P, HEAD], F32, 79)
         h_rest = placed("h_rest", [P, S - HEAD], F32, 80)
-        h_sb = {t: placed("h%d" % t, [P, S], F32, kb) for t, kb in ((1, 4), (2, 71), (3, 0))}
+        h_sb = {t: placed("h%d" % t, [P, S], F32, kb) for t, kb in ((1, 5.75), (2, 74), (3, 122))}
+
+        h2_head = placed("h2_head", [P, HEAD], F32, 73)
+        h3_head = placed("h3_head", [P, BANK], F32, 3.75)
 
         def make_h(t, c0, w, target):
             acc = psum.tile([P, w], F32, name="acc", tag="bank")
@@ -131,34 +134,41 @@ def tile_list_electrode_refit_kernel(
                         rhs=v_w[a][:, cols].bitcast(FP8X4), rhs_scale=v_s[:, a, cols],
                         start=(a == 0 and b == 0), stop=(a == 1 and b == w - n),
                     )
-            nc.scalar.copy(target, acc[:])
+            for part, cols in target:
+                nc.scalar.copy(part, acc[:, cols])
 
         for c0, w in PIECES:
-            make_h(0, c0, w, h_head[:] if c0 == 0 else h_rest[:, c0 - HEAD : c0 - HEAD + w])
+            make_h(0, c0, w, [(h_head[:] if c0 == 0 else h_rest[:, c0 - HEAD : c0 - HEAD + w], slice(0, w))])
         for t in range(1, PACK):
             for c0 in (0, BANK):
-                make_h(t, c0, BANK, h_sb[t][:, c0 : c0 + BANK])
+                if (t, c0) == (2, 0):
+                    make_h(t, c0, BANK, [(h2_head[:], slice(0, HEAD)), (h_sb[t][:, HEAD:BANK], slice(HEAD, BANK))])
+                elif (t, c0) == (3, 0):
+                    make_h(t, c0, BANK, [(h3_head[:], slice(0, BANK))])
+                else:
+                    make_h(t, c0, BANK, [(h_sb[t][:, c0 : c0 + BANK], slice(0, BANK))])
 
-        load_wg(1, 16)
-        load_weight(0, 8)
+        load_wg(1, 17.75)
+        load_weight(0, 9.75)
         load_page(1, 112)
-        gain_sb = placed("gain_sb", [P, 2, PACK], F32, 36.5)
-        bias_sb = placed("bias_sb", [P, PACK], F32, 36.75)
+        gain_sb = placed("gain_sb", [P, 2, PACK], F32, 38.5)
+        bias_sb = placed("bias_sb", [P, PACK], F32, 38.75)
         nc.sync.dma_start(gain_sb[:], gain.rearrange("(f p t) -> p f t", f=2, t=PACK))
-        load_weight(1, 24)
-        load_wg(2, 120)
-        load_wg(3, 32)
-        load_page(2, 37)
-        load_weight(2, 45)
-        wb_w_raw = placed("wb_w_raw", [P, N], I32, 53.5)
+        load_weight(1, 22)
+        load_page(2, 39)
+        load_wg(2, 30)
+        wb_w_raw = placed("wb_w_raw", [P, N], I32, 63.5)
         nc.sync.dma_start(wb_w_raw[:], wb_words[0].rearrange("p c i -> p (c i)").bitcast(I32))
-        wb_s_raw = placed("wb_s_raw", [P, N], U8, 36)
+        load_page(3, 55.5)
+        load_wg(3, 34)
+        load_weight(2, 47)
+        wb_s_raw = placed("wb_s_raw", [P, N], U8, 38)
         nc.gpsimd.memset(wb_s_raw[:].bitcast(I32), 0)
         for q in range(4):
             nc.sync.dma_start(wb_s_raw[QUAD * q : QUAD * q + 4, :].bitcast(I32), wb_scales[0, 4 * q : 4 * q + 4, :].bitcast(I32))
         nc.sync.dma_start(bias_sb[:], bias.rearrange("(p t) -> p t", t=PACK))
 
-        w_s = [held("w_s0", [P, N], U8), held("w_s1", [P, N], U8), placed("w_s2", [P, N], U8, 50.75)]
+        w_s = [placed("w_s%d" % i, [P, N], U8, kb) for i, kb in enumerate((4, 4.5, 52.75))]
         w_w, grouped = {}, {}
 
         def round_weight(i, tile):
@@ -195,8 +205,8 @@ def tile_list_electrode_refit_kernel(
             weighted[t] = placed("weighted%d" % t, [P, S], F32, kb)
             nc.gpsimd.tensor_tensor(weighted[t][:], h_sb[t][:], wg[t][:], ALU.mult)
 
-        def scatter(t):
-            nc.vector.tensor_copy(page[t][:].indirect(idx2[:]), weighted[t][:])
+        def scatter(t, c0=0, c1=S):
+            nc.vector.tensor_copy(page[t][:].indirect(idx2[:, c0 // PER_COL : c1 // PER_COL]), weighted[t][:, c0:c1])
 
         def read_page(t, kb, c0=0, w=M):
             x = placed("x%d_%d" % (t, c0), [P, w], F32, kb)
@@ -214,24 +224,30 @@ def tile_list_electrode_refit_kernel(
         cut = HEAD // PER_COL
         nc.vector.tensor_tensor(page[0][:].indirect(idx2[:, 0:cut]), h_head[:], wg[0][:, 0:HEAD], ALU.mult)
         nc.vector.tensor_tensor(page[0][:].indirect(idx2[:, cut : S // PER_COL]), h_rest[:], wg[0][:, HEAD:S], ALU.mult)
-        weigh(1, 63)
+        weigh(1, 66)
         round_weight(0, held("grouped0", [P, N * PACK], BF16))
-        features(0, read_page(0, 97), 14, 6, between=(1, placed("grouped1", [P, N * PACK], BF16, 97)))
-        weigh(2, 14)
-        load_page(3, 71)
-        weigh(3, 120)
-        scatter(1)
-        features(1, read_page(1, 59), 3, 7)
-        round_weight(2, placed("grouped2", [P, N * PACK], BF16, 7))
-        scatter(2)
-        quantise_weight(0, 14)
-        quantise_weight(1, 16)
-        features(2, read_page(2, 107), 45, 49)
-        wb_w = placed("wb_w", [P, N], I32, 46)
+        features(0, read_page(0, 97), 15.75, 7.75, between=(1, placed("grouped1", [P, N * PACK], BF16, 97)))
+        weighted[2] = placed("weighted2", [P, S], F32, 15.75)
+        nc.gpsimd.tensor_tensor(weighted[2][:, 0:HEAD], h2_head[:], wg[2][:, 0:HEAD], ALU.mult)
+        nc.gpsimd.tensor_tensor(weighted[2][:, HEAD:S], h_sb[2][:, HEAD:S], wg[2][:, HEAD:S], ALU.mult)
+        wb_w = placed("wb_w", [P, N], I32, 76)
         nc.gpsimd.tensor_copy(wb_w[:].rearrange("p (t m) -> p t m", t=PACK), wb_w_raw[:].rearrange("p (m t) -> p t m", t=PACK))
-        wb_s = placed("wb_s", [P, N], U8, 45)
+        weighted[3] = placed("weighted3", [P, S], F32, 30)
+        nc.gpsimd.tensor_tensor(weighted[3][:, 0:BANK], h3_head[:], wg[3][:, 0:BANK], ALU.mult)
+        nc.gpsimd.tensor_tensor(weighted[3][:, BANK:S], h_sb[3][:, BANK:S], wg[3][:, BANK:S], ALU.mult)
+        scatter(1)
+        scatter(2, 0, HEAD)
+        features(1, read_page(1, 70), 5.25, 9.25)
+        wb_s = placed("wb_s", [P, N], U8, 5.25)
         nc.gpsimd.tensor_copy(wb_s[:].rearrange("p (t m) -> p t m", t=PACK), wb_s_raw[:].rearrange("p (m t) -> p t m", t=PACK))
-        scatter(LAST)
+        round_weight(2, placed("grouped2", [P, N * PACK], BF16, 9.25))
+        scatter(2, HEAD, S)
+        scatter(LAST, 0, HEAD)
+        x = read_page(2, 0)
+        quantise_weight(0, 107)
+        quantise_weight(1, 109)
+        features(2, x, 47, 51)
+        scatter(LAST, HEAD, S)
 
         z_w = [held("z_w%d" % f, [P, M], U32) for f in range(2)]
         z_s = [held("z_s%d" % f, [P, M], U8) for f in range(2)]
@@ -295,7 +311,7 @@ def tile_list_electrode_refit_kernel(
             nc.vector.quantize_mx(y_w[:].bitcast(FP8X4), y_s[:, c0 : c0 + w], y_bf[:])
             nc.sync.dma_start(code_rows[:, PACK * c0 : PACK * (c0 + w)].bitcast(I32), y_w[:])
 
-        places = ((49, 50.5), (49.75, 51.25), (48.75, 52), (49.75, 52))
+        places = ((51, 52.5), (51.75, 53.25), (50.75, 54), (51.75, 54))
 
         def make_z(c):
             c0, w = STARTS[c], WIDTHS[c]

@@ -110,7 +110,7 @@ def tile_list_electrode_refit_kernel(
         nc.gpsimd.tensor_copy(w1_s[:, :, 0, :], w1_s_by_slot[:, :, 0, :])
         nc.gpsimd.tensor_copy(w1_s[:, :, 1:PACK, :], w1_s_by_slot[:, :, 1:PACK, :])
 
-        v_w = [placed("v_w0", [P, S], U32, 24), placed("v_w1", [P, S], U32, 32)]
+        v_w = [placed("v_w0", [P, S], U32, 133), placed("v_w1", [P, S], U32, 32)]
         nc.vector.tensor_copy(v_w[0][:], tab_w[0][:].bitcast(U32).indirect(idx[:]))
         for c0, w in PIECES:
             where = idx[:, c0 // PER_COL : (c0 + w) // PER_COL]
@@ -118,10 +118,10 @@ def tile_list_electrode_refit_kernel(
 
         h_head = placed("h_head", [P, HEAD], F32, 79)
         h_rest = placed("h_rest", [P, S - HEAD], F32, 80)
-        h_sb = {t: placed("h%d" % t, [P, S], F32, kb) for t, kb in ((1, 5.75), (2, 74), (3, 122))}
+        h_sb = {t: placed("h%d" % t, [P, S], F32, kb) for t, kb in ((1, 5.75), (2, 74), (3, 0))}
 
         h2_head = placed("h2_head", [P, HEAD], F32, 73)
-        h3_head = placed("h3_head", [P, BANK], F32, 3.75)
+        h3_head = placed("h3_head", [P, BANK], F32, 129.75)
 
         def make_h(t, c0, w, target):
             acc = psum.tile([P, w], F32, name="acc", tag="bank")
@@ -154,13 +154,13 @@ def tile_list_electrode_refit_kernel(
         gain_sb = placed("gain_sb", [P, 2, PACK], F32, 38.5)
         bias_sb = placed("bias_sb", [P, PACK], F32, 38.75)
         nc.sync.dma_start(gain_sb[:], gain.rearrange("(f p t) -> p f t", f=2, t=PACK))
-        load_weight(1, 22)
         load_page(2, 39)
         load_wg(2, 30)
         wb_w_raw = placed("wb_w_raw", [P, N], I32, 63.5)
         nc.sync.dma_start(wb_w_raw[:], wb_words[0].rearrange("p c i -> p (c i)").bitcast(I32))
         load_page(3, 55.5)
         load_wg(3, 34)
+        load_weight(1, 131.75)
         load_weight(2, 47)
         wb_s_raw = placed("wb_s_raw", [P, N], U8, 38)
         nc.gpsimd.memset(wb_s_raw[:].bitcast(I32), 0)
@@ -168,7 +168,7 @@ def tile_list_electrode_refit_kernel(
             nc.sync.dma_start(wb_s_raw[QUAD * q : QUAD * q + 4, :].bitcast(I32), wb_scales[0, 4 * q : 4 * q + 4, :].bitcast(I32))
         nc.sync.dma_start(bias_sb[:], bias.rearrange("(p t) -> p t", t=PACK))
 
-        w_s = [placed("w_s%d" % i, [P, N], U8, kb) for i, kb in enumerate((4, 4.5, 52.75))]
+        w_s = [placed("w_s%d" % i, [P, N], U8, kb) for i, kb in enumerate((130, 130.5, 52.75))]
         w_w, grouped = {}, {}
 
         def round_weight(i, tile):
@@ -213,12 +213,10 @@ def tile_list_electrode_refit_kernel(
             nc.vector.tensor_copy(x[:], page[t][:].indirect(idx3[:, c0 // PER_COL : (c0 + w) // PER_COL]))
             return x[:]
 
-        def features(t, x, kb_square, kb_sin, between=None):
+        def features(t, x, kb_square, kb_sin):
             square = feature(SQUARE, "square%d" % t, x, M, kb_square)
             apply_gain(nc.gpsimd, SQUARE, t, 0, M, square[:])
             sine = feature(SIN, "sine%d" % t, x, M, kb_sin)
-            if between is not None:
-                round_weight(*between)
             apply_gain(nc.scalar, SIN, t, 0, M, sine[:])
 
         cut = HEAD // PER_COL
@@ -226,7 +224,8 @@ def tile_list_electrode_refit_kernel(
         nc.vector.tensor_tensor(page[0][:].indirect(idx2[:, cut : S // PER_COL]), h_rest[:], wg[0][:, HEAD:S], ALU.mult)
         weigh(1, 66)
         round_weight(0, held("grouped0", [P, N * PACK], BF16))
-        features(0, read_page(0, 97), 15.75, 7.75, between=(1, placed("grouped1", [P, N * PACK], BF16, 97)))
+        features(0, read_page(0, 97), 15.75, 7.75)
+        round_weight(1, placed("grouped1", [P, N * PACK], BF16, 7.75))
         weighted[2] = placed("weighted2", [P, S], F32, 15.75)
         nc.gpsimd.tensor_tensor(weighted[2][:, 0:HEAD], h2_head[:], wg[2][:, 0:HEAD], ALU.mult)
         nc.gpsimd.tensor_tensor(weighted[2][:, HEAD:S], h_sb[2][:, HEAD:S], wg[2][:, HEAD:S], ALU.mult)
@@ -237,17 +236,17 @@ def tile_list_electrode_refit_kernel(
         nc.gpsimd.tensor_tensor(weighted[3][:, BANK:S], h_sb[3][:, BANK:S], wg[3][:, BANK:S], ALU.mult)
         scatter(1)
         scatter(2, 0, HEAD)
-        features(1, read_page(1, 70), 5.25, 9.25)
-        wb_s = placed("wb_s", [P, N], U8, 5.25)
+        features(1, read_page(1, 70), 131.25, 135.25)
+        wb_s = placed("wb_s", [P, N], U8, 131.25)
         nc.gpsimd.tensor_copy(wb_s[:].rearrange("p (t m) -> p t m", t=PACK), wb_s_raw[:].rearrange("p (m t) -> p t m", t=PACK))
-        round_weight(2, placed("grouped2", [P, N * PACK], BF16, 9.25))
+        round_weight(2, placed("grouped2", [P, N * PACK], BF16, 135.25))
         scatter(2, HEAD, S)
         scatter(LAST, 0, HEAD)
-        x = read_page(2, 0)
+        x = read_page(2, 126)
         quantise_weight(0, 107)
-        quantise_weight(1, 109)
         features(2, x, 47, 51)
         scatter(LAST, HEAD, S)
+        quantise_weight(1, 109)
 
         z_w = [held("z_w%d" % f, [P, M], U32) for f in range(2)]
         z_s = [held("z_s%d" % f, [P, M], U8) for f in range(2)]

@@ -156,11 +156,11 @@ def tile_list_electrode_refit_kernel(
         nc.sync.dma_start(gain_sb[:], gain.rearrange("(f p t) -> p f t", f=2, t=PACK))
         load_page(2, 39)
         load_wg(2, 30)
+        load_weight(1, 131.75)
         wb_w_raw = placed("wb_w_raw", [P, N], I32, 63.5)
         nc.sync.dma_start(wb_w_raw[:], wb_words[0].rearrange("p c i -> p (c i)").bitcast(I32))
         load_page(3, 55.5)
         load_wg(3, 34)
-        load_weight(1, 131.75)
         load_weight(2, 47)
         wb_s_raw = placed("wb_s_raw", [P, N], U8, 38)
         nc.gpsimd.memset(wb_s_raw[:].bitcast(I32), 0)
@@ -231,22 +231,25 @@ def tile_list_electrode_refit_kernel(
         nc.gpsimd.tensor_tensor(weighted[2][:, HEAD:S], h_sb[2][:, HEAD:S], wg[2][:, HEAD:S], ALU.mult)
         wb_w = placed("wb_w", [P, N], I32, 76)
         nc.gpsimd.tensor_copy(wb_w[:].rearrange("p (t m) -> p t m", t=PACK), wb_w_raw[:].rearrange("p (m t) -> p t m", t=PACK))
+        scatter(1)
+        scatter(2, 0, HEAD)
+        x = read_page(1, 70)
+        apply_gain(nc.gpsimd, SQUARE, 1, 0, BANK, feature(SQUARE, "square1_first", x[:, 0:BANK], BANK, 135.75)[:])
+        apply_gain(nc.scalar, SIN, 1, 0, M, feature(SIN, "sine1", x, M, 131.75)[:])
         weighted[3] = placed("weighted3", [P, S], F32, 30)
         nc.gpsimd.tensor_tensor(weighted[3][:, 0:BANK], h3_head[:], wg[3][:, 0:BANK], ALU.mult)
         nc.gpsimd.tensor_tensor(weighted[3][:, BANK:S], h_sb[3][:, BANK:S], wg[3][:, BANK:S], ALU.mult)
-        scatter(1)
-        scatter(2, 0, HEAD)
-        features(1, read_page(1, 70), 131.25, 135.25)
-        wb_s = placed("wb_s", [P, N], U8, 131.25)
-        nc.gpsimd.tensor_copy(wb_s[:].rearrange("p (t m) -> p t m", t=PACK), wb_s_raw[:].rearrange("p (m t) -> p t m", t=PACK))
-        round_weight(2, placed("grouped2", [P, N * PACK], BF16, 135.25))
+        apply_gain(nc.gpsimd, SQUARE, 1, BANK, M, feature(SQUARE, "square1_second", x[:, BANK:M], BANK, 131.25)[:])
+        round_weight(2, placed("grouped2", [P, N * PACK], BF16, 70))
         scatter(2, HEAD, S)
         scatter(LAST, 0, HEAD)
         x = read_page(2, 126)
         quantise_weight(0, 107)
-        features(2, x, 47, 51)
-        scatter(LAST, HEAD, S)
         quantise_weight(1, 109)
+        features(2, x, 47, 51)
+        wb_s = placed("wb_s", [P, N], U8, 47)
+        nc.gpsimd.tensor_copy(wb_s[:].rearrange("p (t m) -> p t m", t=PACK), wb_s_raw[:].rearrange("p (m t) -> p t m", t=PACK))
+        scatter(LAST, HEAD, S)
 
         z_w = [held("z_w%d" % f, [P, M], U32) for f in range(2)]
         z_s = [held("z_s%d" % f, [P, M], U8) for f in range(2)]

@@ -151,16 +151,22 @@ def tile_list_electrode_refit_kernel(
         load_wg(1, 17.75)
         load_weight(0, 9.75)
         load_page(1, 112)
-        gain_sb = placed("gain_sb", [P, 2, PACK], F32, 38.5)
+        gain_rows = gain.rearrange("(f p t) -> f p t", f=2, t=PACK)
+        gain_sin = placed("gain_sin", [P, PACK], F32, 38.5)
+        gain_first = placed("gain_first", [P, 1], F32, 38.625)
+        gain_rest = placed("gain_rest", [P, PACK - 1], F32, 38.6875)
         bias_sb = placed("bias_sb", [P, PACK], F32, 38.75)
-        nc.sync.dma_start(gain_sb[:], gain.rearrange("(f p t) -> p f t", f=2, t=PACK))
+        nc.sync.dma_start(gain_sin[:], gain_rows[SIN])
         load_page(2, 39)
         load_wg(2, 30)
+        with nc.allow_non_contiguous_dma(reason="one gain a partition"):
+            nc.sync.dma_start(gain_first[:], gain_rows[SQUARE][:, 0:1])
         load_weight(1, 131.75)
         wb_w_raw = placed("wb_w_raw", [P, N], I32, 63.5)
         nc.sync.dma_start(wb_w_raw[:], wb_words[0].rearrange("p c i -> p (c i)").bitcast(I32))
         load_page(3, 55.5)
         load_wg(3, 34)
+        nc.sync.dma_start(gain_rest[:], gain_rows[SQUARE][:, 1:PACK])
         load_weight(2, 47)
         wb_s_raw = placed("wb_s_raw", [P, N], U8, 38)
         nc.gpsimd.memset(wb_s_raw[:].bitcast(I32), 0)
@@ -189,10 +195,14 @@ def tile_list_electrode_refit_kernel(
 
         def apply_gain(eng, f, t, c0, c1, values):
             target = z_bf(f, c0, c1)[:, t : PACK * (c1 - c0) : PACK]
-            if eng is nc.scalar:
-                nc.scalar.activation(target, values, ACT.Copy, scale=gain_sb[:, f, t : t + 1])
+            if f == SIN:
+                factor = gain_sin[:, t : t + 1]
             else:
-                eng.tensor_scalar(target, values, gain_sb[:, f, t : t + 1], 0.0, ALU.mult, ALU.add)
+                factor = gain_first[:] if t == 0 else gain_rest[:, t - 1 : t]
+            if eng is nc.scalar:
+                nc.scalar.activation(target, values, ACT.Copy, scale=factor)
+            else:
+                eng.tensor_scalar(target, values, factor, 0.0, ALU.mult, ALU.add)
 
         def feature(f, name, x, w, kb):
             values = placed(name, [P, w], F32, kb)
@@ -213,41 +223,46 @@ def tile_list_electrode_refit_kernel(
             nc.vector.tensor_copy(x[:], page[t][:].indirect(idx3[:, c0 // PER_COL : (c0 + w) // PER_COL]))
             return x[:]
 
-        def features(t, x, kb_square, kb_sin):
-            square = feature(SQUARE, "square%d" % t, x, M, kb_square)
-            apply_gain(nc.gpsimd, SQUARE, t, 0, M, square[:])
-            sine = feature(SIN, "sine%d" % t, x, M, kb_sin)
-            apply_gain(nc.scalar, SIN, t, 0, M, sine[:])
-
         cut = HEAD // PER_COL
         nc.vector.tensor_tensor(page[0][:].indirect(idx2[:, 0:cut]), h_head[:], wg[0][:, 0:HEAD], ALU.mult)
         nc.vector.tensor_tensor(page[0][:].indirect(idx2[:, cut : S // PER_COL]), h_rest[:], wg[0][:, HEAD:S], ALU.mult)
         weigh(1, 66)
         round_weight(0, held("grouped0", [P, N * PACK], BF16))
-        features(0, read_page(0, 97), 15.75, 7.75)
-        round_weight(1, placed("grouped1", [P, N * PACK], BF16, 7.75))
-        weighted[2] = placed("weighted2", [P, S], F32, 15.75)
+        x = read_page(0, 97)
+        sine = feature(SIN, "sine0", x, M, 9.75)
+        square = feature(SQUARE, "square0", x, M, 13.75)
+        apply_gain(nc.gpsimd, SIN, 0, BANK, M, sine[:, BANK:M])
+        apply_gain(nc.scalar, SIN, 0, 0, BANK, sine[:, 0:BANK])
+        round_weight(1, placed("grouped1", [P, N * PACK], BF16, 97))
+        weighted[2] = placed("weighted2", [P, S], F32, 17.75)
         nc.gpsimd.tensor_tensor(weighted[2][:, 0:HEAD], h2_head[:], wg[2][:, 0:HEAD], ALU.mult)
         nc.gpsimd.tensor_tensor(weighted[2][:, HEAD:S], h_sb[2][:, HEAD:S], wg[2][:, HEAD:S], ALU.mult)
+        apply_gain(nc.gpsimd, SQUARE, 0, 0, M, square[:])
         wb_w = placed("wb_w", [P, N], I32, 76)
         nc.gpsimd.tensor_copy(wb_w[:].rearrange("p (t m) -> p t m", t=PACK), wb_w_raw[:].rearrange("p (m t) -> p t m", t=PACK))
         scatter(1)
         scatter(2, 0, HEAD)
         x = read_page(1, 70)
-        apply_gain(nc.gpsimd, SQUARE, 1, 0, BANK, feature(SQUARE, "square1_first", x[:, 0:BANK], BANK, 135.75)[:])
-        apply_gain(nc.scalar, SIN, 1, 0, M, feature(SIN, "sine1", x, M, 131.75)[:])
+        sine = feature(SIN, "sine1", x, M, 131.75)
+        square = feature(SQUARE, "square1", x, M, 135.75)
+        apply_gain(nc.scalar, SIN, 1, 0, M, sine[:])
         weighted[3] = placed("weighted3", [P, S], F32, 30)
         nc.gpsimd.tensor_tensor(weighted[3][:, 0:BANK], h3_head[:], wg[3][:, 0:BANK], ALU.mult)
         nc.gpsimd.tensor_tensor(weighted[3][:, BANK:S], h_sb[3][:, BANK:S], wg[3][:, BANK:S], ALU.mult)
-        apply_gain(nc.gpsimd, SQUARE, 1, BANK, M, feature(SQUARE, "square1_second", x[:, BANK:M], BANK, 131.25)[:])
+        apply_gain(nc.gpsimd, SQUARE, 1, 0, M, square[:])
         round_weight(2, placed("grouped2", [P, N * PACK], BF16, 70))
         scatter(2, HEAD, S)
         scatter(LAST, 0, HEAD)
         x = read_page(2, 126)
         quantise_weight(0, 107)
         quantise_weight(1, 109)
-        features(2, x, 47, 51)
-        wb_s = placed("wb_s", [P, N], U8, 47)
+        first = feature(SQUARE, "square2_first", x[:, 0:BANK], BANK, 47)
+        sine = feature(SIN, "sine2", x, M, 51)
+        second = feature(SQUARE, "square2_second", x[:, BANK:M], BANK, 49)
+        apply_gain(nc.gpsimd, SQUARE, 2, 0, BANK, first[:])
+        apply_gain(nc.scalar, SIN, 2, 0, M, sine[:])
+        apply_gain(nc.gpsimd, SQUARE, 2, BANK, M, second[:])
+        wb_s = placed("wb_s", [P, N], U8, 49)
         nc.gpsimd.tensor_copy(wb_s[:].rearrange("p (t m) -> p t m", t=PACK), wb_s_raw[:].rearrange("p (m t) -> p t m", t=PACK))
         scatter(LAST, HEAD, S)
 

@@ -53,7 +53,8 @@ def tile_list_electrode_refit_kernel(
         idx2 = lists.tile([P, S // PER_COL], U16, name="idx2")
         idx3 = lists.tile([P, M // PER_COL], U16, name="idx3")
 
-        tab_s = placed("tab_s", [P, T], U8, 83)
+        tab_w = [placed("tab_w%d" % a, [P, T], I32, (13.75, 116)[a]) for a in range(2)]
+        tab_s = placed("tab_s", [P, T], U8, 90)
         w1_s_raw = placed("w1_s_raw", [P, 2, H], U8, 95)
         v_s = placed("v_s", [P, 2, S], U8, 38)
         nc.gpsimd.memset(w1_s_raw[:].rearrange("p a c -> p (a c)").bitcast(I32), 0)
@@ -68,13 +69,12 @@ def tile_list_electrode_refit_kernel(
 
         nc.sync.dma_start(idx[:], offs)
         nc.sync.dma_start(tab_s[P - QUAD : P, :].bitcast(I32), tab_scales.rearrange("a q n -> q a n").bitcast(I32))
+        nc.sync.dma_start(tab_w[0][:], tab_words[0].rearrange("p t i -> p (t i)").bitcast(I32))
+        w1_w_raw = placed("w1_w_raw", [P, 2, 2 * H], U8, 105)
+        nc.sync.dma_start(w1_w_raw[:].bitcast(I32), w1_words.rearrange("a p c -> p a c").bitcast(I32))
         nc.sync.dma_start(idx2[:], offs2)
         nc.sync.dma_start(idx3[:], offs3)
-        w1_w_raw = placed("w1_w_raw", [P, 2, 2 * H], U8, 91)
-        nc.sync.dma_start(w1_w_raw[:].bitcast(I32), w1_words.rearrange("a p c -> p a c").bitcast(I32))
-        tab_w = [placed("tab_w%d" % a, [P, T], I32, (13.75, 116)[a]) for a in range(2)]
-        for a in range(2):
-            nc.sync.dma_start(tab_w[a][:], tab_words[a].rearrange("p t i -> p (t i)").bitcast(I32))
+        nc.sync.dma_start(tab_w[1][:], tab_words[1].rearrange("p t i -> p (t i)").bitcast(I32))
 
         page_rows = page0.rearrange("(p t) n -> t p n", t=PACK)
         wgs_rows = wgs.rearrange("(i t) j -> t i j", t=PACK)
@@ -101,10 +101,10 @@ def tile_list_electrode_refit_kernel(
             row = P - QUAD + 8 * q
             nc.sync.dma_start(v_s[QUAD * q : QUAD * q + 4, :, :].bitcast(I32), picked_s[row : row + 8, :].bitcast(I32))
         load_page(0, 83)
+        load_wg(0, 91, (0, HEAD, S))
 
         w1_w = placed("w1_w", [P, 2, PACK, 2 * P], U8, 47)
-        nc.vector.tensor_copy(w1_w[:].bitcast(U16), w1_w_raw[:].bitcast(U16).rearrange("p a (m t) -> p a t m", t=PACK))
-        load_wg(0, 91, (0, HEAD, S))
+        nc.scalar.copy(w1_w[:].bitcast(U16), w1_w_raw[:].bitcast(U16).rearrange("p a (m t) -> p a t m", t=PACK))
         w1_s = placed("w1_s", [P, 2, PACK, P], U8, 63)
         w1_s_by_slot = w1_s_raw[:].rearrange("p a (m t) -> p a t m", t=PACK)
         nc.gpsimd.tensor_copy(w1_s[:, :, 0, :], w1_s_by_slot[:, :, 0, :])

@@ -292,6 +292,10 @@ def tile_list_electrode_refit_kernel(
                     )
             return acc
 
+        shared_ab = {(0, 2): 2, (3, 0): 8}
+        rounded = {}
+        shared = {(2, 0): 4, (2, 2): 6, (3, 0): 10}
+
         def make_y(c):
             c0, w = STARTS[c], WIDTHS[c]
             y[c] = held("y%d" % c, [P, PACK, w], F32)
@@ -301,10 +305,19 @@ def tile_list_electrode_refit_kernel(
                 for slots in pair:
                     a_ps = product(c, slots, [(w_w[0], w_s[0], SIN)])
                     b_ps = product(c, slots, [(wb_w, wb_s, SQUARE)])
-                    a_sb = deep.tile([P, BANK], F32, name="a_sb", tag="a_sb")
+                    if (c, slots[0]) in shared:
+                        a_sb = placed("a_shared%d" % c, [P, BANK], F32, shared[c, slots[0]])
+                    else:
+                        a_sb = deep.tile([P, BANK], F32, name="a_sb", tag="a_sb")
                     nc.scalar.copy(a_sb[:], a_ps[:])
-                    ab.append(deep.tile([P, BANK], F32, name="ab", tag="ab"))
+                    if (c, slots[0]) in shared_ab:
+                        ab.append(placed("ab_shared%d" % c, [P, BANK], F32, shared_ab[c, slots[0]]))
+                    else:
+                        ab.append(deep.tile([P, BANK], F32, name="ab", tag="ab"))
                     nc.vector.tensor_tensor(ab[-1][:], b_ps[:], a_sb[:], ALU.mult)
+                if c == NCH - 1:
+                    round_y(1)
+                    make_planes(0)
                 for slots, prod in zip(pair, ab):
                     d_ps = product(c, slots, [(w_w[1], w_s[1], SIN), (w_w[2], w_s[2], SQUARE)])
                     for i, t in enumerate(slots):
@@ -314,29 +327,43 @@ def tile_list_electrode_refit_kernel(
             for t0 in range(0, PACK, step):
                 nc.sync.dma_start(y_rows[:, t0 : t0 + step, c0 : c0 + w], y[c][:, t0 : t0 + step, :])
 
-        def make_planes(c):
-            c0, w = STARTS[c], WIDTHS[c]
-            y_bf = held("y_bf%d" % c, [P, w * PACK], BF16)
+        def round_y(c):
+            w = WIDTHS[c]
+            y_bf = placed("y_bf%d" % c, [P, w * PACK], BF16, (4, 6)[c]) if c < 2 else held("y_bf%d" % c, [P, w * PACK], BF16)
             target = y_bf[:].rearrange("p (g i t) -> p g t i", i=4, t=PACK)
             source = y[c][:].rearrange("p t (g i) -> p g t i", i=4)
-            if c < NCH - 1:
+            if c == 0:
+                nc.gpsimd.tensor_scalar(
+                    y_bf[:].rearrange("p (m t) -> p m t", t=PACK), y[c][:].rearrange("p t m -> p m t"), 1.0, 0.0, ALU.mult, ALU.add
+                )
+            elif c < NCH - 1:
                 nc.scalar.copy(target, source)
             else:
                 nc.scalar.copy(target[:, :, 0:2, :], source[:, :, 0:2, :])
                 nc.vector.tensor_copy(target[:, :, 2:4, :], source[:, :, 2:4, :])
-            y_w = held("y_w%d" % c, [P, w], I32)
-            nc.vector.quantize_mx(y_w[:].bitcast(FP8X4), y_s[:, c0 : c0 + w], y_bf[:])
+            rounded[c] = y_bf
+
+        def make_planes(c):
+            c0, w = STARTS[c], WIDTHS[c]
+            y_w = placed("y_w%d" % c, [P, w], I32, (10, 8, 9)[c]) if c < NCH - 1 else held("y_w%d" % c, [P, w], I32)
+            nc.vector.quantize_mx(y_w[:].bitcast(FP8X4), y_s[:, c0 : c0 + w], rounded[c][:])
             nc.sync.dma_start(code_rows[:, PACK * c0 : PACK * (c0 + w)].bitcast(I32), y_w[:])
 
-        places = ((51, 52.5), (51.75, 53.25), (50.75, 54), (51.75, 54))
+        places = ((51, 52.5), (51.75, 53.25), (51.25, 54), (2, 3))
 
         def make_z(c):
             c0, w = STARTS[c], WIDTHS[c]
             x = x_last[:, c0 : c0 + w]
-            apply_gain(nc.gpsimd if c == 0 else nc.vector, SQUARE, LAST, c0, c0 + w, feature(SQUARE, "square_last%d" % c, x, w, places[c][0])[:])
-            apply_gain(nc.scalar, SIN, LAST, c0, c0 + w, feature(SIN, "sine_last%d" % c, x, w, places[c][1])[:])
-            quantise_z(SQUARE, c0, c0 + w)
-            quantise_z(SIN, c0, c0 + w)
+            if c < 2:
+                apply_gain((nc.gpsimd, nc.vector)[c], SQUARE, LAST, c0, c0 + w, feature(SQUARE, "square_last%d" % c, x, w, places[c][0])[:])
+                apply_gain(nc.scalar, SIN, LAST, c0, c0 + w, feature(SIN, "sine_last%d" % c, x, w, places[c][1])[:])
+            else:
+                sine = feature(SIN, "sine_last%d" % c, x, w, places[c][1])
+                square = feature(SQUARE, "square_last%d" % c, x, w, places[c][0])
+                apply_gain(nc.scalar, SIN, LAST, c0, c0 + w, sine[:])
+                apply_gain(nc.gpsimd, SQUARE, LAST, c0, c0 + w, square[:])
+            for f in (SQUARE, SIN) if c < 2 else (SIN, SQUARE):
+                quantise_z(f, c0, c0 + w)
 
         make_z(0)
         quantise_weight(2, 105)
@@ -345,9 +372,13 @@ def tile_list_electrode_refit_kernel(
             make_y(c)
             if c + 2 < NCH:
                 make_z(c + 2)
-            if c >= 1:
-                make_planes(c - 1)
-        make_planes(NCH - 1)
+            if c == 2:
+                round_y(0)
+        round_y(2)
+        make_planes(1)
+        round_y(3)
+        make_planes(2)
+        make_planes(3)
         for q in range(4):
             eng = nc.sync if q % 2 == 0 else nc.scalar
             eng.dma_start(out_2[0, 4 * q : 4 * q + 4, :].bitcast(I32), y_s[QUAD * q : QUAD * q + 4, :].bitcast(I32))

@@ -151,6 +151,9 @@ def tile_list_electrode_refit_kernel(
         load_wg(1, 17.75)
         load_weight(0, 9.75)
         load_page(1, 112)
+        wb_s_raw = w1_s_raw[:, 0, :]
+        for q in range(4):
+            nc.sync.dma_start(wb_s_raw[QUAD * q : QUAD * q + 4, :].bitcast(I32), wb_scales[0, 4 * q : 4 * q + 4, :].bitcast(I32))
         gain_rows = gain.rearrange("(f p t) -> f p t", f=2, t=PACK)
         gain_sin = placed("gain_sin", [P, PACK], F32, 38.5)
         gain_first = placed("gain_first", [P, 1], F32, 38.625)
@@ -168,10 +171,6 @@ def tile_list_electrode_refit_kernel(
         load_wg(3, 34)
         nc.sync.dma_start(gain_rest[:], gain_rows[SQUARE][:, 1:PACK])
         load_weight(2, 47)
-        wb_s_raw = placed("wb_s_raw", [P, N], U8, 38)
-        nc.gpsimd.memset(wb_s_raw[:].bitcast(I32), 0)
-        for q in range(4):
-            nc.sync.dma_start(wb_s_raw[QUAD * q : QUAD * q + 4, :].bitcast(I32), wb_scales[0, 4 * q : 4 * q + 4, :].bitcast(I32))
         nc.sync.dma_start(bias_sb[:], bias.rearrange("(p t) -> p t", t=PACK))
 
         w_s = [placed("w_s%d" % i, [P, N], U8, kb) for i, kb in enumerate((130, 130.5, 52.75))]
@@ -227,6 +226,8 @@ def tile_list_electrode_refit_kernel(
         nc.vector.tensor_tensor(page[0][:].indirect(idx2[:, 0:cut]), h_head[:], wg[0][:, 0:HEAD], ALU.mult)
         nc.vector.tensor_tensor(page[0][:].indirect(idx2[:, cut : S // PER_COL]), h_rest[:], wg[0][:, HEAD:S], ALU.mult)
         weigh(1, 66)
+        wb_s = placed("wb_s", [P, N], U8, 5.75)
+        nc.gpsimd.tensor_copy(wb_s[:].rearrange("p (t m) -> p t m", t=PACK), wb_s_raw.rearrange("p (m t) -> p t m", t=PACK))
         round_weight(0, held("grouped0", [P, N * PACK], BF16))
         x = read_page(0, 97)
         sine = feature(SIN, "sine0", x, M, 9.75)
@@ -262,8 +263,6 @@ def tile_list_electrode_refit_kernel(
         apply_gain(nc.gpsimd, SQUARE, 2, 0, BANK, first[:])
         apply_gain(nc.scalar, SIN, 2, 0, M, sine[:])
         apply_gain(nc.gpsimd, SQUARE, 2, BANK, M, second[:])
-        wb_s = placed("wb_s", [P, N], U8, 49)
-        nc.gpsimd.tensor_copy(wb_s[:].rearrange("p (t m) -> p t m", t=PACK), wb_s_raw[:].rearrange("p (m t) -> p t m", t=PACK))
         scatter(LAST, HEAD, S)
 
         z_w = [held("z_w%d" % f, [P, M], U32) for f in range(2)]
@@ -294,7 +293,7 @@ def tile_list_electrode_refit_kernel(
 
         shared_ab = {(0, 2): 2, (3, 0): 8}
         rounded = {}
-        shared = {(2, 0): 4, (2, 2): 6, (3, 0): 10}
+        shared = {(2, 0): 12, (2, 2): 14, (3, 0): 10}
 
         def make_y(c):
             c0, w = STARTS[c], WIDTHS[c]
@@ -302,8 +301,8 @@ def tile_list_electrode_refit_kernel(
             groups = [range(t0, t0 + BANK // w) for t0 in range(0, PACK, BANK // w)]
             for pair in (groups[i : i + 2] for i in range(0, len(groups), 2)):
                 ab = []
-                for slots in pair:
-                    a_ps = product(c, slots, [(w_w[0], w_s[0], SIN)])
+                early = [product(c, slots, [(w_w[0], w_s[0], SIN)]) for slots in pair]
+                for slots, a_ps in zip(pair, early):
                     b_ps = product(c, slots, [(wb_w, wb_s, SQUARE)])
                     if (c, slots[0]) in shared:
                         a_sb = placed("a_shared%d" % c, [P, BANK], F32, shared[c, slots[0]])
@@ -329,7 +328,7 @@ def tile_list_electrode_refit_kernel(
 
         def round_y(c):
             w = WIDTHS[c]
-            y_bf = placed("y_bf%d" % c, [P, w * PACK], BF16, (4, 6)[c]) if c < 2 else held("y_bf%d" % c, [P, w * PACK], BF16)
+            y_bf = placed("y_bf%d" % c, [P, w * PACK], BF16, (12, 14)[c]) if c < 2 else held("y_bf%d" % c, [P, w * PACK], BF16)
             target = y_bf[:].rearrange("p (g i t) -> p g t i", i=4, t=PACK)
             source = y[c][:].rearrange("p t (g i) -> p g t i", i=4)
             if c == 0:

@@ -256,7 +256,6 @@ def tile_list_electrode_refit_kernel(
         scatter(LAST, 0, HEAD)
         x = read_page(2, 126)
         quantise_weight(0, 107)
-        quantise_weight(1, 109)
         first = feature(SQUARE, "square2_first", x[:, 0:BANK], BANK, 47)
         sine = feature(SIN, "sine2", x, M, 51)
         second = feature(SQUARE, "square2_second", x[:, BANK:M], BANK, 49)
@@ -264,6 +263,7 @@ def tile_list_electrode_refit_kernel(
         apply_gain(nc.scalar, SIN, 2, 0, M, sine[:])
         apply_gain(nc.gpsimd, SQUARE, 2, BANK, M, second[:])
         scatter(LAST, HEAD, S)
+        quantise_weight(1, 109)
 
         z_w = [held("z_w%d" % f, [P, M], U32) for f in range(2)]
         z_s = [held("z_s%d" % f, [P, M], U8) for f in range(2)]

@@ -232,15 +232,14 @@ def tile_list_electrode_refit_kernel(
         x = read_page(0, 97)
         sine = feature(SIN, "sine0", x, M, 9.75)
         square = feature(SQUARE, "square0", x, M, 13.75)
-        apply_gain(nc.gpsimd, SIN, 0, BANK, M, sine[:, BANK:M])
-        apply_gain(nc.scalar, SIN, 0, 0, BANK, sine[:, 0:BANK])
-        round_weight(1, placed("grouped1", [P, N * PACK], BF16, 97))
+        apply_gain(nc.scalar, SIN, 0, 0, M, sine[:])
+        round_weight(1, placed("grouped1", [P, N * PACK], BF16, 9.75))
         weighted[2] = placed("weighted2", [P, S], F32, 17.75)
         nc.gpsimd.tensor_tensor(weighted[2][:, 0:HEAD], h2_head[:], wg[2][:, 0:HEAD], ALU.mult)
         nc.gpsimd.tensor_tensor(weighted[2][:, HEAD:S], h_sb[2][:, HEAD:S], wg[2][:, HEAD:S], ALU.mult)
         apply_gain(nc.gpsimd, SQUARE, 0, 0, M, square[:])
-        wb_w = placed("wb_w", [P, N], I32, 76)
-        nc.gpsimd.tensor_copy(wb_w[:].rearrange("p (t m) -> p t m", t=PACK), wb_w_raw[:].rearrange("p (m t) -> p t m", t=PACK))
+        wb_w = placed("wb_w", [P, N], U32, 76)
+        nc.scalar.copy(wb_w[:].rearrange("p (t m) -> p t m", t=PACK), wb_w_raw[:].bitcast(U32).rearrange("p (m t) -> p t m", t=PACK))
         scatter(1)
         scatter(2, 0, HEAD)
         x = read_page(1, 70)
@@ -256,6 +255,7 @@ def tile_list_electrode_refit_kernel(
         scatter(LAST, 0, HEAD)
         x = read_page(2, 126)
         quantise_weight(0, 107)
+        quantise_weight(1, 109)
         first = feature(SQUARE, "square2_first", x[:, 0:BANK], BANK, 47)
         sine = feature(SIN, "sine2", x, M, 51)
         second = feature(SQUARE, "square2_second", x[:, BANK:M], BANK, 49)
@@ -263,7 +263,6 @@ def tile_list_electrode_refit_kernel(
         apply_gain(nc.scalar, SIN, 2, 0, M, sine[:])
         apply_gain(nc.gpsimd, SQUARE, 2, BANK, M, second[:])
         scatter(LAST, HEAD, S)
-        quantise_weight(1, 109)
 
         z_w = [held("z_w%d" % f, [P, M], U32) for f in range(2)]
         z_s = [held("z_s%d" % f, [P, M], U8) for f in range(2)]
@@ -278,8 +277,7 @@ def tile_list_electrode_refit_kernel(
         def quantise_z(f, c0, c1):
             nc.vector.quantize_mx(z_w[f][:, c0:c1].bitcast(FP8X4), z_s[f][:, c0:c1], z_bf(f, c0, c1))
 
-        def product(c, slots, terms):
-            c0, w = STARTS[c], WIDTHS[c]
+        def product(slots, c0, w, terms):
             acc = psum.tile([P, BANK], F32, name="acc", tag="bank")
             for i, t in enumerate(slots):
                 cols = slice(P * t, P * (t + 1))
@@ -291,40 +289,51 @@ def tile_list_electrode_refit_kernel(
                     )
             return acc
 
-        shared_ab = {(0, 2): 2, (3, 0): 8}
+        shared_ab = {(0, 1): 2, (3, 0): 8}
         rounded = {}
-        shared = {(2, 0): 12, (2, 2): 14, (3, 0): 10}
+        shared = {(2, 0): 12, (2, 1): 14, (3, 0): 10}
 
         def make_y(c):
             c0, w = STARTS[c], WIDTHS[c]
             y[c] = held("y%d" % c, [P, PACK, w], F32)
-            groups = [range(t0, t0 + BANK // w) for t0 in range(0, PACK, BANK // w)]
-            for pair in (groups[i : i + 2] for i in range(0, len(groups), 2)):
-                ab = []
-                early = [product(c, slots, [(w_w[0], w_s[0], SIN)]) for slots in pair]
-                for slots, a_ps in zip(pair, early):
-                    b_ps = product(c, slots, [(wb_w, wb_s, SQUARE)])
-                    if (c, slots[0]) in shared:
-                        a_sb = placed("a_shared%d" % c, [P, BANK], F32, shared[c, slots[0]])
-                    else:
-                        a_sb = deep.tile([P, BANK], F32, name="a_sb", tag="a_sb")
-                    nc.scalar.copy(a_sb[:], a_ps[:])
-                    if (c, slots[0]) in shared_ab:
-                        ab.append(placed("ab_shared%d" % c, [P, BANK], F32, shared_ab[c, slots[0]]))
-                    else:
-                        ab.append(deep.tile([P, BANK], F32, name="ab", tag="ab"))
-                    nc.vector.tensor_tensor(ab[-1][:], b_ps[:], a_sb[:], ALU.mult)
+            if c < NCH - 1:
+                parts = [(range(2 * n, 2 * n + 2), 0, w) for n in range(2)]
+            else:
+                parts = [(range(PACK), n * w // 2, w // 2) for n in range(2)]
+                rounded[c] = held("y_bf%d" % c, [P, w * PACK], BF16)
+            early = [product(slots, c0 + b0, bw, [(w_w[0], w_s[0], SIN)]) for slots, b0, bw in parts]
+            ab = []
+            for n, (slots, b0, bw) in enumerate(parts):
+                b_ps = product(slots, c0 + b0, bw, [(wb_w, wb_s, SQUARE)])
+                if (c, n) in shared:
+                    a_sb = placed("a_shared%d_%d" % (c, n), [P, BANK], F32, shared[c, n])
+                else:
+                    a_sb = deep.tile([P, BANK], F32, name="a_sb", tag="a_sb")
+                nc.scalar.copy(a_sb[:], early[n][:])
+                if (c, n) in shared_ab:
+                    ab.append(placed("ab_shared%d" % c, [P, BANK], F32, shared_ab[c, n]))
+                else:
+                    ab.append(deep.tile([P, BANK], F32, name="ab", tag="ab"))
+                nc.vector.tensor_tensor(ab[-1][:], b_ps[:], a_sb[:], ALU.mult)
+            if c == NCH - 1:
+                round_y(1)
+                make_planes((0,), 10)
+                round_y(2)
+            for (slots, b0, bw), prod in zip(parts, ab):
+                d_ps = product(slots, c0 + b0, bw, [(w_w[1], w_s[1], SIN), (w_w[2], w_s[2], SQUARE)])
+                for i, t in enumerate(slots):
+                    cols = slice(i * bw, (i + 1) * bw)
+                    nc.vector.scalar_tensor_tensor(
+                        y[c][:, t, b0 : b0 + bw], d_ps[:, cols], bias_sb[:, t : t + 1], prod[:, cols], ALU.add, ALU.add
+                    )
                 if c == NCH - 1:
-                    round_y(1)
-                    make_planes(0)
-                for slots, prod in zip(pair, ab):
-                    d_ps = product(c, slots, [(w_w[1], w_s[1], SIN), (w_w[2], w_s[2], SQUARE)])
-                    for i, t in enumerate(slots):
-                        cols = slice(i * w, (i + 1) * w)
-                        nc.vector.scalar_tensor_tensor(y[c][:, t, :], d_ps[:, cols], bias_sb[:, t : t + 1], prod[:, cols], ALU.add, ALU.add)
-            step = PACK if c < NCH - 1 else 2
-            for t0 in range(0, PACK, step):
-                nc.sync.dma_start(y_rows[:, t0 : t0 + step, c0 : c0 + w], y[c][:, t0 : t0 + step, :])
+                    nc.sync.dma_start(y_rows[:, :, c0 + b0 : c0 + b0 + bw], y[c][:, :, b0 : b0 + bw])
+                    nc.scalar.copy(
+                        rounded[c][:, PACK * b0 : PACK * (b0 + bw)].rearrange("p (g i t) -> p g t i", i=4, t=PACK),
+                        y[c][:, :, b0 : b0 + bw].rearrange("p t (g i) -> p g t i", i=4),
+                    )
+            if c < NCH - 1:
+                nc.sync.dma_start(y_rows[:, :, c0 : c0 + w], y[c][:])
 
         def round_y(c):
             w = WIDTHS[c]
@@ -335,18 +344,17 @@ def tile_list_electrode_refit_kernel(
                 nc.gpsimd.tensor_scalar(
                     y_bf[:].rearrange("p (m t) -> p m t", t=PACK), y[c][:].rearrange("p t m -> p m t"), 1.0, 0.0, ALU.mult, ALU.add
                 )
-            elif c < NCH - 1:
-                nc.scalar.copy(target, source)
             else:
-                nc.scalar.copy(target[:, :, 0:2, :], source[:, :, 0:2, :])
-                nc.vector.tensor_copy(target[:, :, 2:4, :], source[:, :, 2:4, :])
+                nc.scalar.copy(target, source)
             rounded[c] = y_bf
 
-        def make_planes(c):
-            c0, w = STARTS[c], WIDTHS[c]
-            y_w = placed("y_w%d" % c, [P, w], I32, (10, 8, 9)[c]) if c < NCH - 1 else held("y_w%d" % c, [P, w], I32)
-            nc.vector.quantize_mx(y_w[:].bitcast(FP8X4), y_s[:, c0 : c0 + w], rounded[c][:])
-            nc.sync.dma_start(code_rows[:, PACK * c0 : PACK * (c0 + w)].bitcast(I32), y_w[:])
+        def make_planes(chunks, kb):
+            first, end = STARTS[chunks[0]], STARTS[chunks[-1]] + WIDTHS[chunks[-1]]
+            y_w = placed("y_w%d" % chunks[0], [P, end - first], I32, kb)
+            for c in chunks:
+                c0, c1 = STARTS[c], STARTS[c] + WIDTHS[c]
+                nc.vector.quantize_mx(y_w[:, c0 - first : c1 - first].bitcast(FP8X4), y_s[:, c0:c1], rounded[c][:])
+            nc.sync.dma_start(code_rows[:, PACK * first : PACK * end].bitcast(I32), y_w[:])
 
         places = ((51, 52.5), (51.75, 53.25), (51.25, 54), (2, 3))
 
@@ -373,11 +381,8 @@ def tile_list_electrode_refit_kernel(
                 make_z(c + 2)
             if c == 2:
                 round_y(0)
-        round_y(2)
-        make_planes(1)
-        round_y(3)
-        make_planes(2)
-        make_planes(3)
+        make_planes((1, 2), 8)
+        make_planes((3,), 16)
         for q in range(4):
             eng = nc.sync if q % 2 == 0 else nc.scalar
             eng.dma_start(out_2[0, 4 * q : 4 * q + 4, :].bitcast(I32), y_s[QUAD * q : QUAD * q + 4, :].bitcast(I32))

@@ -24,10 +24,10 @@ PER_COL = 16
 KB = 1024
 HEAD = 256
 PIECES = ((0, HEAD), (HEAD, BANK), (HEAD + BANK, S - HEAD - BANK))
-WIDTHS = (256, 256, 256, 256)
-STARTS = tuple(sum(WIDTHS[:c]) for c in range(len(WIDTHS)))
-NCH = len(WIDTHS)
+CHUNK = 256
+NCH = M // CHUNK
 LAST = PACK - 1
+EARLY = M - T2 // 16
 SIN, SQUARE = 0, 1
 
 
@@ -119,7 +119,6 @@ def tile_list_electrode_refit_kernel(
         h_head = placed("h_head", [P, HEAD], F32, 79)
         h_rest = placed("h_rest", [P, S - HEAD], F32, 80)
         h_sb = {t: placed("h%d" % t, [P, S], F32, kb) for t, kb in ((1, 5.75), (2, 74), (3, 0))}
-
         h2_head = placed("h2_head", [P, HEAD], F32, 73)
         h3_head = placed("h3_head", [P, BANK], F32, 129.75)
 
@@ -143,7 +142,7 @@ def tile_list_electrode_refit_kernel(
             for c0 in (0, BANK):
                 if (t, c0) == (2, 0):
                     make_h(t, c0, BANK, [(h2_head[:], slice(0, HEAD)), (h_sb[t][:, HEAD:BANK], slice(HEAD, BANK))])
-                elif (t, c0) == (3, 0):
+                elif (t, c0) == (LAST, 0):
                     make_h(t, c0, BANK, [(h3_head[:], slice(0, BANK))])
                 else:
                     make_h(t, c0, BANK, [(h_sb[t][:, c0 : c0 + BANK], slice(0, BANK))])
@@ -210,22 +209,23 @@ def tile_list_electrode_refit_kernel(
 
         weighted = {}
 
-        def weigh(t, kb):
+        def weigh(t, kb, parts):
             weighted[t] = placed("weighted%d" % t, [P, S], F32, kb)
-            nc.gpsimd.tensor_tensor(weighted[t][:], h_sb[t][:], wg[t][:], ALU.mult)
+            for c0, c1, values in parts:
+                nc.gpsimd.tensor_tensor(weighted[t][:, c0:c1], values, wg[t][:, c0:c1], ALU.mult)
 
-        def scatter(t, c0=0, c1=S):
+        def scatter(t, c0, c1):
             nc.vector.tensor_copy(page[t][:].indirect(idx2[:, c0 // PER_COL : c1 // PER_COL]), weighted[t][:, c0:c1])
 
-        def read_page(t, kb, c0=0, w=M):
-            x = placed("x%d_%d" % (t, c0), [P, w], F32, kb)
-            nc.vector.tensor_copy(x[:], page[t][:].indirect(idx3[:, c0 // PER_COL : (c0 + w) // PER_COL]))
+        def read_page(t, kb, c0=0, c1=M):
+            x = placed("x%d_%d" % (t, c0), [P, c1 - c0], F32, kb)
+            nc.vector.tensor_copy(x[:], page[t][:].indirect(idx3[:, c0 // PER_COL : c1 // PER_COL]))
             return x[:]
 
         cut = HEAD // PER_COL
         nc.vector.tensor_tensor(page[0][:].indirect(idx2[:, 0:cut]), h_head[:], wg[0][:, 0:HEAD], ALU.mult)
         nc.vector.tensor_tensor(page[0][:].indirect(idx2[:, cut : S // PER_COL]), h_rest[:], wg[0][:, HEAD:S], ALU.mult)
-        weigh(1, 66)
+        weigh(1, 66, [(0, S, h_sb[1][:])])
         wb_s = placed("wb_s", [P, N], U8, 5.75)
         nc.gpsimd.tensor_copy(wb_s[:].rearrange("p (t m) -> p t m", t=PACK), wb_s_raw.rearrange("p (m t) -> p t m", t=PACK))
         round_weight(0, held("grouped0", [P, N * PACK], BF16))
@@ -234,45 +234,45 @@ def tile_list_electrode_refit_kernel(
         square = feature(SQUARE, "square0", x, M, 13.75)
         apply_gain(nc.scalar, SIN, 0, 0, M, sine[:])
         round_weight(1, placed("grouped1", [P, N * PACK], BF16, 9.75))
-        weighted[2] = placed("weighted2", [P, S], F32, 17.75)
-        nc.gpsimd.tensor_tensor(weighted[2][:, 0:HEAD], h2_head[:], wg[2][:, 0:HEAD], ALU.mult)
-        nc.gpsimd.tensor_tensor(weighted[2][:, HEAD:S], h_sb[2][:, HEAD:S], wg[2][:, HEAD:S], ALU.mult)
+        weigh(2, 17.75, [(0, HEAD, h2_head[:]), (HEAD, S, h_sb[2][:, HEAD:S])])
         apply_gain(nc.gpsimd, SQUARE, 0, 0, M, square[:])
         wb_w = placed("wb_w", [P, N], U32, 76)
         nc.scalar.copy(wb_w[:].rearrange("p (t m) -> p t m", t=PACK), wb_w_raw[:].bitcast(U32).rearrange("p (m t) -> p t m", t=PACK))
-        scatter(1)
+        scatter(1, 0, S)
         scatter(2, 0, HEAD)
         x = read_page(1, 70)
         sine = feature(SIN, "sine1", x, M, 131.75)
         square = feature(SQUARE, "square1", x, M, 135.75)
         apply_gain(nc.scalar, SIN, 1, 0, M, sine[:])
-        weighted[3] = placed("weighted3", [P, S], F32, 30)
-        nc.gpsimd.tensor_tensor(weighted[3][:, 0:BANK], h3_head[:], wg[3][:, 0:BANK], ALU.mult)
-        nc.gpsimd.tensor_tensor(weighted[3][:, BANK:S], h_sb[3][:, BANK:S], wg[3][:, BANK:S], ALU.mult)
+        weigh(LAST, 30, [(0, BANK, h3_head[:]), (BANK, S, h_sb[LAST][:, BANK:S])])
         apply_gain(nc.gpsimd, SQUARE, 1, 0, M, square[:])
         round_weight(2, placed("grouped2", [P, N * PACK], BF16, 70))
         scatter(2, HEAD, S)
         scatter(LAST, 0, HEAD)
-        x = read_page(2, 126)
+        x = read_page(2, 126.5, 0, EARLY)
         quantise_weight(0, 107)
         quantise_weight(1, 109)
         first = feature(SQUARE, "square2_first", x[:, 0:BANK], BANK, 47)
-        sine = feature(SIN, "sine2", x, M, 51)
-        second = feature(SQUARE, "square2_second", x[:, BANK:M], BANK, 49)
+        sine = feature(SIN, "sine2", x, EARLY, 51)
+        second = feature(SQUARE, "square2_second", x[:, BANK:EARLY], EARLY - BANK, 49)
         apply_gain(nc.gpsimd, SQUARE, 2, 0, BANK, first[:])
-        apply_gain(nc.scalar, SIN, 2, 0, M, sine[:])
-        apply_gain(nc.gpsimd, SQUARE, 2, BANK, M, second[:])
+        apply_gain(nc.scalar, SIN, 2, 0, EARLY, sine[:])
+        apply_gain(nc.gpsimd, SQUARE, 2, BANK, EARLY, second[:])
         scatter(LAST, HEAD, S)
+        x = read_page(2, 2, EARLY, M)
+        square = feature(SQUARE, "square2_late", x, M - EARLY, 54)
+        late_sine = feature(SIN, "sine2_late", x, M - EARLY, 53.5)
+        apply_gain(nc.gpsimd, SQUARE, 2, EARLY, M, square[:])
 
         z_w = [held("z_w%d" % f, [P, M], U32) for f in range(2)]
         z_s = [held("z_s%d" % f, [P, M], U8) for f in range(2)]
         x_last = placed("x_last", [P, M], F32, 101)
-        for c0, c1 in ((0, STARTS[1]), (STARTS[1], M)):
+        for c0, c1 in ((0, CHUNK), (CHUNK, M)):
             nc.vector.tensor_copy(x_last[:, c0:c1], page[LAST][:].indirect(idx3[:, c0 // PER_COL : c1 // PER_COL]))
         y_s = held("y_s", [P, M], U8)
         y_rows = out_0.rearrange("(p t) m -> p t m", t=PACK)
         code_rows = out_1[0].rearrange("p m t -> p (m t)")
-        y = {}
+        y, rounded = {}, {}
 
         def quantise_z(f, c0, c1):
             nc.vector.quantize_mx(z_w[f][:, c0:c1].bitcast(FP8X4), z_s[f][:, c0:c1], z_bf(f, c0, c1))
@@ -289,35 +289,34 @@ def tile_list_electrode_refit_kernel(
                     )
             return acc
 
-        shared_ab = {(0, 1): 2, (3, 0): 8}
-        rounded = {}
-        shared = {(2, 0): 12, (2, 1): 14, (3, 0): 10}
+        a_place = {(2, 0): 12, (2, 1): 14, (3, 0): 10}
+        ab_place = {(0, 1): 2, (3, 0): 8}
 
         def make_y(c):
-            c0, w = STARTS[c], WIDTHS[c]
+            c0, w = c * CHUNK, CHUNK
             y[c] = held("y%d" % c, [P, PACK, w], F32)
             if c < NCH - 1:
                 parts = [(range(2 * n, 2 * n + 2), 0, w) for n in range(2)]
             else:
                 parts = [(range(PACK), n * w // 2, w // 2) for n in range(2)]
                 rounded[c] = held("y_bf%d" % c, [P, w * PACK], BF16)
-            early = [product(slots, c0 + b0, bw, [(w_w[0], w_s[0], SIN)]) for slots, b0, bw in parts]
+            a_ps = [product(slots, c0 + b0, bw, [(w_w[0], w_s[0], SIN)]) for slots, b0, bw in parts]
             ab = []
             for n, (slots, b0, bw) in enumerate(parts):
                 b_ps = product(slots, c0 + b0, bw, [(wb_w, wb_s, SQUARE)])
-                if (c, n) in shared:
-                    a_sb = placed("a_shared%d_%d" % (c, n), [P, BANK], F32, shared[c, n])
+                if (c, n) in a_place:
+                    a_sb = placed("a_sb%d_%d" % (c, n), [P, BANK], F32, a_place[c, n])
                 else:
                     a_sb = deep.tile([P, BANK], F32, name="a_sb", tag="a_sb")
-                nc.scalar.copy(a_sb[:], early[n][:])
-                if (c, n) in shared_ab:
-                    ab.append(placed("ab_shared%d" % c, [P, BANK], F32, shared_ab[c, n]))
+                nc.scalar.copy(a_sb[:], a_ps[n][:])
+                if (c, n) in ab_place:
+                    ab.append(placed("ab%d" % c, [P, BANK], F32, ab_place[c, n]))
                 else:
                     ab.append(deep.tile([P, BANK], F32, name="ab", tag="ab"))
                 nc.vector.tensor_tensor(ab[-1][:], b_ps[:], a_sb[:], ALU.mult)
             if c == NCH - 1:
                 round_y(1)
-                make_planes((0,), 10)
+                make_planes((0,), a_place[c, 0])
                 round_y(2)
             for (slots, b0, bw), prod in zip(parts, ab):
                 d_ps = product(slots, c0 + b0, bw, [(w_w[1], w_s[1], SIN), (w_w[2], w_s[2], SQUARE)])
@@ -336,39 +335,47 @@ def tile_list_electrode_refit_kernel(
                 nc.sync.dma_start(y_rows[:, :, c0 : c0 + w], y[c][:])
 
         def round_y(c):
-            w = WIDTHS[c]
-            y_bf = placed("y_bf%d" % c, [P, w * PACK], BF16, (12, 14)[c]) if c < 2 else held("y_bf%d" % c, [P, w * PACK], BF16)
-            target = y_bf[:].rearrange("p (g i t) -> p g t i", i=4, t=PACK)
-            source = y[c][:].rearrange("p t (g i) -> p g t i", i=4)
+            shape = [P, CHUNK * PACK]
+            y_bf = placed("y_bf%d" % c, shape, BF16, a_place[2, c]) if c < 2 else held("y_bf%d" % c, shape, BF16)
             if c == 0:
                 nc.gpsimd.tensor_scalar(
                     y_bf[:].rearrange("p (m t) -> p m t", t=PACK), y[c][:].rearrange("p t m -> p m t"), 1.0, 0.0, ALU.mult, ALU.add
                 )
             else:
-                nc.scalar.copy(target, source)
+                nc.scalar.copy(
+                    y_bf[:].rearrange("p (g i t) -> p g t i", i=4, t=PACK), y[c][:].rearrange("p t (g i) -> p g t i", i=4)
+                )
             rounded[c] = y_bf
 
         def make_planes(chunks, kb):
-            first, end = STARTS[chunks[0]], STARTS[chunks[-1]] + WIDTHS[chunks[-1]]
-            y_w = placed("y_w%d" % chunks[0], [P, end - first], I32, kb)
+            begin, end = chunks[0] * CHUNK, (chunks[-1] + 1) * CHUNK
+            y_w = placed("y_w%d" % chunks[0], [P, end - begin], I32, kb)
             for c in chunks:
-                c0, c1 = STARTS[c], STARTS[c] + WIDTHS[c]
-                nc.vector.quantize_mx(y_w[:, c0 - first : c1 - first].bitcast(FP8X4), y_s[:, c0:c1], rounded[c][:])
-            nc.sync.dma_start(code_rows[:, PACK * first : PACK * end].bitcast(I32), y_w[:])
+                w = CHUNK if c < NCH - 1 else CHUNK // 2
+                for b0 in range(0, CHUNK, w):
+                    c0, c1 = c * CHUNK + b0, c * CHUNK + b0 + w
+                    nc.vector.quantize_mx(
+                        y_w[:, c0 - begin : c1 - begin].bitcast(FP8X4), y_s[:, c0:c1], rounded[c][:, PACK * b0 : PACK * (b0 + w)]
+                    )
+            nc.sync.dma_start(code_rows[:, PACK * begin : PACK * end].bitcast(I32), y_w[:])
 
-        places = ((51, 52.5), (51.75, 53.25), (51.25, 54), (2, 3))
+        places = ((51, 52.5), (51.75, 53.25), (51.25, 54), (ab_place[0, 1], ab_place[0, 1] + 1))
 
         def make_z(c):
-            c0, w = STARTS[c], WIDTHS[c]
+            c0, w = c * CHUNK, CHUNK
             x = x_last[:, c0 : c0 + w]
             if c < 2:
-                apply_gain((nc.gpsimd, nc.vector)[c], SQUARE, LAST, c0, c0 + w, feature(SQUARE, "square_last%d" % c, x, w, places[c][0])[:])
-                apply_gain(nc.scalar, SIN, LAST, c0, c0 + w, feature(SIN, "sine_last%d" % c, x, w, places[c][1])[:])
+                squares = feature(SQUARE, "square_last%d" % c, x, w, places[c][0])
+                apply_gain((nc.gpsimd, nc.vector)[c], SQUARE, LAST, c0, c0 + w, squares[:])
+                sines = feature(SIN, "sine_last%d" % c, x, w, places[c][1])
+                if c == 0:
+                    apply_gain(nc.scalar, SIN, 2, EARLY, M, late_sine[:])
+                apply_gain(nc.scalar, SIN, LAST, c0, c0 + w, sines[:])
             else:
-                sine = feature(SIN, "sine_last%d" % c, x, w, places[c][1])
-                square = feature(SQUARE, "square_last%d" % c, x, w, places[c][0])
-                apply_gain(nc.scalar, SIN, LAST, c0, c0 + w, sine[:])
-                apply_gain(nc.gpsimd, SQUARE, LAST, c0, c0 + w, square[:])
+                sines = feature(SIN, "sine_last%d" % c, x, w, places[c][1])
+                squares = feature(SQUARE, "square_last%d" % c, x, w, places[c][0])
+                apply_gain(nc.scalar, SIN, LAST, c0, c0 + w, sines[:])
+                apply_gain(nc.gpsimd, SQUARE, LAST, c0, c0 + w, squares[:])
             for f in (SQUARE, SIN) if c < 2 else (SIN, SQUARE):
                 quantise_z(f, c0, c0 + w)
 
@@ -379,10 +386,10 @@ def tile_list_electrode_refit_kernel(
             make_y(c)
             if c + 2 < NCH:
                 make_z(c + 2)
-            if c == 2:
+            if c == NCH - 2:
                 round_y(0)
-        make_planes((1, 2), 8)
-        make_planes((3,), 16)
+        make_planes((1, 2), ab_place[NCH - 1, 0])
+        make_planes((NCH - 1,), 16)
         for q in range(4):
             eng = nc.sync if q % 2 == 0 else nc.scalar
             eng.dma_start(out_2[0, 4 * q : 4 * q + 4, :].bitcast(I32), y_s[QUAD * q : QUAD * q + 4, :].bitcast(I32))

@@ -85,11 +85,13 @@ def tile_list_electrode_refit_kernel(
             page[t] = placed("page%d" % t, [P, T2], F32, kb)
             nc.sync.dma_start(page[t][:], page_rows[t])
 
-        def load_wg(t, kb, cuts=(0, S)):
+        def load_wg_part(t, quadrants, c0, c1):
+            for q in quadrants:
+                nc.sync.dma_start(wg[t][QUAD * q : QUAD * (q + 1), c0:c1], wgs_rows[t][:, c0:c1])
+
+        def load_wg(t, kb):
             wg[t] = placed("wg%d" % t, [P, S], F32, kb)
-            for c0, c1 in zip(cuts, cuts[1:]):
-                for q in (0, 2, 1, 3):
-                    nc.sync.dma_start(wg[t][QUAD * q : QUAD * (q + 1), c0:c1], wgs_rows[t][:, c0:c1])
+            load_wg_part(t, (0, 2, 1, 3), 0, S)
 
         def load_weight(i, kb):
             w_raw[i] = placed("w_raw%d" % i, [P, PACK, N], F32, kb)
@@ -100,8 +102,11 @@ def tile_list_electrode_refit_kernel(
         for q in range(4):
             row = P - QUAD + 8 * q
             nc.sync.dma_start(v_s[QUAD * q : QUAD * q + 4, :, :].bitcast(I32), picked_s[row : row + 8, :].bitcast(I32))
+        wg[0] = placed("wg0", [P, S], F32, 91)
+        load_wg_part(0, (0,), 0, HEAD)
         load_page(0, 83)
-        load_wg(0, 91, (0, HEAD, S))
+        load_wg_part(0, (2, 1, 3), 0, HEAD)
+        load_wg_part(0, (0, 2, 1, 3), HEAD, S)
 
         w1_w = placed("w1_w", [P, 2, PACK, 2 * P], U8, 47)
         nc.scalar.copy(w1_w[:].bitcast(U16), w1_w_raw[:].bitcast(U16).rearrange("p a (m t) -> p a t m", t=PACK))

@@ -40,7 +40,6 @@ def tile_list_electrode_refit_kernel(
         lists = ctx.enter_context(tc.tile_pool(name="lists", bufs=1))
         arena = ctx.enter_context(tc.tile_pool(name="arena", bufs=1))
         keep = ctx.enter_context(tc.tile_pool(name="keep", bufs=1))
-        deep = ctx.enter_context(tc.tile_pool(name="deep", bufs=4))
         psum = ctx.enter_context(tc.psum_pool(name="psum", bufs=8))
 
         def held(name, shape, dtype):
@@ -125,7 +124,6 @@ def tile_list_electrode_refit_kernel(
         h_rest = placed("h_rest", [P, S - HEAD], F32, 80)
         h_sb = {t: placed("h%d" % t, [P, S], F32, kb) for t, kb in ((1, 5.75), (2, 74), (3, 0))}
         h2_head = placed("h2_head", [P, HEAD], F32, 73)
-        h3_head = placed("h3_head", [P, BANK], F32, 129.75)
 
         def make_h(t, c0, w, target):
             acc = psum.tile([P, w], F32, name="acc", tag="bank")
@@ -147,8 +145,6 @@ def tile_list_electrode_refit_kernel(
             for c0 in (0, BANK):
                 if (t, c0) == (2, 0):
                     make_h(t, c0, BANK, [(h2_head[:], slice(0, HEAD)), (h_sb[t][:, HEAD:BANK], slice(HEAD, BANK))])
-                elif (t, c0) == (LAST, 0):
-                    make_h(t, c0, BANK, [(h3_head[:], slice(0, BANK))])
                 else:
                     make_h(t, c0, BANK, [(h_sb[t][:, c0 : c0 + BANK], slice(0, BANK))])
 
@@ -177,7 +173,7 @@ def tile_list_electrode_refit_kernel(
         load_weight(2, 47)
         nc.sync.dma_start(bias_sb[:], bias.rearrange("(p t) -> p t", t=PACK))
 
-        w_s = [placed("w_s%d" % i, [P, N], U8, kb) for i, kb in enumerate((130, 130.5, 52.75))]
+        w_s = [placed("w_s%d" % i, [P, N], U8, kb) for i, kb in enumerate((130, 50.875, 51.375))]
         w_w, grouped = {}, {}
 
         def round_weight(i, tile):
@@ -245,104 +241,109 @@ def tile_list_electrode_refit_kernel(
         nc.scalar.copy(wb_w[:].rearrange("p (t m) -> p t m", t=PACK), wb_w_raw[:].bitcast(U32).rearrange("p (m t) -> p t m", t=PACK))
         scatter(1, 0, S)
         scatter(2, 0, HEAD)
-        x = read_page(1, 70)
-        sine = feature(SIN, "sine1", x, M, 131.75)
-        square = feature(SQUARE, "square1", x, M, 135.75)
-        apply_gain(nc.scalar, SIN, 1, 0, M, sine[:])
-        weigh(LAST, 30, [(0, BANK, h3_head[:]), (BANK, S, h_sb[LAST][:, BANK:S])])
-        apply_gain(nc.gpsimd, SQUARE, 1, 0, M, square[:])
+        x = read_page(1, 70.5, 0, EARLY)
+        sine = feature(SIN, "sine1", x, EARLY, 131.75)
+        square = feature(SQUARE, "square1", x, EARLY, 135.75)
+        apply_gain(nc.scalar, SIN, 1, 0, EARLY, sine[:])
+        weigh(LAST, 30, [(0, S, h_sb[LAST][:])])
+        apply_gain(nc.gpsimd, SQUARE, 1, 0, EARLY, square[:])
         round_weight(2, placed("grouped2", [P, N * PACK], BF16, 70))
         scatter(2, HEAD, S)
-        scatter(LAST, 0, HEAD)
+        x = read_page(1, 75, EARLY, M)
+        square = feature(SQUARE, "square1_late", x, M - EARLY, 50.5)
+        late_sine = feature(SIN, "sine1_late", x, M - EARLY, 54.5)
+        apply_gain(nc.gpsimd, SQUARE, 1, EARLY, M, square[:])
         x = read_page(2, 126.5, 0, EARLY)
-        quantise_weight(0, 107)
-        quantise_weight(1, 109)
         first = feature(SQUARE, "square2_first", x[:, 0:BANK], BANK, 47)
+        apply_gain(nc.scalar, SIN, 1, EARLY, M, late_sine[:])
         sine = feature(SIN, "sine2", x, EARLY, 51)
         second = feature(SQUARE, "square2_second", x[:, BANK:EARLY], EARLY - BANK, 49)
         apply_gain(nc.gpsimd, SQUARE, 2, 0, BANK, first[:])
         apply_gain(nc.scalar, SIN, 2, 0, EARLY, sine[:])
         apply_gain(nc.gpsimd, SQUARE, 2, BANK, EARLY, second[:])
-        scatter(LAST, HEAD, S)
+        scatter(LAST, 0, S)
         x = read_page(2, 2, EARLY, M)
-        square = feature(SQUARE, "square2_late", x, M - EARLY, 54)
+        square = feature(SQUARE, "square2_late", x, M - EARLY, 50.75)
         late_sine = feature(SIN, "sine2_late", x, M - EARLY, 53.5)
         apply_gain(nc.gpsimd, SQUARE, 2, EARLY, M, square[:])
 
+        x_first = read_page(LAST, 101, 0, CHUNK)
+        x_second = read_page(LAST, 102, CHUNK, 2 * CHUNK)
+        x_rest = read_page(LAST, 103, 2 * CHUNK, M)
         z_w = [held("z_w%d" % f, [P, M], U32) for f in range(2)]
-        z_s = [held("z_s%d" % f, [P, M], U8) for f in range(2)]
-        x_last = placed("x_last", [P, M], F32, 101)
-        for c0, c1 in ((0, CHUNK), (CHUNK, M)):
-            nc.vector.tensor_copy(x_last[:, c0:c1], page[LAST][:].indirect(idx3[:, c0 // PER_COL : c1 // PER_COL]))
+        z_s = {}
         y_s = held("y_s", [P, M], U8)
         y_rows = out_0.rearrange("(p t) m -> p t m", t=PACK)
         code_rows = out_1[0].rearrange("p m t -> p (m t)")
-        y, rounded = {}, {}
+        y, rounded, banks, a_sb, ab = {}, {}, {}, {}, {}
 
-        def quantise_z(f, c0, c1):
-            nc.vector.quantize_mx(z_w[f][:, c0:c1].bitcast(FP8X4), z_s[f][:, c0:c1], z_bf(f, c0, c1))
+        a_place = {(0, 0): 84, (0, 1): 86, (1, 0): 88, (1, 1): 112, (2, 0): 12, (2, 1): 14, (3, 0): 10, (3, 1): 114}
+        ab_place = {(0, 0): 116, (0, 1): 118, (1, 0): 18, (1, 1): 20, (2, 0): 24, (2, 1): 26, (3, 0): 8, (3, 1): 28}
+        scale_place = {(SQUARE, 0): 51.875, (SIN, 2): ab_place[0, 0], (SIN, 3): ab_place[1, 0]}
 
-        def product(slots, c0, w, terms):
+        def quantise_z(f, c):
+            name, c0 = "z_s%d_%d" % (f, c), c * CHUNK
+            if (f, c) in scale_place:
+                z_s[f, c] = placed(name, [P, CHUNK], U8, scale_place[f, c])
+            else:
+                z_s[f, c] = held(name, [P, CHUNK], U8)
+            nc.vector.quantize_mx(z_w[f][:, c0 : c0 + CHUNK].bitcast(FP8X4), z_s[f, c][:], z_bf(f, c0, c0 + CHUNK))
+
+        def part(c, n):
+            if c < NCH - 1:
+                return range(2 * n, 2 * n + 2), 0, CHUNK
+            return range(PACK), n * CHUNK // 2, CHUNK // 2
+
+        def product(kind, c, n):
+            terms = {
+                "A": lambda: [(w_w[0], w_s[0], SIN)],
+                "B": lambda: [(wb_w, wb_s, SQUARE)],
+                "D": lambda: [(w_w[1], w_s[1], SIN), (w_w[2], w_s[2], SQUARE)],
+            }[kind]()
+            slots, b0, w = part(c, n)
             acc = psum.tile([P, BANK], F32, name="acc", tag="bank")
             for i, t in enumerate(slots):
                 cols = slice(P * t, P * (t + 1))
-                for n, (words, scales, f) in enumerate(terms):
+                for k, (words, scales, f) in enumerate(terms):
                     nc.tensor.matmul_mx(
                         acc[:, i * w : (i + 1) * w], lhsT=words[:, cols].bitcast(FP8X4), lhsT_scale=scales[:, cols],
-                        rhs=z_w[f][:, c0 : c0 + w].bitcast(FP8X4), rhs_scale=z_s[f][:, c0 : c0 + w],
-                        start=(n == 0), stop=(n == len(terms) - 1),
+                        rhs=z_w[f][:, c * CHUNK + b0 : c * CHUNK + b0 + w].bitcast(FP8X4), rhs_scale=z_s[f, c][:, b0 : b0 + w],
+                        start=(k == 0), stop=(k == len(terms) - 1),
                     )
-            return acc
+            banks[kind, c, n] = acc
 
-        a_place = {(2, 0): 12, (2, 1): 14, (3, 0): 10}
-        ab_place = {(0, 1): 2, (3, 0): 8}
+        def copy_a(c, n):
+            a_sb[c, n] = placed("a_sb%d_%d" % (c, n), [P, BANK], F32, a_place[c, n])
+            nc.scalar.copy(a_sb[c, n][:], banks["A", c, n][:])
 
-        def make_y(c):
-            c0, w = c * CHUNK, CHUNK
-            y[c] = held("y%d" % c, [P, PACK, w], F32)
-            if c < NCH - 1:
-                parts = [(range(2 * n, 2 * n + 2), 0, w) for n in range(2)]
-            else:
-                parts = [(range(PACK), n * w // 2, w // 2) for n in range(2)]
-                rounded[c] = held("y_bf%d" % c, [P, w * PACK], BF16)
-            a_ps = [product(slots, c0 + b0, bw, [(w_w[0], w_s[0], SIN)]) for slots, b0, bw in parts]
-            ab = []
-            for n, (slots, b0, bw) in enumerate(parts):
-                b_ps = product(slots, c0 + b0, bw, [(wb_w, wb_s, SQUARE)])
-                if (c, n) in a_place:
-                    a_sb = placed("a_sb%d_%d" % (c, n), [P, BANK], F32, a_place[c, n])
-                else:
-                    a_sb = deep.tile([P, BANK], F32, name="a_sb", tag="a_sb")
-                nc.scalar.copy(a_sb[:], a_ps[n][:])
-                if (c, n) in ab_place:
-                    ab.append(placed("ab%d" % c, [P, BANK], F32, ab_place[c, n]))
-                else:
-                    ab.append(deep.tile([P, BANK], F32, name="ab", tag="ab"))
-                nc.vector.tensor_tensor(ab[-1][:], b_ps[:], a_sb[:], ALU.mult)
-            if c == NCH - 1:
-                round_y(1)
-                make_planes((0,), a_place[c, 0])
-                round_y(2)
-            for (slots, b0, bw), prod in zip(parts, ab):
-                d_ps = product(slots, c0 + b0, bw, [(w_w[1], w_s[1], SIN), (w_w[2], w_s[2], SQUARE)])
-                for i, t in enumerate(slots):
-                    cols = slice(i * bw, (i + 1) * bw)
-                    nc.vector.scalar_tensor_tensor(
-                        y[c][:, t, b0 : b0 + bw], d_ps[:, cols], bias_sb[:, t : t + 1], prod[:, cols], ALU.add, ALU.add
-                    )
+        def multiply(c, n):
+            ab[c, n] = placed("ab%d_%d" % (c, n), [P, BANK], F32, ab_place[c, n])
+            nc.vector.tensor_tensor(ab[c, n][:], banks["B", c, n][:], a_sb[c, n][:], ALU.mult)
+
+        def add_up(c, n):
+            slots, b0, w = part(c, n)
+            c0 = c * CHUNK
+            if n == 0:
+                y[c] = held("y%d" % c, [P, PACK, CHUNK], F32)
                 if c == NCH - 1:
-                    nc.sync.dma_start(y_rows[:, :, c0 + b0 : c0 + b0 + bw], y[c][:, :, b0 : b0 + bw])
-                    nc.scalar.copy(
-                        rounded[c][:, PACK * b0 : PACK * (b0 + bw)].rearrange("p (g i t) -> p g t i", i=4, t=PACK),
-                        y[c][:, :, b0 : b0 + bw].rearrange("p t (g i) -> p g t i", i=4),
-                    )
-            if c < NCH - 1:
-                nc.sync.dma_start(y_rows[:, :, c0 : c0 + w], y[c][:])
+                    rounded[c] = held("y_bf%d" % c, [P, CHUNK * PACK], BF16)
+            for i, t in enumerate(slots):
+                cols = slice(i * w, (i + 1) * w)
+                nc.vector.scalar_tensor_tensor(
+                    y[c][:, t, b0 : b0 + w], banks["D", c, n][:, cols], bias_sb[:, t : t + 1], ab[c, n][:, cols], ALU.add, ALU.add
+                )
+            if c == NCH - 1:
+                nc.sync.dma_start(y_rows[:, :, c0 + b0 : c0 + b0 + w], y[c][:, :, b0 : b0 + w])
+                nc.scalar.copy(
+                    rounded[c][:, PACK * b0 : PACK * (b0 + w)].rearrange("p (g i t) -> p g t i", i=4, t=PACK),
+                    y[c][:, :, b0 : b0 + w].rearrange("p t (g i) -> p g t i", i=4),
+                )
+            elif n == 1:
+                nc.sync.dma_start(y_rows[:, :, c0 : c0 + CHUNK], y[c][:])
 
         def round_y(c):
-            shape = [P, CHUNK * PACK]
-            y_bf = placed("y_bf%d" % c, shape, BF16, a_place[2, c]) if c < 2 else held("y_bf%d" % c, shape, BF16)
-            if c == 0:
+            y_bf = placed("y_bf%d" % c, [P, CHUNK * PACK], BF16, (ab_place[1, 1] + 1, ab_place[2, 1], a_place[3, 0])[c])
+            if c == 2:
                 nc.gpsimd.tensor_scalar(
                     y_bf[:].rearrange("p (m t) -> p m t", t=PACK), y[c][:].rearrange("p t m -> p m t"), 1.0, 0.0, ALU.mult, ALU.add
                 )
@@ -364,35 +365,68 @@ def tile_list_electrode_refit_kernel(
                     )
             nc.sync.dma_start(code_rows[:, PACK * begin : PACK * end].bitcast(I32), y_w[:])
 
-        places = ((51, 52.5), (51.75, 53.25), (51.25, 54), (ab_place[0, 1], ab_place[0, 1] + 1))
+        def x_last(c):
+            return (x_first, x_second)[c] if c < 2 else x_rest[:, (c - 2) * CHUNK : (c - 1) * CHUNK]
 
-        def make_z(c):
-            c0, w = c * CHUNK, CHUNK
-            x = x_last[:, c0 : c0 + w]
-            if c < 2:
-                squares = feature(SQUARE, "square_last%d" % c, x, w, places[c][0])
-                apply_gain((nc.gpsimd, nc.vector)[c], SQUARE, LAST, c0, c0 + w, squares[:])
-                sines = feature(SIN, "sine_last%d" % c, x, w, places[c][1])
-                if c == 0:
-                    apply_gain(nc.scalar, SIN, 2, EARLY, M, late_sine[:])
-                apply_gain(nc.scalar, SIN, LAST, c0, c0 + w, sines[:])
-            else:
-                sines = feature(SIN, "sine_last%d" % c, x, w, places[c][1])
-                squares = feature(SQUARE, "square_last%d" % c, x, w, places[c][0])
-                apply_gain(nc.scalar, SIN, LAST, c0, c0 + w, sines[:])
-                apply_gain(nc.gpsimd, SQUARE, LAST, c0, c0 + w, squares[:])
-            for f in (SQUARE, SIN) if c < 2 else (SIN, SQUARE):
-                quantise_z(f, c0, c0 + w)
+        def gain_last(eng, f, c, values):
+            apply_gain(eng, f, LAST, c * CHUNK, (c + 1) * CHUNK, values)
 
-        make_z(0)
+        squares = feature(SQUARE, "square_last0", x_last(0), CHUNK, 54.25)
+        gain_last(nc.gpsimd, SQUARE, 0, squares[:])
+        sines = feature(SIN, "sine_last0", x_last(0), CHUNK, 51.25)
+        second_sines = feature(SIN, "sine_last1", x_last(1), CHUNK, 52.25)
+        gain_last(nc.scalar, SIN, 0, sines[:])
+        gain_last(nc.scalar, SIN, 1, second_sines[:])
+        apply_gain(nc.scalar, SIN, 2, EARLY, M, late_sine[:])
+        quantise_weight(0, 100)
+        quantise_z(SIN, 0)
+        quantise_z(SQUARE, 0)
+        quantise_weight(1, 109)
         quantise_weight(2, 105)
-        make_z(1)
+        quantise_z(SIN, 1)
+        scaled = placed("scaled1", [P, CHUNK], F32, 70)
+        nc.gpsimd.tensor_scalar(scaled[:], x_last(1), gain_rest[:, LAST - 1 : LAST], 0.0, ALU.mult, ALU.add)
+        nc.gpsimd.tensor_tensor(z_bf(SQUARE, CHUNK, 2 * CHUNK)[:, LAST : PACK * CHUNK : PACK], scaled[:], x_last(1), ALU.mult)
+
+        def sines_of(c):
+            values = feature(SIN, "sine_last%d" % c, x_last(c), CHUNK, 71 if c == 2 else ab_place[0, 1] + 1)
+            gain_last(nc.scalar, SIN, c, values[:])
+
+        def squares_of(c):
+            values = feature(SQUARE, "square_last%d" % c, x_last(c), CHUNK, ab_place[c - 2, 1])
+            gain_last(nc.gpsimd, SQUARE, c, values[:])
+
+        for n in range(2):
+            product("A", 0, n)
         for c in range(NCH):
-            make_y(c)
-            if c + 2 < NCH:
-                make_z(c + 2)
+            for n in range(2):
+                product("B", c, n)
+            if c >= 1 and c + 1 < NCH:
+                squares_of(c + 1)
             if c == NCH - 2:
                 round_y(0)
+            for n in range(2):
+                if c == 0:
+                    copy_a(c, n)
+                multiply(c, n)
+            if c == NCH - 1:
+                round_y(1)
+                round_y(2)
+            if c + 2 < NCH:
+                sines_of(c + 2)
+            for n in range(2):
+                product("D", c, n)
+                if c + 1 < NCH:
+                    product("A", c + 1, n)
+                    copy_a(c + 1, n)
+            add_up(c, 0)
+            if c + 1 < NCH:
+                quantise_z(SQUARE, c + 1)
+            add_up(c, 1)
+            if c + 2 < NCH:
+                quantise_z(SIN, c + 2)
+            if c == NCH - 2:
+                make_planes((0,), ab_place[c, 0])
         make_planes((1, 2), ab_place[NCH - 1, 0])
         make_planes((NCH - 1,), 16)
         for q in range(4):

@@ -263,9 +263,9 @@ def tile_list_electrode_refit_kernel(
         apply_gain(nc.gpsimd, SQUARE, 2, BANK, EARLY, second[:])
         scatter(LAST, 0, S)
         x = read_page(2, 2, EARLY, M)
-        square = feature(SQUARE, "square2_late", x, M - EARLY, 50.75)
-        late_sine = feature(SIN, "sine2_late", x, M - EARLY, 53.5)
-        apply_gain(nc.gpsimd, SQUARE, 2, EARLY, M, square[:])
+        square = feature(SQUARE, "square2_late", x, M - EARLY, 53.25)
+        late_sine = feature(SIN, "sine2_late", x, M - EARLY, 53.75)
+        late_square = square
 
         x_first = read_page(LAST, 101, 0, CHUNK)
         x_second = read_page(LAST, 102, CHUNK, 2 * CHUNK)
@@ -317,8 +317,8 @@ def tile_list_electrode_refit_kernel(
             nc.scalar.copy(a_sb[c, n][:], banks["A", c, n][:])
 
         def multiply(c, n):
-            ab[c, n] = placed("ab%d_%d" % (c, n), [P, BANK], F32, ab_place[c, n])
-            nc.vector.tensor_tensor(ab[c, n][:], banks["B", c, n][:], a_sb[c, n][:], ALU.mult)
+            ab[c, n] = placed("ab%d_%d" % (c, n), [P, BANK + CHUNK if (c, n) == (1, 1) else BANK], F32, ab_place[c, n])
+            nc.vector.tensor_tensor(ab[c, n][:, 0:BANK], banks["B", c, n][:], a_sb[c, n][:], ALU.mult)
 
         def add_up(c, n):
             slots, b0, w = part(c, n)
@@ -342,14 +342,17 @@ def tile_list_electrode_refit_kernel(
                 nc.sync.dma_start(y_rows[:, :, c0 : c0 + CHUNK], y[c][:])
 
         def round_y(c):
-            y_bf = placed("y_bf%d" % c, [P, CHUNK * PACK], BF16, (ab_place[1, 1] + 1, ab_place[2, 1], a_place[3, 0])[c])
+            if c == 0:
+                y_bf = ab[1, 1][:, CHUNK : BANK + CHUNK].bitcast(BF16)
+            else:
+                y_bf = placed("y_bf%d" % c, [P, CHUNK * PACK], BF16, (ab_place[2, 1], 30)[c - 1])[:]
             if c == 2:
                 nc.gpsimd.tensor_scalar(
-                    y_bf[:].rearrange("p (m t) -> p m t", t=PACK), y[c][:].rearrange("p t m -> p m t"), 1.0, 0.0, ALU.mult, ALU.add
+                    y_bf.rearrange("p (m t) -> p m t", t=PACK), y[c][:].rearrange("p t m -> p m t"), 1.0, 0.0, ALU.mult, ALU.add
                 )
             else:
                 nc.scalar.copy(
-                    y_bf[:].rearrange("p (g i t) -> p g t i", i=4, t=PACK), y[c][:].rearrange("p t (g i) -> p g t i", i=4)
+                    y_bf.rearrange("p (g i t) -> p g t i", i=4, t=PACK), y[c][:].rearrange("p t (g i) -> p g t i", i=4)
                 )
             rounded[c] = y_bf
 
@@ -378,23 +381,23 @@ def tile_list_electrode_refit_kernel(
         gain_last(nc.scalar, SIN, 0, sines[:])
         gain_last(nc.scalar, SIN, 1, second_sines[:])
         apply_gain(nc.scalar, SIN, 2, EARLY, M, late_sine[:])
+        apply_gain(nc.scalar, SQUARE, 2, EARLY, M, late_square[:])
         quantise_weight(0, 100)
         quantise_z(SIN, 0)
         quantise_z(SQUARE, 0)
         quantise_weight(1, 109)
         quantise_weight(2, 105)
         quantise_z(SIN, 1)
-        scaled = placed("scaled1", [P, CHUNK], F32, 70)
-        nc.gpsimd.tensor_scalar(scaled[:], x_last(1), gain_rest[:, LAST - 1 : LAST], 0.0, ALU.mult, ALU.add)
-        nc.gpsimd.tensor_tensor(z_bf(SQUARE, CHUNK, 2 * CHUNK)[:, LAST : PACK * CHUNK : PACK], scaled[:], x_last(1), ALU.mult)
 
         def sines_of(c):
-            values = feature(SIN, "sine_last%d" % c, x_last(c), CHUNK, 71 if c == 2 else ab_place[0, 1] + 1)
-            gain_last(nc.scalar, SIN, c, values[:])
+            values = placed("sine_last2", [P, CHUNK], F32, 71)[:] if c == 2 else ab[0, 1][:, CHUNK : 2 * CHUNK]
+            nc.scalar.activation(values, x_last(c), ACT.Sin)
+            gain_last(nc.scalar, SIN, c, values)
 
         def squares_of(c):
-            values = feature(SQUARE, "square_last%d" % c, x_last(c), CHUNK, ab_place[c - 2, 1])
-            gain_last(nc.gpsimd, SQUARE, c, values[:])
+            values = placed("square_last1", [P, CHUNK], F32, 70)[:] if c == 1 else ab[c - 2, 1][:, 0:CHUNK]
+            nc.scalar.activation(values, x_last(c), ACT.Square)
+            gain_last(nc.gpsimd, SQUARE, c, values)
 
         for n in range(2):
             product("A", 0, n)
@@ -409,6 +412,8 @@ def tile_list_electrode_refit_kernel(
                 if c == 0:
                     copy_a(c, n)
                 multiply(c, n)
+            if c == 0:
+                squares_of(1)
             if c == NCH - 1:
                 round_y(1)
                 round_y(2)

@@ -55,7 +55,7 @@ def tile_list_electrode_refit_kernel(
         tab_w = [placed("tab_w%d" % a, [P, T], I32, (13.75, 116)[a]) for a in range(2)]
         tab_s = placed("tab_s", [P, T], U8, 90)
         w1_s_raw = placed("w1_s_raw", [P, 2, H], U8, 95)
-        v_s = placed("v_s", [P, 2, S], U8, 38)
+        v_s = placed("v_s", [P, 2, S], U8, 144)
         nc.gpsimd.memset(w1_s_raw[:].rearrange("p a c -> p (a c)").bitcast(I32), 0)
         nc.vector.memset(tab_s[0 : P - QUAD, :].bitcast(I32), 0)
         nc.vector.memset(v_s[:].rearrange("p a c -> p (a c)").bitcast(I32), 0)
@@ -96,7 +96,7 @@ def tile_list_electrode_refit_kernel(
             w_raw[i] = placed("w_raw%d" % i, [P, PACK, N], F32, kb)
             nc.sync.dma_start(w_raw[i][:], w_src[i].rearrange("(p j) n -> p j n", j=PACK))
 
-        picked_s = placed("picked_s", [P, S], U8, 96)
+        picked_s = placed("picked_s", [P, S], U8, 63)
         nc.vector.tensor_copy(picked_s[:], tab_s[:].indirect(idx[:]))
         for q in range(4):
             row = P - QUAD + 8 * q
@@ -107,20 +107,20 @@ def tile_list_electrode_refit_kernel(
         load_wg_part(0, (2, 1, 3), 0, HEAD)
         load_wg_part(0, (0, 2, 1, 3), HEAD, S)
 
-        w1_w = placed("w1_w", [P, 2, PACK, 2 * P], U8, 47)
+        w1_w = placed("w1_w", [P, 2, PACK, 2 * P], U8, 45.5)
         nc.scalar.copy(w1_w[:].bitcast(U16), w1_w_raw[:].bitcast(U16).rearrange("p a (m t) -> p a t m", t=PACK))
-        w1_s = placed("w1_s", [P, 2, PACK, P], U8, 63)
+        w1_s = placed("w1_s", [P, 2, PACK, P], U8, 146)
         w1_s_by_slot = w1_s_raw[:].rearrange("p a (m t) -> p a t m", t=PACK)
         nc.gpsimd.tensor_copy(w1_s[:, :, 0, :], w1_s_by_slot[:, :, 0, :])
         nc.gpsimd.tensor_copy(w1_s[:, :, 1:PACK, :], w1_s_by_slot[:, :, 1:PACK, :])
 
-        v_w = [placed("v_w0", [P, S], U32, 133), placed("v_w1", [P, S], U32, 32)]
+        v_w = [placed("v_w0", [P, S], U32, 140), placed("v_w1", [P, S], U32, 32)]
         nc.vector.tensor_copy(v_w[0][:], tab_w[0][:].bitcast(U32).indirect(idx[:]))
         for c0, w in PIECES:
             where = idx[:, c0 // PER_COL : (c0 + w) // PER_COL]
             nc.vector.tensor_copy(v_w[1][:, c0 : c0 + w], tab_w[1][:].bitcast(U32).indirect(where))
 
-        h_head = placed("h_head", [P, HEAD], F32, 79)
+        h_head = placed("h_head", [P, HEAD], F32, 135)
         h_rest = placed("h_rest", [P, S - HEAD], F32, 80)
         h_sb = {t: placed("h%d" % t, [P, S], F32, kb) for t, kb in ((1, 5.75), (2, 74), (3, 0))}
         h2_head = placed("h2_head", [P, HEAD], F32, 73)
@@ -155,10 +155,10 @@ def tile_list_electrode_refit_kernel(
         for q in range(4):
             nc.sync.dma_start(wb_s_raw[QUAD * q : QUAD * q + 4, :].bitcast(I32), wb_scales[0, 4 * q : 4 * q + 4, :].bitcast(I32))
         gain_rows = gain.rearrange("(f p t) -> f p t", f=2, t=PACK)
-        gain_sin = placed("gain_sin", [P, PACK], F32, 38.5)
-        gain_first = placed("gain_first", [P, 1], F32, 38.625)
-        gain_rest = placed("gain_rest", [P, PACK - 1], F32, 38.6875)
-        bias_sb = placed("bias_sb", [P, PACK], F32, 38.75)
+        gain_sin = placed("gain_sin", [P, PACK], F32, 121.5)
+        gain_first = placed("gain_first", [P, 1], F32, 121.625)
+        gain_rest = placed("gain_rest", [P, PACK - 1], F32, 121.6875)
+        bias_sb = placed("bias_sb", [P, PACK], F32, 121.75)
         nc.sync.dma_start(gain_sin[:], gain_rows[SIN])
         load_page(2, 39)
         load_wg(2, 30)
@@ -167,13 +167,13 @@ def tile_list_electrode_refit_kernel(
         load_weight(1, 131.75)
         wb_w_raw = placed("wb_w_raw", [P, N], I32, 63.5)
         nc.sync.dma_start(wb_w_raw[:], wb_words[0].rearrange("p c i -> p (c i)").bitcast(I32))
-        load_page(3, 55.5)
         load_wg(3, 34)
         nc.sync.dma_start(gain_rest[:], gain_rows[SQUARE][:, 1:PACK])
         load_weight(2, 47)
+        load_page(3, 55.5)
         nc.sync.dma_start(bias_sb[:], bias.rearrange("(p t) -> p t", t=PACK))
 
-        w_s = [placed("w_s%d" % i, [P, N], U8, kb) for i, kb in enumerate((130, 50.875, 51.375))]
+        w_s = [placed("w_s%d" % i, [P, N], U8, kb) for i, kb in enumerate((111, 50.875, 51.375))]
         w_w, grouped = {}, {}
 
         def round_weight(i, tile):
@@ -262,14 +262,14 @@ def tile_list_electrode_refit_kernel(
         apply_gain(nc.scalar, SIN, 2, 0, EARLY, sine[:])
         apply_gain(nc.gpsimd, SQUARE, 2, BANK, EARLY, second[:])
         scatter(LAST, 0, S)
-        x = read_page(2, 2, EARLY, M)
+        x = read_page(2, 126.5, EARLY, M)
         square = feature(SQUARE, "square2_late", x, M - EARLY, 53.25)
         late_sine = feature(SIN, "sine2_late", x, M - EARLY, 53.75)
         late_square = square
 
-        x_first = read_page(LAST, 101, 0, CHUNK)
-        x_second = read_page(LAST, 102, CHUNK, 2 * CHUNK)
-        x_rest = read_page(LAST, 103, 2 * CHUNK, M)
+        x_first = read_page(LAST, 127, 0, CHUNK)
+        x_second = read_page(LAST, 128, CHUNK, 2 * CHUNK)
+        x_rest = read_page(LAST, 129, 2 * CHUNK, M)
         z_w = [held("z_w%d" % f, [P, M], U32) for f in range(2)]
         z_s = {}
         y_s = held("y_s", [P, M], U8)
@@ -382,11 +382,11 @@ def tile_list_electrode_refit_kernel(
         gain_last(nc.scalar, SIN, 1, second_sines[:])
         apply_gain(nc.scalar, SIN, 2, EARLY, M, late_sine[:])
         apply_gain(nc.scalar, SQUARE, 2, EARLY, M, late_square[:])
-        quantise_weight(0, 100)
+        quantise_weight(0, 126)
         quantise_z(SIN, 0)
         quantise_z(SQUARE, 0)
         quantise_weight(1, 109)
-        quantise_weight(2, 105)
+        quantise_weight(2, 107)
         quantise_z(SIN, 1)
 
         def sines_of(c):

@@ -173,7 +173,7 @@ def tile_list_electrode_refit_kernel(
         load_page(3, 55.5)
         nc.sync.dma_start(bias_sb[:], bias.rearrange("(p t) -> p t", t=PACK))
 
-        w_s = [placed("w_s%d" % i, [P, N], U8, kb) for i, kb in enumerate((111, 50.875, 51.375))]
+        w_s = [placed("w_s%d" % i, [P, N], U8, kb) for i, kb in enumerate((127, 50.875, 51.375))]
         w_w, grouped = {}, {}
 
         def round_weight(i, tile):
@@ -267,9 +267,10 @@ def tile_list_electrode_refit_kernel(
         late_sine = feature(SIN, "sine2_late", x, M - EARLY, 53.75)
         late_square = square
 
-        x_first = read_page(LAST, 127, 0, CHUNK)
-        x_second = read_page(LAST, 128, CHUNK, 2 * CHUNK)
-        x_rest = read_page(LAST, 129, 2 * CHUNK, M)
+        x_first = read_page(LAST, 127.5, 0, CHUNK)
+        x_second = read_page(LAST, 128.5, CHUNK, 2 * CHUNK)
+        quantise_weight(0, 100)
+        x_rest = read_page(LAST, 129.5, 2 * CHUNK, M)
         z_w = [held("z_w%d" % f, [P, M], U32) for f in range(2)]
         z_s = {}
         y_s = held("y_s", [P, M], U8)
@@ -342,10 +343,10 @@ def tile_list_electrode_refit_kernel(
                 nc.sync.dma_start(y_rows[:, :, c0 : c0 + CHUNK], y[c][:])
 
         def round_y(c):
-            if c == 0:
+            if c != 1:
                 y_bf = ab[1, 1][:, CHUNK : BANK + CHUNK].bitcast(BF16)
             else:
-                y_bf = placed("y_bf%d" % c, [P, CHUNK * PACK], BF16, (ab_place[2, 1], 30)[c - 1])[:]
+                y_bf = placed("y_bf%d" % c, [P, CHUNK * PACK], BF16, ab_place[2, 1])[:]
             if c == 2:
                 nc.gpsimd.tensor_scalar(
                     y_bf.rearrange("p (m t) -> p m t", t=PACK), y[c][:].rearrange("p t m -> p m t"), 1.0, 0.0, ALU.mult, ALU.add
@@ -382,7 +383,6 @@ def tile_list_electrode_refit_kernel(
         gain_last(nc.scalar, SIN, 1, second_sines[:])
         apply_gain(nc.scalar, SIN, 2, EARLY, M, late_sine[:])
         apply_gain(nc.scalar, SQUARE, 2, EARLY, M, late_square[:])
-        quantise_weight(0, 126)
         quantise_z(SIN, 0)
         quantise_z(SQUARE, 0)
         quantise_weight(1, 109)
@@ -395,7 +395,7 @@ def tile_list_electrode_refit_kernel(
             gain_last(nc.scalar, SIN, c, values)
 
         def squares_of(c):
-            values = placed("square_last1", [P, CHUNK], F32, 70)[:] if c == 1 else ab[c - 2, 1][:, 0:CHUNK]
+            values = placed("square_last1", [P, CHUNK], F32, 12.75)[:] if c == 1 else ab[c - 2, 1][:, 0:CHUNK]
             nc.scalar.activation(values, x_last(c), ACT.Square)
             gain_last(nc.gpsimd, SQUARE, c, values)
 
@@ -411,9 +411,9 @@ def tile_list_electrode_refit_kernel(
             for n in range(2):
                 if c == 0:
                     copy_a(c, n)
+                    if n == 0:
+                        squares_of(1)
                 multiply(c, n)
-            if c == 0:
-                squares_of(1)
             if c == NCH - 1:
                 round_y(1)
                 round_y(2)

@@ -93,8 +93,8 @@ def tile_list_electrode_refit_kernel(
             load_wg_part(t, (0, 2, 1, 3), 0, S)
 
         def load_weight(i, kb):
-            w_raw[i] = placed("w_raw%d" % i, [P, PACK, N], F32, kb)
-            nc.sync.dma_start(w_raw[i][:], w_src[i].rearrange("(p j) n -> p j n", j=PACK))
+            w_raw[i] = placed("w_raw%d" % i, [P, PACK * N], F32, kb)
+            nc.sync.dma_start(w_raw[i][:], w_src[i].rearrange("(p j) n -> p (j n)", j=PACK))
 
         picked_s = placed("picked_s", [P, S], U8, 63)
         nc.vector.tensor_copy(picked_s[:], tab_s[:].indirect(idx[:]))
@@ -155,32 +155,32 @@ def tile_list_electrode_refit_kernel(
         for q in range(4):
             nc.sync.dma_start(wb_s_raw[QUAD * q : QUAD * q + 4, :].bitcast(I32), wb_scales[0, 4 * q : 4 * q + 4, :].bitcast(I32))
         gain_rows = gain.rearrange("(f p t) -> f p t", f=2, t=PACK)
-        gain_sin = placed("gain_sin", [P, PACK], F32, 121.5)
-        gain_first = placed("gain_first", [P, 1], F32, 121.625)
-        gain_rest = placed("gain_rest", [P, PACK - 1], F32, 121.6875)
-        bias_sb = placed("bias_sb", [P, PACK], F32, 121.75)
+        gain_sin = placed("gain_sin", [P, PACK], F32, 122.5)
+        gain_first = placed("gain_first", [P, 1], F32, 122.625)
+        gain_rest = placed("gain_rest", [P, PACK - 1], F32, 122.6875)
+        bias_sb = placed("bias_sb", [P, PACK], F32, 122.75)
         nc.sync.dma_start(gain_sin[:], gain_rows[SIN])
         load_page(2, 39)
         load_wg(2, 30)
         with nc.allow_non_contiguous_dma(reason="one gain a partition"):
             nc.sync.dma_start(gain_first[:], gain_rows[SQUARE][:, 0:1])
         load_weight(1, 131.75)
+        load_weight(2, 47)
         wb_w_raw = placed("wb_w_raw", [P, N], I32, 63.5)
         nc.sync.dma_start(wb_w_raw[:], wb_words[0].rearrange("p c i -> p (c i)").bitcast(I32))
+        load_page(3, 55.5)
         load_wg(3, 34)
         nc.sync.dma_start(gain_rest[:], gain_rows[SQUARE][:, 1:PACK])
-        load_weight(2, 47)
-        load_page(3, 55.5)
         nc.sync.dma_start(bias_sb[:], bias.rearrange("(p t) -> p t", t=PACK))
 
-        w_s = [placed("w_s%d" % i, [P, N], U8, kb) for i, kb in enumerate((127, 50.875, 51.375))]
+        w_s = [placed("w_s%d" % i, [P, N], U8, kb) for i, kb in enumerate((33.5, 70.75, 71.25))]
         w_w, grouped = {}, {}
 
         def round_weight(i, tile):
             grouped[i] = tile
             nc.scalar.copy(
                 tile[:].rearrange("p (t m j) -> p m j t", t=PACK, j=PACK),
-                w_raw[i][:].rearrange("p j (m t) -> p m j t", t=PACK),
+                w_raw[i][:].rearrange("p (j m t) -> p m j t", j=PACK, t=PACK),
             )
 
         def quantise_weight(i, kb):
@@ -237,40 +237,46 @@ def tile_list_electrode_refit_kernel(
         round_weight(1, placed("grouped1", [P, N * PACK], BF16, 9.75))
         weigh(2, 17.75, [(0, HEAD, h2_head[:]), (HEAD, S, h_sb[2][:, HEAD:S])])
         apply_gain(nc.gpsimd, SQUARE, 0, 0, M, square[:])
-        wb_w = placed("wb_w", [P, N], U32, 76)
-        nc.scalar.copy(wb_w[:].rearrange("p (t m) -> p t m", t=PACK), wb_w_raw[:].bitcast(U32).rearrange("p (m t) -> p t m", t=PACK))
+        round_weight(2, placed("grouped2", [P, N * PACK], BF16, 148))
+        spare = w_raw[2]
+
+        def feature_in(f, x, c0, w):
+            nc.scalar.activation(spare[:, c0 : c0 + w], x, ACT.Sin if f == SIN else ACT.Square)
+            return spare[:, c0 : c0 + w]
+
         scatter(1, 0, S)
         scatter(2, 0, HEAD)
         x = read_page(1, 70.5, 0, EARLY)
-        sine = feature(SIN, "sine1", x, EARLY, 131.75)
-        square = feature(SQUARE, "square1", x, EARLY, 135.75)
-        apply_gain(nc.scalar, SIN, 1, 0, EARLY, sine[:])
+        sine = feature_in(SIN, x, 0, EARLY)
+        square = feature_in(SQUARE, x, 1152, EARLY)
+        apply_gain(nc.scalar, SIN, 1, 0, EARLY, sine)
         weigh(LAST, 30, [(0, S, h_sb[LAST][:])])
-        apply_gain(nc.gpsimd, SQUARE, 1, 0, EARLY, square[:])
-        round_weight(2, placed("grouped2", [P, N * PACK], BF16, 70))
+        apply_gain(nc.gpsimd, SQUARE, 1, 0, EARLY, square)
+        wb_w = placed("wb_w", [P, N], U32, 68.75)
+        nc.scalar.copy(wb_w[:].rearrange("p (t m) -> p t m", t=PACK), wb_w_raw[:].bitcast(U32).rearrange("p (m t) -> p t m", t=PACK))
         scatter(2, HEAD, S)
         x = read_page(1, 75, EARLY, M)
-        square = feature(SQUARE, "square1_late", x, M - EARLY, 50.5)
-        late_sine = feature(SIN, "sine1_late", x, M - EARLY, 54.5)
-        apply_gain(nc.gpsimd, SQUARE, 1, EARLY, M, square[:])
+        square = feature_in(SQUARE, x, 512, M - EARLY)
+        late_sine = feature_in(SIN, x, 640, M - EARLY)
+        apply_gain(nc.gpsimd, SQUARE, 1, EARLY, M, square)
         x = read_page(2, 126.5, 0, EARLY)
-        first = feature(SQUARE, "square2_first", x[:, 0:BANK], BANK, 47)
-        apply_gain(nc.scalar, SIN, 1, EARLY, M, late_sine[:])
-        sine = feature(SIN, "sine2", x, EARLY, 51)
-        second = feature(SQUARE, "square2_second", x[:, BANK:EARLY], EARLY - BANK, 49)
-        apply_gain(nc.gpsimd, SQUARE, 2, 0, BANK, first[:])
+        first = feature_in(SQUARE, x[:, 0:BANK], 0, BANK)
+        apply_gain(nc.scalar, SIN, 1, EARLY, M, late_sine)
+        sine = feature(SIN, "sine2", x, EARLY, 70.75)
+        second = feature_in(SQUARE, x[:, BANK:EARLY], 768, EARLY - BANK)
+        apply_gain(nc.gpsimd, SQUARE, 2, 0, BANK, first)
         apply_gain(nc.scalar, SIN, 2, 0, EARLY, sine[:])
-        apply_gain(nc.gpsimd, SQUARE, 2, BANK, EARLY, second[:])
+        apply_gain(nc.gpsimd, SQUARE, 2, BANK, EARLY, second)
         scatter(LAST, 0, S)
-        x = read_page(2, 126.5, EARLY, M)
-        square = feature(SQUARE, "square2_late", x, M - EARLY, 53.25)
-        late_sine = feature(SIN, "sine2_late", x, M - EARLY, 53.75)
+        x = read_page(2, 2, EARLY, M)
+        square = feature(SQUARE, "square2_late", x, M - EARLY, 73)
+        late_sine = feature(SIN, "sine2_late", x, M - EARLY, 73.5)
         late_square = square
 
-        x_first = read_page(LAST, 127.5, 0, CHUNK)
-        x_second = read_page(LAST, 128.5, CHUNK, 2 * CHUNK)
+        x_first = read_page(LAST, 102, 0, CHUNK)
+        x_second = read_page(LAST, 103, CHUNK, 2 * CHUNK)
         quantise_weight(0, 100)
-        x_rest = read_page(LAST, 129.5, 2 * CHUNK, M)
+        x_rest = read_page(LAST, 120, 2 * CHUNK, M)
         z_w = [held("z_w%d" % f, [P, M], U32) for f in range(2)]
         z_s = {}
         y_s = held("y_s", [P, M], U8)
@@ -280,7 +286,7 @@ def tile_list_electrode_refit_kernel(
 
         a_place = {(0, 0): 84, (0, 1): 86, (1, 0): 88, (1, 1): 112, (2, 0): 12, (2, 1): 14, (3, 0): 10, (3, 1): 114}
         ab_place = {(0, 0): 116, (0, 1): 118, (1, 0): 18, (1, 1): 20, (2, 0): 24, (2, 1): 26, (3, 0): 8, (3, 1): 28}
-        scale_place = {(SQUARE, 0): 51.875, (SIN, 2): ab_place[0, 0], (SIN, 3): ab_place[1, 0]}
+        scale_place = {(SQUARE, 0): 71.75, (SIN, 2): a_place[0, 1], (SIN, 3): a_place[1, 1]}
 
         def quantise_z(f, c):
             name, c0 = "z_s%d_%d" % (f, c), c * CHUNK
@@ -375,10 +381,10 @@ def tile_list_electrode_refit_kernel(
         def gain_last(eng, f, c, values):
             apply_gain(eng, f, LAST, c * CHUNK, (c + 1) * CHUNK, values)
 
-        squares = feature(SQUARE, "square_last0", x_last(0), CHUNK, 54.25)
+        squares = feature(SQUARE, "square_last0", x_last(0), CHUNK, 74)
         gain_last(nc.gpsimd, SQUARE, 0, squares[:])
-        sines = feature(SIN, "sine_last0", x_last(0), CHUNK, 51.25)
-        second_sines = feature(SIN, "sine_last1", x_last(1), CHUNK, 52.25)
+        sines = feature(SIN, "sine_last0", x_last(0), CHUNK, 71)
+        second_sines = feature(SIN, "sine_last1", x_last(1), CHUNK, 72)
         gain_last(nc.scalar, SIN, 0, sines[:])
         gain_last(nc.scalar, SIN, 1, second_sines[:])
         apply_gain(nc.scalar, SIN, 2, EARLY, M, late_sine[:])
@@ -390,12 +396,12 @@ def tile_list_electrode_refit_kernel(
         quantise_z(SIN, 1)
 
         def sines_of(c):
-            values = placed("sine_last2", [P, CHUNK], F32, 71)[:] if c == 2 else ab[0, 1][:, CHUNK : 2 * CHUNK]
+            values = placed("sine_last2", [P, CHUNK], F32, 149)[:] if c == 2 else ab[0, 0][:, 0:CHUNK]
             nc.scalar.activation(values, x_last(c), ACT.Sin)
             gain_last(nc.scalar, SIN, c, values)
 
         def squares_of(c):
-            values = placed("square_last1", [P, CHUNK], F32, 12.75)[:] if c == 1 else ab[c - 2, 1][:, 0:CHUNK]
+            values = placed("square_last1", [P, CHUNK], F32, 12.75)[:] if c == 1 else ab[c - 2, 0][:, CHUNK:BANK]
             nc.scalar.activation(values, x_last(c), ACT.Square)
             gain_last(nc.gpsimd, SQUARE, c, values)
 
@@ -404,8 +410,6 @@ def tile_list_electrode_refit_kernel(
         for c in range(NCH):
             for n in range(2):
                 product("B", c, n)
-            if c >= 1 and c + 1 < NCH:
-                squares_of(c + 1)
             if c == NCH - 2:
                 round_y(0)
             for n in range(2):
@@ -417,21 +421,26 @@ def tile_list_electrode_refit_kernel(
             if c == NCH - 1:
                 round_y(1)
                 round_y(2)
-            if c + 2 < NCH:
-                sines_of(c + 2)
+            if c == 0:
+                sines_of(2)
             for n in range(2):
                 product("D", c, n)
                 if c + 1 < NCH:
                     product("A", c + 1, n)
                     copy_a(c + 1, n)
-            add_up(c, 0)
+                if n == 0:
+                    add_up(c, 0)
+                    if c + 2 < NCH:
+                        squares_of(c + 2)
+            if c == 0:
+                sines_of(3)
             if c + 1 < NCH:
                 quantise_z(SQUARE, c + 1)
-            add_up(c, 1)
             if c + 2 < NCH:
                 quantise_z(SIN, c + 2)
             if c == NCH - 2:
-                make_planes((0,), ab_place[c, 0])
+                make_planes((0,), a_place[c, 1])
+            add_up(c, 1)
         make_planes((1, 2), ab_place[NCH - 1, 0])
         make_planes((NCH - 1,), 16)
         for q in range(4):

@@ -272,6 +272,15 @@ def tile_list_electrode_refit_kernel(
         square = feature(SQUARE, "square2_late", x, M - EARLY, 73)
         late_sine = feature(SIN, "sine2_late", x, M - EARLY, 73.5)
         late_square = square
+        warm_w = placed("warm_w", [P, 2 * P], U8, 70.75)
+        nc.scalar.copy(warm_w[:].bitcast(U16), w1_w_raw[:, 0, :].bitcast(U16)[:, 0:H:PACK])
+        warm = psum.tile([P, BANK], F32, name="acc", tag="bank")
+        for n in range(4):
+            cols = slice(BANK * (n % 2), BANK * (n % 2 + 1))
+            nc.tensor.matmul_mx(
+                warm[:], lhsT=warm_w[:].bitcast(FP4X4), lhsT_scale=w1_s[:, 0, 0, :],
+                rhs=v_w[0][:, cols].bitcast(FP8X4), rhs_scale=v_s[:, 0, cols], start=True, stop=True,
+            )
 
         x_first = read_page(LAST, 102, 0, CHUNK)
         x_second = read_page(LAST, 103, CHUNK, 2 * CHUNK)
@@ -302,22 +311,20 @@ def tile_list_electrode_refit_kernel(
             return range(PACK), n * CHUNK // 2, CHUNK // 2
 
         def product(kind, c, n):
-            terms = {
-                "A": lambda: [(w_w[0], w_s[0], SIN)],
-                "B": lambda: [(wb_w, wb_s, SQUARE)],
-                "D": lambda: [(w_w[1], w_s[1], SIN), (w_w[2], w_s[2], SQUARE)],
-            }[kind]()
+            words, scales, f = {
+                "A": (w_w[0], w_s[0], SIN), "B": (wb_w, wb_s, SQUARE), "D": (w_w[1], w_s[1], SIN), "E": (w_w[2], w_s[2], SQUARE),
+            }[kind]
             slots, b0, w = part(c, n)
-            acc = psum.tile([P, BANK], F32, name="acc", tag="bank")
+            if kind != "E":
+                banks[kind, c, n] = psum.tile([P, BANK], F32, name="acc", tag="bank")
+            acc = banks["D" if kind == "E" else kind, c, n]
             for i, t in enumerate(slots):
                 cols = slice(P * t, P * (t + 1))
-                for k, (words, scales, f) in enumerate(terms):
-                    nc.tensor.matmul_mx(
-                        acc[:, i * w : (i + 1) * w], lhsT=words[:, cols].bitcast(FP8X4), lhsT_scale=scales[:, cols],
-                        rhs=z_w[f][:, c * CHUNK + b0 : c * CHUNK + b0 + w].bitcast(FP8X4), rhs_scale=z_s[f, c][:, b0 : b0 + w],
-                        start=(k == 0), stop=(k == len(terms) - 1),
-                    )
-            banks[kind, c, n] = acc
+                nc.tensor.matmul_mx(
+                    acc[:, i * w : (i + 1) * w], lhsT=words[:, cols].bitcast(FP8X4), lhsT_scale=scales[:, cols],
+                    rhs=z_w[f][:, c * CHUNK + b0 : c * CHUNK + b0 + w].bitcast(FP8X4), rhs_scale=z_s[f, c][:, b0 : b0 + w],
+                    start=kind in "AB" or (kind == "D" and i == 0), stop=kind in "AB" or (kind == "E" and i == len(slots) - 1),
+                )
 
         def copy_a(c, n):
             a_sb[c, n] = placed("a_sb%d_%d" % (c, n), [P, BANK], F32, a_place[c, n])
@@ -381,13 +388,13 @@ def tile_list_electrode_refit_kernel(
         def gain_last(eng, f, c, values):
             apply_gain(eng, f, LAST, c * CHUNK, (c + 1) * CHUNK, values)
 
+        sines = feature(SIN, "sine_last0", x_last(0), CHUNK, 71)
         squares = feature(SQUARE, "square_last0", x_last(0), CHUNK, 74)
         gain_last(nc.gpsimd, SQUARE, 0, squares[:])
-        sines = feature(SIN, "sine_last0", x_last(0), CHUNK, 71)
-        second_sines = feature(SIN, "sine_last1", x_last(1), CHUNK, 72)
         gain_last(nc.scalar, SIN, 0, sines[:])
-        gain_last(nc.scalar, SIN, 1, second_sines[:])
+        second_sines = feature(SIN, "sine_last1", x_last(1), CHUNK, 72)
         apply_gain(nc.scalar, SIN, 2, EARLY, M, late_sine[:])
+        gain_last(nc.scalar, SIN, 1, second_sines[:])
         apply_gain(nc.scalar, SQUARE, 2, EARLY, M, late_square[:])
         quantise_z(SIN, 0)
         quantise_z(SQUARE, 0)
@@ -424,7 +431,9 @@ def tile_list_electrode_refit_kernel(
             if c == 0:
                 sines_of(2)
             for n in range(2):
-                product("D", c, n)
+                if c == 0:
+                    product("D", c, n)
+                product("E", c, n)
                 if c + 1 < NCH:
                     product("A", c + 1, n)
                     copy_a(c + 1, n)
@@ -434,6 +443,9 @@ def tile_list_electrode_refit_kernel(
                         squares_of(c + 2)
             if c == 0:
                 sines_of(3)
+            if c + 1 < NCH:
+                for n in range(2):
+                    product("D", c + 1, n)
             if c + 1 < NCH:
                 quantise_z(SQUARE, c + 1)
             if c + 2 < NCH:

@@ -28,6 +28,7 @@ CHUNK = 256
 NCH = M // CHUNK
 LAST = PACK - 1
 EARLY = M - T2 // 16
+EARLY1 = M - 256
 SIN, SQUARE = 0, 1
 
 
@@ -173,7 +174,7 @@ def tile_list_electrode_refit_kernel(
         nc.sync.dma_start(gain_rest[:], gain_rows[SQUARE][:, 1:PACK])
         nc.sync.dma_start(bias_sb[:], bias.rearrange("(p t) -> p t", t=PACK))
 
-        w_s = [placed("w_s%d" % i, [P, N], U8, kb) for i, kb in enumerate((33.5, 70.75, 71.25))]
+        w_s = [placed("w_s%d" % i, [P, N], U8, kb) for i, kb in enumerate((33.5, 71.25, 71.75))]
         w_w, grouped = {}, {}
 
         def round_weight(i, tile):
@@ -246,33 +247,33 @@ def tile_list_electrode_refit_kernel(
 
         scatter(1, 0, S)
         scatter(2, 0, HEAD)
-        x = read_page(1, 70.5, 0, EARLY)
-        sine = feature_in(SIN, x, 0, EARLY)
-        square = feature_in(SQUARE, x, 1152, EARLY)
-        apply_gain(nc.scalar, SIN, 1, 0, EARLY, sine)
+        x = read_page(1, 71, 0, EARLY1)
+        sine = feature_in(SIN, x, 0, EARLY1)
+        square = feature_in(SQUARE, x, 1280, EARLY1)
+        apply_gain(nc.scalar, SIN, 1, 0, EARLY1, sine)
         weigh(LAST, 30, [(0, S, h_sb[LAST][:])])
-        apply_gain(nc.gpsimd, SQUARE, 1, 0, EARLY, square)
-        wb_w = placed("wb_w", [P, N], U32, 68.75)
+        apply_gain(nc.gpsimd, SQUARE, 1, 0, EARLY1, square)
+        wb_w = placed("wb_w", [P, N], U32, 69.25)
         nc.scalar.copy(wb_w[:].rearrange("p (t m) -> p t m", t=PACK), wb_w_raw[:].bitcast(U32).rearrange("p (m t) -> p t m", t=PACK))
         scatter(2, HEAD, S)
-        x = read_page(1, 75, EARLY, M)
-        square = feature_in(SQUARE, x, 512, M - EARLY)
-        late_sine = feature_in(SIN, x, 640, M - EARLY)
-        apply_gain(nc.gpsimd, SQUARE, 1, EARLY, M, square)
+        x = read_page(1, 75.5, EARLY1, M)
+        late_sine = feature_in(SIN, x, 256, M - EARLY1)
+        square = feature_in(SQUARE, x, 0, M - EARLY1)
+        apply_gain(nc.gpsimd, SQUARE, 1, EARLY1, M, square)
+        apply_gain(nc.scalar, SIN, 1, EARLY1, M, late_sine)
         x = read_page(2, 126.5, 0, EARLY)
-        first = feature_in(SQUARE, x[:, 0:BANK], 0, BANK)
-        apply_gain(nc.scalar, SIN, 1, EARLY, M, late_sine)
-        sine = feature(SIN, "sine2", x, EARLY, 70.75)
-        second = feature_in(SQUARE, x[:, BANK:EARLY], 768, EARLY - BANK)
+        first = feature_in(SQUARE, x[:, 0:BANK], 512, BANK)
+        sine = feature(SIN, "sine2", x, EARLY, 71.25)
+        second = feature(SQUARE, "square2_second", x[:, BANK:EARLY], EARLY - BANK, 76)[:]
         apply_gain(nc.gpsimd, SQUARE, 2, 0, BANK, first)
         apply_gain(nc.scalar, SIN, 2, 0, EARLY, sine[:])
         apply_gain(nc.gpsimd, SQUARE, 2, BANK, EARLY, second)
         scatter(LAST, 0, S)
         x = read_page(2, 2, EARLY, M)
-        square = feature(SQUARE, "square2_late", x, M - EARLY, 73)
-        late_sine = feature(SIN, "sine2_late", x, M - EARLY, 73.5)
+        square = feature(SQUARE, "square2_late", x, M - EARLY, 73.5)
+        late_sine = feature(SIN, "sine2_late", x, M - EARLY, 74)
         late_square = square
-        warm_w = placed("warm_w", [P, 2 * P], U8, 70.75)
+        warm_w = placed("warm_w", [P, 2 * P], U8, 71.25)
         nc.scalar.copy(warm_w[:].bitcast(U16), w1_w_raw[:, 0, :].bitcast(U16)[:, 0:H:PACK])
         warm = psum.tile([P, BANK], F32, name="acc", tag="bank")
         for n in range(4):
@@ -295,7 +296,7 @@ def tile_list_electrode_refit_kernel(
 
         a_place = {(0, 0): 84, (0, 1): 86, (1, 0): 88, (1, 1): 112, (2, 0): 12, (2, 1): 14, (3, 0): 10, (3, 1): 114}
         ab_place = {(0, 0): 116, (0, 1): 118, (1, 0): 18, (1, 1): 20, (2, 0): 24, (2, 1): 26, (3, 0): 8, (3, 1): 28}
-        scale_place = {(SQUARE, 0): 71.75, (SIN, 2): a_place[0, 1], (SIN, 3): a_place[1, 1]}
+        scale_place = {(SQUARE, 0): 72.25, (SIN, 2): a_place[0, 1], (SIN, 3): a_place[1, 1]}
 
         def quantise_z(f, c):
             name, c0 = "z_s%d_%d" % (f, c), c * CHUNK
@@ -388,11 +389,11 @@ def tile_list_electrode_refit_kernel(
         def gain_last(eng, f, c, values):
             apply_gain(eng, f, LAST, c * CHUNK, (c + 1) * CHUNK, values)
 
-        sines = feature(SIN, "sine_last0", x_last(0), CHUNK, 71)
-        squares = feature(SQUARE, "square_last0", x_last(0), CHUNK, 74)
+        sines = feature(SIN, "sine_last0", x_last(0), CHUNK, 71.5)
+        squares = feature(SQUARE, "square_last0", x_last(0), CHUNK, 74.5)
         gain_last(nc.gpsimd, SQUARE, 0, squares[:])
         gain_last(nc.scalar, SIN, 0, sines[:])
-        second_sines = feature(SIN, "sine_last1", x_last(1), CHUNK, 72)
+        second_sines = feature(SIN, "sine_last1", x_last(1), CHUNK, 72.5)
         apply_gain(nc.scalar, SIN, 2, EARLY, M, late_sine[:])
         gain_last(nc.scalar, SIN, 1, second_sines[:])
         apply_gain(nc.scalar, SQUARE, 2, EARLY, M, late_square[:])

@@ -273,15 +273,6 @@ def tile_list_electrode_refit_kernel(
         square = feature(SQUARE, "square2_late", x, M - EARLY, 73.5)
         late_sine = feature(SIN, "sine2_late", x, M - EARLY, 74)
         late_square = square
-        warm_w = placed("warm_w", [P, 2 * P], U8, 71.25)
-        nc.scalar.copy(warm_w[:].bitcast(U16), w1_w_raw[:, 0, :].bitcast(U16)[:, 0:H:PACK])
-        warm = psum.tile([P, BANK], F32, name="acc", tag="bank")
-        for n in range(4):
-            cols = slice(BANK * (n % 2), BANK * (n % 2 + 1))
-            nc.tensor.matmul_mx(
-                warm[:], lhsT=warm_w[:].bitcast(FP4X4), lhsT_scale=w1_s[:, 0, 0, :],
-                rhs=v_w[0][:, cols].bitcast(FP8X4), rhs_scale=v_s[:, 0, cols], start=True, stop=True,
-            )
 
         x_first = read_page(LAST, 102, 0, CHUNK)
         x_second = read_page(LAST, 103, CHUNK, 2 * CHUNK)

from contextlib import ExitStack

import concourse.mybir as mybir

K, H, F, N, T, S, T2, M = 1024, 512, 1024, 512, 2048, 1024, 2048, 1024
FLOPS = 2 * (K * H * S + H * N * M + H * N * M + F * N * M)

F32 = mybir.dt.float32
BF16 = mybir.dt.bfloat16
I32 = mybir.dt.int32
U32 = mybir.dt.uint32
U16 = mybir.dt.uint16
U8 = mybir.dt.uint8
FP8X4 = mybir.dt.float8_e4m3fn_x4
FP4X4 = mybir.dt.float4_e2m1fn_x4
ALU = mybir.AluOpType
ACT = mybir.ActivationFunctionType

P = 128
PACK = 4
QUAD = 32
BANK = 512
PER_COL = 16
KB = 1024
HEAD = 256
PIECES = ((0, HEAD), (HEAD, BANK), (HEAD + BANK, S - HEAD - BANK))
CHUNK = 256
NCH = M // CHUNK
LAST = PACK - 1
EARLY = M - T2 // 16
EARLY1 = M - 256
SIN, SQUARE = 0, 1


def tile_list_electrode_refit_kernel(
    tc, tab_words, tab_scales, offs, offs2, offs3, w1_words, w1_scales, wgs, page0, gain, wa, wb_words, wb_scales, wd, bias,
    out_0, out_1, out_2,
):
    nc = tc.nc
    with ExitStack() as ctx:
        lists = ctx.enter_context(tc.tile_pool(name="lists", bufs=1))
        arena = ctx.enter_context(tc.tile_pool(name="arena", bufs=1))
        keep = ctx.enter_context(tc.tile_pool(name="keep", bufs=1))
        psum = ctx.enter_context(tc.psum_pool(name="psum", bufs=8))

        def held(name, shape, dtype):
            return keep.tile(shape, dtype, name=name, align_bytes=64)

        def placed(name, shape, dtype, kb):
            return arena.tile(shape, dtype, name=name, align_bytes=64, offset=int(kb * KB))

        idx = lists.tile([P, S // PER_COL], U16, name="idx")
        idx2 = lists.tile([P, S // PER_COL], U16, name="idx2")
        idx3 = lists.tile([P, M // PER_COL], U16, name="idx3")

        tab_w = [placed("tab_w%d" % a, [P, T], I32, (13.75, 116)[a]) for a in range(2)]
        tab_s = placed("tab_s", [P, T], U8, 90)
        w1_s_raw = placed("w1_s_raw", [P, 2, H], U8, 95)
        v_s = placed("v_s", [P, 2, S], U8, 144)
        nc.gpsimd.memset(w1_s_raw[:].rearrange("p a c -> p (a c)").bitcast(I32), 0)
        nc.vector.memset(tab_s[0 : P - QUAD, :].bitcast(I32), 0)
        nc.vector.memset(v_s[:].rearrange("p a c -> p (a c)").bitcast(I32), 0)
        for q in range(4):
            eng = nc.gpsimd if q % 2 == 0 else nc.scalar
            eng.dma_start(
                w1_s_raw[QUAD * q : QUAD * q + 4, :, :].bitcast(I32),
                w1_scales[:, 4 * q : 4 * q + 4, :].rearrange("a r c -> r a c").bitcast(I32),
            )

        nc.sync.dma_start(idx[:], offs)
        nc.sync.dma_start(tab_s[P - QUAD : P, :].bitcast(I32), tab_scales.rearrange("a q n -> q a n").bitcast(I32))
        nc.sync.dma_start(tab_w[0][:], tab_words[0].rearrange("p t i -> p (t i)").bitcast(I32))
        w1_w_raw = placed("w1_w_raw", [P, 2, 2 * H], U8, 105)
        nc.sync.dma_start(w1_w_raw[:].bitcast(I32), w1_words.rearrange("a p c -> p a c").bitcast(I32))
        nc.sync.dma_start(idx2[:], offs2)
        nc.sync.dma_start(idx3[:], offs3)
        nc.sync.dma_start(tab_w[1][:], tab_words[1].rearrange("p t i -> p (t i)").bitcast(I32))

        page_rows = page0.rearrange("(p t) n -> t p n", t=PACK)
        wgs_rows = wgs.rearrange("(i t) j -> t i j", t=PACK)
        w_src = (wa, wd[0:H, :], wd[H:F, :])
        page, wg, w_raw = {}, {}, {}

        def load_page(t, kb):
            page[t] = placed("page%d" % t, [P, T2], F32, kb)
            nc.sync.dma_start(page[t][:], page_rows[t])

        def load_wg_part(t, quadrants, c0, c1):
            for q in quadrants:
                nc.sync.dma_start(wg[t][QUAD * q : QUAD * (q + 1), c0:c1], wgs_rows[t][:, c0:c1])

        def load_wg(t, kb):
            wg[t] = placed("wg%d" % t, [P, S], F32, kb)
            load_wg_part(t, (0, 2, 1, 3), 0, S)

        def load_weight(i, kb):
            w_raw[i] = placed("w_raw%d" % i, [P, PACK * N], F32, kb)
            nc.sync.dma_start(w_raw[i][:], w_src[i].rearrange("(p j) n -> p (j n)", j=PACK))

        picked_s = placed("picked_s", [P, S], U8, 63)
        nc.vector.tensor_copy(picked_s[:], tab_s[:].indirect(idx[:]))
        for q in range(4):
            row = P - QUAD + 8 * q
            nc.sync.dma_start(v_s[QUAD * q : QUAD * q + 4, :, :].bitcast(I32), picked_s[row : row + 8, :].bitcast(I32))
        wg[0] = placed("wg0", [P, S], F32, 91)
        load_wg_part(0, (0,), 0, HEAD)
        load_page(0, 83)
        load_wg_part(0, (2, 1, 3), 0, HEAD)
        load_wg_part(0, (0, 2, 1, 3), HEAD, S)

        w1_w = placed("w1_w", [P, 2, PACK, 2 * P], U8, 45.5)
        nc.scalar.copy(w1_w[:].bitcast(U16), w1_w_raw[:].bitcast(U16).rearrange("p a (m t) -> p a t m", t=PACK))
        w1_s = placed("w1_s", [P, 2, PACK, P], U8, 146)
        w1_s_by_slot = w1_s_raw[:].rearrange("p a (m t) -> p a t m", t=PACK)
        nc.gpsimd.tensor_copy(w1_s[:, :, 0, :], w1_s_by_slot[:, :, 0, :])
        nc.gpsimd.tensor_copy(w1_s[:, :, 1:PACK, :], w1_s_by_slot[:, :, 1:PACK, :])

        v_w = [placed("v_w0", [P, S], U32, 140), placed("v_w1", [P, S], U32, 32)]
        nc.vector.tensor_copy(v_w[0][:], tab_w[0][:].bitcast(U32).indirect(idx[:]))
        for c0, w in PIECES:
            where = idx[:, c0 // PER_COL : (c0 + w) // PER_COL]
            nc.vector.tensor_copy(v_w[1][:, c0 : c0 + w], tab_w[1][:].bitcast(U32).indirect(where))

        h_head = placed("h_head", [P, HEAD], F32, 135)
        h_rest = placed("h_rest", [P, S - HEAD], F32, 80)
        h_sb = {t: placed("h%d" % t, [P, S], F32, kb) for t, kb in ((1, 5.75), (2, 74), (3, 0))}
        h2_head = placed("h2_head", [P, HEAD], F32, 73)

        def make_h(t, c0, w, target):
            acc = psum.tile([P, w], F32, name="acc", tag="bank")
            n = BANK if w == BANK else P
            for a in range(2):
                for b in range(0, w, n):
                    cols = slice(c0 + b, c0 + b + n)
                    nc.tensor.matmul_mx(
                        acc[:, b : b + n], lhsT=w1_w[:, a, t, :].bitcast(FP4X4), lhsT_scale=w1_s[:, a, t, :],
                        rhs=v_w[a][:, cols].bitcast(FP8X4), rhs_scale=v_s[:, a, cols],
                        start=(a == 0 and b == 0), stop=(a == 1 and b == w - n),
                    )
            for part, cols in target:
                nc.scalar.copy(part, acc[:, cols])

        for c0, w in PIECES:
            make_h(0, c0, w, [(h_head[:] if c0 == 0 else h_rest[:, c0 - HEAD : c0 - HEAD + w], slice(0, w))])
        for t in range(1, PACK):
            for c0 in (0, BANK):
                if (t, c0) == (2, 0):
                    make_h(t, c0, BANK, [(h2_head[:], slice(0, HEAD)), (h_sb[t][:, HEAD:BANK], slice(HEAD, BANK))])
                else:
                    make_h(t, c0, BANK, [(h_sb[t][:, c0 : c0 + BANK], slice(0, BANK))])

        load_wg(1, 17.75)
        load_weight(0, 9.75)
        load_page(1, 112)
        wb_s_raw = w1_s_raw[:, 0, :]
        for q in range(4):
            nc.sync.dma_start(wb_s_raw[QUAD * q : QUAD * q + 4, :].bitcast(I32), wb_scales[0, 4 * q : 4 * q + 4, :].bitcast(I32))
        gain_rows = gain.rearrange("(f p t) -> f p t", f=2, t=PACK)
        gain_sin = placed("gain_sin", [P, PACK], F32, 122.5)
        gain_first = placed("gain_first", [P, 1], F32, 122.625)
        gain_rest = placed("gain_rest", [P, PACK - 1], F32, 122.6875)
        bias_sb = placed("bias_sb", [P, PACK], F32, 122.75)
        nc.sync.dma_start(gain_sin[:], gain_rows[SIN])
        load_page(2, 39)
        load_wg(2, 30)
        with nc.allow_non_contiguous_dma(reason="one gain a partition"):
            nc.sync.dma_start(gain_first[:], gain_rows[SQUARE][:, 0:1])
        load_weight(1, 131.75)
        load_weight(2, 47)
        wb_w_raw = placed("wb_w_raw", [P, N], I32, 63.5)
        nc.sync.dma_start(wb_w_raw[:], wb_words[0].rearrange("p c i -> p (c i)").bitcast(I32))
        load_page(3, 55.5)
        load_wg(3, 34)
        nc.sync.dma_start(gain_rest[:], gain_rows[SQUARE][:, 1:PACK])
        nc.sync.dma_start(bias_sb[:], bias.rearrange("(p t) -> p t", t=PACK))

        w_s = [placed("w_s%d" % i, [P, N], U8, kb) for i, kb in enumerate((33.5, 71.25, 71.75))]
        w_w, grouped = {}, {}

        def round_weight(i, tile):
            grouped[i] = tile
            nc.scalar.copy(
                tile[:].rearrange("p (t m j) -> p m j t", t=PACK, j=PACK),
                w_raw[i][:].rearrange("p (j m t) -> p m j t", j=PACK, t=PACK),
            )

        def quantise_weight(i, kb):
            w_w[i] = placed("w_w%d" % i, [P, N], U32, kb)
            nc.vector.quantize_mx(w_w[i][:].bitcast(FP8X4), w_s[i][:], grouped[i][:])

        z_all = [held("z_bf%d" % f, [P, M * PACK], BF16) for f in range(2)]

        def z_bf(f, c0, c1):
            return z_all[f][:, PACK * c0 : PACK * c1]

        def apply_gain(eng, f, t, c0, c1, values):
            target = z_bf(f, c0, c1)[:, t : PACK * (c1 - c0) : PACK]
            if f == SIN:
                factor = gain_sin[:, t : t + 1]
            else:
                factor = gain_first[:] if t == 0 else gain_rest[:, t - 1 : t]
            if eng is nc.scalar:
                nc.scalar.activation(target, values, ACT.Copy, scale=factor)
            else:
                eng.tensor_scalar(target, values, factor, 0.0, ALU.mult, ALU.add)

        def feature(f, name, x, w, kb):
            values = placed(name, [P, w], F32, kb)
            nc.scalar.activation(values[:], x, ACT.Sin if f == SIN else ACT.Square)
            return values

        weighted = {}

        def weigh(t, kb, parts):
            weighted[t] = placed("weighted%d" % t, [P, S], F32, kb)
            for c0, c1, values in parts:
                nc.gpsimd.tensor_tensor(weighted[t][:, c0:c1], values, wg[t][:, c0:c1], ALU.mult)

        def scatter(t, c0, c1):
            nc.vector.tensor_copy(page[t][:].indirect(idx2[:, c0 // PER_COL : c1 // PER_COL]), weighted[t][:, c0:c1])

        def read_page(t, kb, c0=0, c1=M):
            x = placed("x%d_%d" % (t, c0), [P, c1 - c0], F32, kb)
            nc.vector.tensor_copy(x[:], page[t][:].indirect(idx3[:, c0 // PER_COL : c1 // PER_COL]))
            return x[:]

        cut = HEAD // PER_COL
        nc.vector.tensor_tensor(page[0][:].indirect(idx2[:, 0:cut]), h_head[:], wg[0][:, 0:HEAD], ALU.mult)
        nc.vector.tensor_tensor(page[0][:].indirect(idx2[:, cut : S // PER_COL]), h_rest[:], wg[0][:, HEAD:S], ALU.mult)
        weigh(1, 66, [(0, S, h_sb[1][:])])
        wb_s = placed("wb_s", [P, N], U8, 5.75)
        nc.gpsimd.tensor_copy(wb_s[:].rearrange("p (t m) -> p t m", t=PACK), wb_s_raw.rearrange("p (m t) -> p t m", t=PACK))
        round_weight(0, held("grouped0", [P, N * PACK], BF16))
        x = read_page(0, 97)
        sine = feature(SIN, "sine0", x, M, 9.75)
        square = feature(SQUARE, "square0", x, M, 13.75)
        apply_gain(nc.scalar, SIN, 0, 0, M, sine[:])
        round_weight(1, placed("grouped1", [P, N * PACK], BF16, 9.75))
        weigh(2, 17.75, [(0, HEAD, h2_head[:]), (HEAD, S, h_sb[2][:, HEAD:S])])
        apply_gain(nc.gpsimd, SQUARE, 0, 0, M, square[:])
        round_weight(2, placed("grouped2", [P, N * PACK], BF16, 148))
        spare = w_raw[2]

        def feature_in(f, x, c0, w):
            nc.scalar.activation(spare[:, c0 : c0 + w], x, ACT.Sin if f == SIN else ACT.Square)
            return spare[:, c0 : c0 + w]

        scatter(1, 0, S)
        scatter(2, 0, HEAD)
        x = read_page(1, 71, 0, EARLY1)
        sine = feature_in(SIN, x, 0, EARLY1)
        square = feature_in(SQUARE, x, 1280, EARLY1)
        apply_gain(nc.scalar, SIN, 1, 0, EARLY1, sine)
        weigh(LAST, 30, [(0, S, h_sb[LAST][:])])
        apply_gain(nc.gpsimd, SQUARE, 1, 0, EARLY1, square)
        wb_w = placed("wb_w", [P, N], U32, 69.25)
        nc.scalar.copy(wb_w[:].rearrange("p (t m) -> p t m", t=PACK), wb_w_raw[:].bitcast(U32).rearrange("p (m t) -> p t m", t=PACK))
        scatter(2, HEAD, S)
        x = read_page(1, 75.5, EARLY1, M)
        late_sine = feature_in(SIN, x, 256, M - EARLY1)
        square = feature_in(SQUARE, x, 0, M - EARLY1)
        apply_gain(nc.gpsimd, SQUARE, 1, EARLY1, M, square)
        apply_gain(nc.scalar, SIN, 1, EARLY1, M, late_sine)
        x = read_page(2, 126.5, 0, EARLY)
        first = feature_in(SQUARE, x[:, 0:BANK], 512, BANK)
        sine = feature(SIN, "sine2", x, EARLY, 71.25)
        second = feature(SQUARE, "square2_second", x[:, BANK:EARLY], EARLY - BANK, 76)[:]
        apply_gain(nc.gpsimd, SQUARE, 2, 0, BANK, first)
        apply_gain(nc.scalar, SIN, 2, 0, EARLY, sine[:])
        apply_gain(nc.gpsimd, SQUARE, 2, BANK, EARLY, second)
        scatter(LAST, 0, S)
        x = read_page(2, 2, EARLY, M)
        square = feature(SQUARE, "square2_late", x, M - EARLY, 73.5)
        late_sine = feature(SIN, "sine2_late", x, M - EARLY, 74)
        late_square = square

        x_first = read_page(LAST, 102, 0, CHUNK)
        x_second = read_page(LAST, 103, CHUNK, 2 * CHUNK)
        quantise_weight(0, 100)
        x_rest = read_page(LAST, 120, 2 * CHUNK, M)
        z_w = [held("z_w%d" % f, [P, M], U32) for f in range(2)]
        z_s = {}
        y_s = held("y_s", [P, M], U8)
        y_rows = out_0.rearrange("(p t) m -> p t m", t=PACK)
        code_rows = out_1[0].rearrange("p m t -> p (m t)")
        y, rounded, banks, a_sb, ab = {}, {}, {}, {}, {}

        a_place = {(0, 0): 84, (0, 1): 86, (1, 0): 88, (1, 1): 112, (2, 0): 12, (2, 1): 14, (3, 0): 10, (3, 1): 114}
        ab_place = {(0, 0): 116, (0, 1): 118, (1, 0): 18, (1, 1): 20, (2, 0): 24, (2, 1): 26, (3, 0): 8, (3, 1): 28}
        scale_place = {(SQUARE, 0): 72.25, (SIN, 2): a_place[0, 1], (SIN, 3): a_place[1, 1]}

        def quantise_z(f, c):
            name, c0 = "z_s%d_%d" % (f, c), c * CHUNK
            if (f, c) in scale_place:
                z_s[f, c] = placed(name, [P, CHUNK], U8, scale_place[f, c])
            else:
                z_s[f, c] = held(name, [P, CHUNK], U8)
            nc.vector.quantize_mx(z_w[f][:, c0 : c0 + CHUNK].bitcast(FP8X4), z_s[f, c][:], z_bf(f, c0, c0 + CHUNK))

        def part(c, n):
            if c < NCH - 1:
                return range(2 * n, 2 * n + 2), 0, CHUNK
            return range(PACK), n * CHUNK // 2, CHUNK // 2

        def product(kind, c, n):
            words, scales, f = {
                "A": (w_w[0], w_s[0], SIN), "B": (wb_w, wb_s, SQUARE), "D": (w_w[1], w_s[1], SIN), "E": (w_w[2], w_s[2], SQUARE),
            }[kind]
            slots, b0, w = part(c, n)
            if kind != "E":
                banks[kind, c, n] = psum.tile([P, BANK], F32, name="acc", tag="bank")
            acc = banks["D" if kind == "E" else kind, c, n]
            for i, t in enumerate(slots):
                cols = slice(P * t, P * (t + 1))
                nc.tensor.matmul_mx(
                    acc[:, i * w : (i + 1) * w], lhsT=words[:, cols].bitcast(FP8X4), lhsT_scale=scales[:, cols],
                    rhs=z_w[f][:, c * CHUNK + b0 : c * CHUNK + b0 + w].bitcast(FP8X4), rhs_scale=z_s[f, c][:, b0 : b0 + w],
                    start=kind in "AB" or (kind == "D" and i == 0), stop=kind in "AB" or (kind == "E" and i == len(slots) - 1),
                )

        def copy_a(c, n):
            a_sb[c, n] = placed("a_sb%d_%d" % (c, n), [P, BANK], F32, a_place[c, n])
            nc.scalar.copy(a_sb[c, n][:], banks["A", c, n][:])

        def multiply(c, n):
            ab[c, n] = placed("ab%d_%d" % (c, n), [P, BANK + CHUNK if (c, n) == (1, 1) else BANK], F32, ab_place[c, n])
            nc.vector.tensor_tensor(ab[c, n][:, 0:BANK], banks["B", c, n][:], a_sb[c, n][:], ALU.mult)

        def add_up(c, n):
            slots, b0, w = part(c, n)
            c0 = c * CHUNK
            if n == 0:
                y[c] = held("y%d" % c, [P, PACK, CHUNK], F32)
                if c == NCH - 1:
                    rounded[c] = held("y_bf%d" % c, [P, CHUNK * PACK], BF16)
            for i, t in enumerate(slots):
                cols = slice(i * w, (i + 1) * w)
                nc.vector.scalar_tensor_tensor(
                    y[c][:, t, b0 : b0 + w], banks["D", c, n][:, cols], bias_sb[:, t : t + 1], ab[c, n][:, cols], ALU.add, ALU.add
                )
            if c == NCH - 1:
                nc.sync.dma_start(y_rows[:, :, c0 + b0 : c0 + b0 + w], y[c][:, :, b0 : b0 + w])
                nc.scalar.copy(
                    rounded[c][:, PACK * b0 : PACK * (b0 + w)].rearrange("p (g i t) -> p g t i", i=4, t=PACK),
                    y[c][:, :, b0 : b0 + w].rearrange("p t (g i) -> p g t i", i=4),
                )
            elif n == 1:
                nc.sync.dma_start(y_rows[:, :, c0 : c0 + CHUNK], y[c][:])

        def round_y(c):
            if c != 1:
                y_bf = ab[1, 1][:, CHUNK : BANK + CHUNK].bitcast(BF16)
            else:
                y_bf = placed("y_bf%d" % c, [P, CHUNK * PACK], BF16, ab_place[2, 1])[:]
            if c == 2:
                nc.gpsimd.tensor_scalar(
                    y_bf.rearrange("p (m t) -> p m t", t=PACK), y[c][:].rearrange("p t m -> p m t"), 1.0, 0.0, ALU.mult, ALU.add
                )
            else:
                nc.scalar.copy(
                    y_bf.rearrange("p (g i t) -> p g t i", i=4, t=PACK), y[c][:].rearrange("p t (g i) -> p g t i", i=4)
                )
            rounded[c] = y_bf

        def make_planes(chunks, kb):
            begin, end = chunks[0] * CHUNK, (chunks[-1] + 1) * CHUNK
            y_w = placed("y_w%d" % chunks[0], [P, end - begin], I32, kb)
            for c in chunks:
                w = CHUNK if c < NCH - 1 else CHUNK // 2
                for b0 in range(0, CHUNK, w):
                    c0, c1 = c * CHUNK + b0, c * CHUNK + b0 + w
                    nc.vector.quantize_mx(
                        y_w[:, c0 - begin : c1 - begin].bitcast(FP8X4), y_s[:, c0:c1], rounded[c][:, PACK * b0 : PACK * (b0 + w)]
                    )
            nc.sync.dma_start(code_rows[:, PACK * begin : PACK * end].bitcast(I32), y_w[:])

        def x_last(c):
            return (x_first, x_second)[c] if c < 2 else x_rest[:, (c - 2) * CHUNK : (c - 1) * CHUNK]

        def gain_last(eng, f, c, values):
            apply_gain(eng, f, LAST, c * CHUNK, (c + 1) * CHUNK, values)

        sines = feature(SIN, "sine_last0", x_last(0), CHUNK, 71.5)
        squares = feature(SQUARE, "square_last0", x_last(0), CHUNK, 74.5)
        gain_last(nc.gpsimd, SQUARE, 0, squares[:])
        gain_last(nc.scalar, SIN, 0, sines[:])
        second_sines = feature(SIN, "sine_last1", x_last(1), CHUNK, 72.5)
        apply_gain(nc.scalar, SIN, 2, EARLY, M, late_sine[:])
        gain_last(nc.scalar, SIN, 1, second_sines[:])
        apply_gain(nc.scalar, SQUARE, 2, EARLY, M, late_square[:])
        quantise_z(SIN, 0)
        quantise_z(SQUARE, 0)
        quantise_weight(1, 109)
        quantise_weight(2, 107)
        quantise_z(SIN, 1)

        def sines_of(c):
            values = placed("sine_last2", [P, CHUNK], F32, 149)[:] if c == 2 else ab[0, 0][:, 0:CHUNK]
            nc.scalar.activation(values, x_last(c), ACT.Sin)
            gain_last(nc.scalar, SIN, c, values)

        def squares_of(c):
            values = placed("square_last1", [P, CHUNK], F32, 12.75)[:] if c == 1 else ab[c - 2, 0][:, CHUNK:BANK]
            nc.scalar.activation(values, x_last(c), ACT.Square)
            gain_last(nc.gpsimd, SQUARE, c, values)

        for n in range(2):
            product("A", 0, n)
        for c in range(NCH):
            for n in range(2):
                product("B", c, n)
            if c == NCH - 2:
                round_y(0)
            for n in range(2):
                if c == 0:
                    copy_a(c, n)
                    if n == 0:
                        squares_of(1)
                multiply(c, n)
            if c == NCH - 1:
                round_y(1)
                round_y(2)
            if c == 0:
                sines_of(2)
            for n in range(2):
                if c == 0:
                    product("D", c, n)
                product("E", c, n)
                if c + 1 < NCH:
                    product("A", c + 1, n)
                    copy_a(c + 1, n)
                if n == 0:
                    add_up(c, 0)
                    if c + 2 < NCH:
                        squares_of(c + 2)
            if c == 0:
                sines_of(3)
            if c + 1 < NCH:
                for n in range(2):
                    product("D", c + 1, n)
            if c + 1 < NCH:
                quantise_z(SQUARE, c + 1)
            if c + 2 < NCH:
                quantise_z(SIN, c + 2)
            if c == NCH - 2:
                make_planes((0,), a_place[c, 1])
            add_up(c, 1)
        make_planes((1, 2), ab_place[NCH - 1, 0])
        make_planes((NCH - 1,), 16)
        for q in range(4):
            eng = nc.sync if q % 2 == 0 else nc.scalar
            eng.dma_start(out_2[0, 4 * q : 4 * q + 4, :].bitcast(I32), y_s[QUAD * q : QUAD * q + 4, :].bitcast(I32))
